import numpy as np
import ml_dtypes


def mxq(x, axis, fmt="e4m3"):
    dtype, down = {"e4m3": (ml_dtypes.float8_e4m3fn, 7), "e5m2": (ml_dtypes.float8_e5m2, 14)}[fmt]
    v = np.moveaxis(np.asarray(x, np.float32).astype(ml_dtypes.bfloat16).astype(np.float64), axis, -1)
    blocks = v.reshape(v.shape[:-1] + (-1, 32))
    amax = np.abs(blocks).max(-1, keepdims=True)
    byte = np.maximum(np.where(amax > 0, np.frexp(amax)[1] - 1 + 127, 0) - down, 1)
    scale = np.exp2(byte - 127.0)
    codes = (blocks / scale).astype(np.float32).astype(dtype).astype(np.float64)
    return np.moveaxis((codes * scale).reshape(v.shape), -1, axis)


WIDE = False


def mx_kscale(k):
    if not WIDE:
        return np.ones(k)
    levels = np.array([18, -18])
    if k % 512:
        return np.exp2(np.random.permutation(np.resize(levels, k // 32))).repeat(32)
    a = np.empty((k // 512, 16))
    for p in range(k // 512):
        a[p, :8] = np.random.permutation(np.resize(levels, 8))
        for g in range(8):
            far = levels[np.abs(levels - a[p, g]) >= 10]
            a[p, g + 8] = far[np.random.randint(len(far))]
    return np.exp2(a.ravel()).repeat(32)


def f64(x):
    return np.asarray(x).astype(np.float64)


def striped(idx):
    return np.tile(np.asarray(idx).reshape(-1, 16).T, (8, 1)).astype(np.uint16)


def unstriped(offs):
    return offs[:16].T.reshape(-1).astype(np.int64)


N, C, D, R = 1024, 4096, 512, 512


def eight(codes):
    return np.concatenate([codes[h].reshape(-1, 16).T for h in range(8)]).astype(np.uint16)


def uneight(offs):
    return np.stack([offs[16 * h:16 * h + 16].T.reshape(-1) for h in range(8)]).astype(np.int64)


def setup_inputs():
    n = np.random.standard_normal
    s = mx_kscale(D)[:, None]
    u = mx_kscale(N)
    grid = lambda x: np.round(x * 32) / 32
    return {
        "xT": (n((D, R)) * (1.0 / np.sqrt(D)) * s).astype(np.float32),
        "cb": (grid(n((D, C))) / s).astype(np.float32),
        "norm": np.tile(np.random.randint(32, 129, N) / 64.0 / u, (128, 1)).astype(np.float32),
        "ts": np.tile(np.random.uniform(0.5, 1.5, N) * u, (128, 1)).astype(np.float32),
        "y": n((R, N)).astype(np.float32),
        "wt": (np.random.uniform(0.5, 1.5, (R, 1)) * 1.0 / np.sqrt(N)).astype(np.float32),
        "offs": eight(np.random.randint(0, C, (8, N))),
    }


def reference(xT, cb, norm, ts, y, wt, offs):
    code = uneight(offs)
    k = np.concatenate([f64(cb)[64 * h:64 * h + 64][:, code[h]] for h in range(8)]) * f64(norm)[:1]
    a = f64(ts)[:1] * (mxq(f64(xT), 0, "e4m3").T @ mxq(k, 0, "e4m3"))
    g = f64(wt) * np.tanh(a - f64(y))
    h = f64(ts)[:1] * g
    return mxq(h, 1, "e5m2") @ mxq(k, 1, "e4m3").T

@@ -1,0 +1,259 @@
+from contextlib import ExitStack
+
+import concourse.mybir as mybir
+from concourse.masks import make_identity
+
+N, C, D, R = 1024, 4096, 512, 512
+FLOPS = 2 * 2 * R * D * N
+BYTES = 4 * (D * R + D * C + 2 * N + R * N + R + R * D) + 2 * 128 * (N // 16)
+
+F32 = mybir.dt.float32
+BF16 = mybir.dt.bfloat16
+U32 = mybir.dt.uint32
+U16 = mybir.dt.uint16
+U8 = mybir.dt.uint8
+E4 = mybir.dt.float8_e4m3fn_x4
+E5 = mybir.dt.float8_e5m2_x4
+MULT = mybir.AluOpType.mult
+SUB = mybir.AluOpType.subtract
+TANH = mybir.ActivationFunctionType.Tanh
+
+P = 128
+PACK = 4
+KP = P * PACK
+G = N // KP
+RT = R // P
+
+
+def tile_attend_gpq_lch_x_kernel(tc, xT, cb, norm, ts, y, wt, offs, out):
+    nc = tc.nc
+    with ExitStack() as ctx:
+        keep = ctx.enter_context(tc.tile_pool(name="keep", bufs=1))
+        ring = ctx.enter_context(tc.tile_pool(name="ring", bufs=4))
+        psum = ctx.enter_context(tc.psum_pool(name="psum", bufs=4))
+
+        offsets = keep.tile([P, N // 16], U16, name="offsets")
+        win = [keep.tile([P, C], F32, name="win%d" % t) for t in range(PACK)]
+        x_raw = keep.tile([P, PACK, R], F32, name="x_raw")
+        y_raw = [keep.tile([P, RT, KP], F32, name="y_raw%d" % g) for g in range(G)]
+        norm_col = keep.tile([P, G, PACK], F32, name="norm_col")
+        ts_col = keep.tile([P, G, 1, PACK], F32, name="ts_col")
+        wt_col = keep.tile([P, PACK], F32, name="wt_col")
+        cb_planes = cb.rearrange("(p t) c -> t p c", t=PACK)
+
+        def load_y(g):
+            nc.sync.dma_start(out=y_raw[g][:], in_=y[:, g * KP:(g + 1) * KP].rearrange("(i p) c -> p i c", p=P))
+
+        nc.sync.dma_start(offsets[:], offs)
+        nc.scalar.dma_start(out=wt_col[:], in_=wt.rearrange("(p j) o -> p (j o)", j=PACK))
+        nc.scalar.dma_start(out=ts_col[:, :, 0, :], in_=ts[0:1, :].rearrange("o (g p j) -> p (o g) j", g=G, j=PACK))
+        nc.sync.dma_start(out=norm_col[:], in_=norm[0:1, :].rearrange("o (g p j) -> p (o g) j", g=G, j=PACK))
+        nc.sync.dma_start(out=win[0][:], in_=cb_planes[0])
+        load_y(0)
+        nc.sync.dma_start(out=x_raw[:], in_=xT.rearrange("(p t) r -> p t r", t=PACK))
+        nc.sync.dma_start(out=win[1][:], in_=cb_planes[1])
+        load_y(1)
+        nc.sync.dma_start(out=win[2][:], in_=cb_planes[2])
+        nc.sync.dma_start(out=win[3][:], in_=cb_planes[3])
+
+        ident = keep.tile([P, P], F32, name="ident")
+        make_identity(nc, ident[:])
+
+        def spread(col, row):
+            bank = psum.tile([P, PACK, P], F32, name="turn", tag="turn")
+            for j in range(PACK):
+                nc.tensor.transpose(bank[:, j, :], col[:, j:j + 1].to_broadcast([P, P]), ident[:])
+            nc.scalar.copy(out=row.rearrange("m (p j) -> m p j", j=PACK), in_=bank[:].rearrange("m j p -> m p j"))
+
+        wt_row = keep.tile([P, R, 1], F32, name="wt_row")
+        spread(wt_col[:], wt_row[:, :, 0])
+        norm_row = keep.tile([P, G, KP], F32, name="norm_row")
+        for g in range(G):
+            spread(norm_col[:, g, :], norm_row[:, g, :])
+        weight = [keep.tile([P, R, PACK], F32, name="weight%d" % g) for g in range(G)]
+        for g in range(G):
+            nc.vector.tensor_tensor(weight[g][:], wt_row[:].to_broadcast([P, R, PACK]),
+                                    ts_col[:, g, :, :].to_broadcast([P, R, PACK]), MULT)
+
+        yT = [keep.tile([P, PACK, R], F32, name="yT%d" % g) for g in range(G)]
+
+        def turn_y(g, t):
+            bank = psum.tile([P, RT, P], F32, name="turn", tag="turn")
+            for i in range(RT):
+                nc.tensor.transpose(bank[:, i, :], y_raw[g][:, i, t:KP:PACK], ident[:])
+            nc.scalar.copy(out=yT[g][:, t, :], in_=bank[:].rearrange("m i p -> m (i p)"))
+
+        k_d = [keep.tile([P, PACK, P, PACK], BF16, name="k_d%d" % g, tag="k_d%d" % g, align_bytes=64) for g in range(G)]
+        k_n = keep.tile([P, G, PACK, KP], BF16, name="k_n", align_bytes=64)
+        k_n_words = k_n[:].rearrange("m g t c -> m (g t c)").bitcast(F32).rearrange(
+            "m (g t p u) -> m g t p u", g=G, t=PACK, u=2)
+        kn_codes = keep.tile([P, G, D], U32, name="kn_codes", align_bytes=64)
+        kn_scales = keep.tile([P, G, D], U8, name="kn_scales", align_bytes=64)
+        k_f32 = [keep.tile([P, PACK, KP], F32, name="k_f32_%d" % g) for g in range(G)]
+        k32 = {(t, g): k_f32[g][:, t, :] for t in range(PACK) for g in range(G)}
+
+        def gather(t, g, parts=1):
+            width = KP // parts
+            for c in range(parts):
+                first = (g * KP + c * width) // 16
+                nc.vector.tensor_tensor(k32[t, g][:, c * width:(c + 1) * width],
+                                        win[t][:].indirect(offsets[:, first:first + width // 16]),
+                                        norm_row[:, g, c * width:(c + 1) * width], MULT)
+
+        def place(t, g, copy, tiles=slice(0, PACK), ms=slice(0, P)):
+            src = k32[t, g].rearrange("p (m a) -> p a m", a=PACK)
+            copy(out=k_d[g][:, tiles, ms, t], in_=src[:, tiles, ms])
+
+        def place_early(g):
+            src = k_f32[g][:, 0:PACK - 1, :].rearrange("p t (m a) -> p m a t", a=PACK)
+            nc.vector.tensor_copy(out=k_d[g][:, :, :, 0:PACK - 1].rearrange("p a m t -> p m a t"), in_=src)
+
+        pairs = {}
+        k_bank = {}
+
+        def round_k(t, g):
+            if t < PACK - 1:
+                pairs[t, g] = ring.tile([P, KP], BF16, name="pairs", tag="pairs")
+            elif g == 0:
+                late_pairs = keep.tile([P, G, KP], BF16, name="late_pairs", tag="k_d0", align_bytes=64)
+                for e in range(G):
+                    pairs[t, e] = late_pairs[:, e, :]
+            nc.scalar.copy(out=pairs[t, g][:].rearrange("p (u m e) -> p u m e", u=2, e=2),
+                           in_=k32[t, g].rearrange("p (m u e) -> p u m e", u=2, e=2))
+
+        def turn_k(t, g):
+            bank = psum.tile([P, 2, P], F32, name="turn", tag="turn")
+            words = pairs[t, g][:].bitcast(F32)
+            for u in range(2):
+                nc.tensor.transpose(bank[:, u, :], words[:, u * P:(u + 1) * P], ident[:])
+            nc.scalar.copy(out=k_n_words[:, g, t, :, :], in_=bank[:].rearrange("m u p -> m p u"))
+
+        def quant_kn(t, g, planes=1):
+            cols = slice(t * P, (t + planes) * P)
+            nc.vector.quantize_mx(out=kn_codes[:, g, cols].bitcast(E4), scales=kn_scales[:, g, cols],
+                                  in_=k_n[:, g, t:t + planes, :].rearrange("m t c -> m (t c)"))
+
+        x_bf = keep.tile([P, R, PACK], BF16, name="x_bf", align_bytes=64)
+        x_codes = keep.tile([P, R], U32, name="x_codes", align_bytes=64)
+        x_scales = keep.tile([P, R], U8, name="x_scales", align_bytes=64)
+
+        on_v, on_s = nc.vector.tensor_copy, nc.scalar.copy
+        low, high = slice(0, 2), slice(2, 4)
+        for t in range(PACK - 1):
+            for g in range(G):
+                gather(t, g)
+            for g in range(G):
+                round_k(t, g)
+            for g in range(G):
+                turn_k(t, g)
+                if t == PACK - 2:
+                    place_early(g)
+            for g in range(G):
+                if (t, g) != (PACK - 2, G - 1):
+                    quant_kn(t, g)
+            if t == 0:
+                for a in range(PACK):
+                    turn_y(0, a)
+            if t == 0:
+                nc.scalar.copy(out=x_bf[:], in_=x_raw[:].rearrange("p t r -> p r t"))
+                nc.vector.quantize_mx(out=x_codes[:].bitcast(E4), scales=x_scales[:],
+                                      in_=x_bf[:].rearrange("p r t -> p (r t)"))
+            if t == 1:
+                for a in range(PACK):
+                    turn_y(1, a)
+
+        kd_codes = [keep.tile([P, KP], U32, name="kd_codes%d" % g, align_bytes=64) for g in range(G)]
+        kd_scales = [keep.tile([P, KP], U8, name="kd_scales%d" % g, align_bytes=64) for g in range(G)]
+        z = [keep.tile([P, PACK, R], F32, name="z%d" % g) for g in range(G)]
+        h_bf = [keep.tile([P, R, PACK], BF16, name="h_bf%d" % g, align_bytes=64) for g in range(G)]
+        h_codes = [keep.tile([P, R], U32, name="h_codes%d" % g, align_bytes=64) for g in range(G)]
+        h_scales = [keep.tile([P, R], U8, name="h_scales%d" % g, align_bytes=64) for g in range(G)]
+        th = {}
+        sums = {}
+
+        def quant_kd(g):
+            nc.vector.quantize_mx(out=kd_codes[g][:].bitcast(E4), scales=kd_scales[g][:],
+                                  in_=k_d[g][:].rearrange("p a m t -> p (a m t)"))
+
+        acc = {}
+
+        def scores(g, a):
+            acc[g, a] = psum.tile([P, R], F32, name="acc", tag="acc")
+            cols = slice(a * P, (a + 1) * P)
+            nc.tensor.matmul_mx(out=acc[g, a][:], lhsT=kd_codes[g][:, cols].bitcast(E4),
+                                lhsT_scale=kd_scales[g][:, cols],
+                                rhs=x_codes[:].bitcast(E4), rhs_scale=x_scales[:], start=True, stop=True)
+
+        def residual(g, a):
+            nc.vector.scalar_tensor_tensor(out=z[g][:, a, :], in0=acc[g, a][:], scalar=ts_col[:, g, 0, a:a + 1],
+                                           in1=yT[g][:, a, :], op0=MULT, op1=SUB)
+
+        def tanh(g, i):
+            th[g, i] = ring.tile([P, P, PACK], F32, name="th", tag="th", bufs=G * RT)
+            nc.scalar.activation(out=th[g, i][:], in_=z[g][:, :, i * P:(i + 1) * P].rearrange("m a r -> m r a"),
+                                 func=TANH)
+
+        def weigh(g, i):
+            rows = slice(i * P, (i + 1) * P)
+            nc.vector.tensor_tensor(h_bf[g][:, rows, :], th[g, i][:], weight[g][:, rows, :], MULT)
+
+        def quant_h(g, i, tiles=1):
+            rows = slice(i * P, (i + tiles) * P)
+            nc.vector.quantize_mx(out=h_codes[g][:, rows].bitcast(E5), scales=h_scales[g][:, rows],
+                                  in_=h_bf[g][:, rows, :].rearrange("m r a -> m (r a)"))
+
+        def grad(g, i):
+            rows = slice(i * P, (i + 1) * P)
+            if g == 0:
+                sums[i] = psum.tile([P, D], F32, name="acc", tag="acc")
+            nc.tensor.matmul_mx(out=sums[i][:], lhsT=h_codes[g][:, rows].bitcast(E5), lhsT_scale=h_scales[g][:, rows],
+                                rhs=kn_codes[:, g, :].bitcast(E4), rhs_scale=kn_scales[:, g, :],
+                                start=(g == 0), stop=(g == G - 1))
+
+        def finish(i):
+            res = ring.tile([P, D], F32, name="res", tag="res")
+            dst = res[:].rearrange("r (p t) -> r p t", t=PACK)
+            src = sums[i][:].rearrange("r (t p) -> r p t", t=PACK)
+            if i == RT - 1:
+                nc.vector.tensor_copy(out=dst, in_=src)
+            else:
+                nc.scalar.copy(out=dst, in_=src)
+            nc.sync.dma_start(out=out[i * P:(i + 1) * P, :], in_=res[:])
+
+        last = PACK - 1
+        gather(last, 0, parts=2)
+        place(last, 0, on_s, ms=slice(0, P // 2))
+        place(last, 0, on_s, ms=slice(P // 2, P))
+        gather(last, 1)
+        place(last, 1, on_s, high)
+        quant_kd(0)
+        place(last, 1, on_v, low)
+        for a in range(PACK):
+            scores(0, a)
+        round_k(last, 0)
+        round_k(last, 1)
+        quant_kd(1)
+        for a in range(PACK):
+            residual(0, a)
+            scores(1, a)
+        for g in range(G):
+            turn_k(last, g)
+        for i in range(RT):
+            tanh(0, i)
+        for a in range(PACK):
+            residual(1, a)
+        for i in range(RT):
+            weigh(0, i)
+            tanh(1, i)
+        quant_kn(last, 0)
+        quant_h(0, 0, tiles=RT)
+        quant_kn(last - 1, 1, planes=2)
+        for i in range(RT):
+            grad(0, i)
+        weigh(1, 0)
+        for i in range(RT):
+            if i + 1 < RT:
+                weigh(1, i + 1)
+            quant_h(1, i)
+            grad(1, i)
+            finish(i)

@@ -35,26 +35,31 @@ def tile_attend_gpq_lch_x_kernel(tc, xT, cb, norm, ts, y, wt, offs, out):
         offsets = keep.tile([P, N // 16], U16, name="offsets")
         win = [keep.tile([P, C], F32, name="win%d" % t) for t in range(PACK)]
         x_raw = keep.tile([P, PACK, R], F32, name="x_raw")
-        y_raw = [keep.tile([P, RT, KP], F32, name="y_raw%d" % g) for g in range(G)]
-        norm_col = keep.tile([P, G, PACK], F32, name="norm_col")
+        y_raw = {}
+        norm_col = keep.tile([P, G, PACK], F32, name="norm_col", tag="x_bf", align_bytes=64)
         ts_col = keep.tile([P, G, 1, PACK], F32, name="ts_col")
         wt_col = keep.tile([P, PACK], F32, name="wt_col")
         cb_planes = cb.rearrange("(p t) c -> t p c", t=PACK)
 
-        def load_y(g):
-            nc.sync.dma_start(out=y_raw[g][:], in_=y[:, g * KP:(g + 1) * KP].rearrange("(i p) c -> p i c", p=P))
+        def load_y(g, first, count, tag):
+            rows = keep.tile([P, count, KP], F32, name=tag + "_y", tag=tag)
+            nc.sync.dma_start(out=rows[:], in_=y[first * P:(first + count) * P, g * KP:(g + 1) * KP].rearrange(
+                "(i p) c -> p i c", p=P))
+            for i in range(count):
+                y_raw[g, first + i] = rows[:, i, :]
 
+        nc.sync.dma_start(out=x_raw[:], in_=xT.rearrange("(p t) r -> p t r", t=PACK))
         nc.sync.dma_start(offsets[:], offs)
         nc.scalar.dma_start(out=wt_col[:], in_=wt.rearrange("(p j) o -> p (j o)", j=PACK))
         nc.scalar.dma_start(out=ts_col[:, :, 0, :], in_=ts[0:1, :].rearrange("o (g p j) -> p (o g) j", g=G, j=PACK))
-        nc.sync.dma_start(out=norm_col[:], in_=norm[0:1, :].rearrange("o (g p j) -> p (o g) j", g=G, j=PACK))
+        nc.scalar.dma_start(out=norm_col[:], in_=norm[0:1, :].rearrange("o (g p j) -> p (o g) j", g=G, j=PACK))
         nc.sync.dma_start(out=win[0][:], in_=cb_planes[0])
-        load_y(0)
-        nc.sync.dma_start(out=x_raw[:], in_=xT.rearrange("(p t) r -> p t r", t=PACK))
+        load_y(0, 0, RT, "y0")
         nc.sync.dma_start(out=win[1][:], in_=cb_planes[1])
-        load_y(1)
+        load_y(1, 0, 2, "y1")
         nc.sync.dma_start(out=win[2][:], in_=cb_planes[2])
         nc.sync.dma_start(out=win[3][:], in_=cb_planes[3])
+        load_y(1, 2, 2, "y2")
 
         ident = keep.tile([P, P], F32, name="ident")
         make_identity(nc, ident[:])
@@ -77,11 +82,13 @@ def tile_attend_gpq_lch_x_kernel(tc, xT, cb, norm, ts, y, wt, offs, out):
 
         yT = [keep.tile([P, PACK, R], F32, name="yT%d" % g) for g in range(G)]
 
-        def turn_y(g, t):
-            bank = psum.tile([P, RT, P], F32, name="turn", tag="turn")
-            for i in range(RT):
-                nc.tensor.transpose(bank[:, i, :], y_raw[g][:, i, t:KP:PACK], ident[:])
-            nc.scalar.copy(out=yT[g][:, t, :], in_=bank[:].rearrange("m i p -> m (i p)"))
+        def turn_y(g, first_a, count_a, first_i, count_i):
+            bank = psum.tile([P, count_a, count_i, P], F32, name="turn", tag="turn")
+            for a in range(count_a):
+                for i in range(count_i):
+                    nc.tensor.transpose(bank[:, a, i, :], y_raw[g, first_i + i][:, first_a + a:KP:PACK], ident[:])
+            nc.scalar.copy(out=yT[g][:, first_a:first_a + count_a, first_i * P:(first_i + count_i) * P],
+                           in_=bank[:].rearrange("m a i p -> m a (i p)"))
 
         k_d = [keep.tile([P, PACK, P, PACK], BF16, name="k_d%d" % g, tag="k_d%d" % g, align_bytes=64) for g in range(G)]
         k_n = keep.tile([P, G, PACK, KP], BF16, name="k_n", align_bytes=64)
@@ -104,9 +111,9 @@ def tile_attend_gpq_lch_x_kernel(tc, xT, cb, norm, ts, y, wt, offs, out):
             src = k32[t, g].rearrange("p (m a) -> p a m", a=PACK)
             copy(out=k_d[g][:, tiles, ms, t], in_=src[:, tiles, ms])
 
-        def place_early(g):
-            src = k_f32[g][:, 0:PACK - 1, :].rearrange("p t (m a) -> p m a t", a=PACK)
-            nc.vector.tensor_copy(out=k_d[g][:, :, :, 0:PACK - 1].rearrange("p a m t -> p m a t"), in_=src)
+        def place_pair(g, copy):
+            src = k_f32[g][:, 0:2, :].rearrange("p t (m a) -> p m a t", a=PACK)
+            copy(out=k_d[g][:, :, :, 0:2].rearrange("p a m t -> p m a t"), in_=src)
 
         pairs = {}
         k_bank = {}
@@ -133,12 +140,15 @@ def tile_attend_gpq_lch_x_kernel(tc, xT, cb, norm, ts, y, wt, offs, out):
             nc.vector.quantize_mx(out=kn_codes[:, g, cols].bitcast(E4), scales=kn_scales[:, g, cols],
                                   in_=k_n[:, g, t:t + planes, :].rearrange("m t c -> m (t c)"))
 
-        x_bf = keep.tile([P, R, PACK], BF16, name="x_bf", align_bytes=64)
+        x_bf = keep.tile([P, R, PACK], BF16, name="x_bf", tag="x_bf", align_bytes=64)
         x_codes = keep.tile([P, R], U32, name="x_codes", align_bytes=64)
         x_scales = keep.tile([P, R], U8, name="x_scales", align_bytes=64)
 
         on_v, on_s = nc.vector.tensor_copy, nc.scalar.copy
         low, high = slice(0, 2), slice(2, 4)
+        nc.scalar.copy(out=x_bf[:], in_=x_raw[:].rearrange("p t r -> p r t"))
+        nc.vector.quantize_mx(out=x_codes[:].bitcast(E4), scales=x_scales[:],
+                              in_=x_bf[:].rearrange("p r t -> p (r t)"))
         for t in range(PACK - 1):
             for g in range(G):
                 gather(t, g)
@@ -146,21 +156,21 @@ def tile_attend_gpq_lch_x_kernel(tc, xT, cb, norm, ts, y, wt, offs, out):
                 round_k(t, g)
             for g in range(G):
                 turn_k(t, g)
-                if t == PACK - 2:
-                    place_early(g)
-            for g in range(G):
-                if (t, g) != (PACK - 2, G - 1):
+                if t == 1:
+                    place_pair(g, on_v if g == 0 else on_s)
+            if t == 2:
+                place(t, 0, on_v)
+                place(t, 1, on_v, low)
+                place(t, 1, on_s, high)
+            else:
+                for g in range(G):
                     quant_kn(t, g)
             if t == 0:
                 for a in range(PACK):
-                    turn_y(0, a)
-            if t == 0:
-                nc.scalar.copy(out=x_bf[:], in_=x_raw[:].rearrange("p t r -> p r t"))
-                nc.vector.quantize_mx(out=x_codes[:].bitcast(E4), scales=x_scales[:],
-                                      in_=x_bf[:].rearrange("p r t -> p (r t)"))
+                    turn_y(0, a, 1, 0, RT)
             if t == 1:
-                for a in range(PACK):
-                    turn_y(1, a)
+                for a in range(0, PACK, 2):
+                    turn_y(1, a, 2, 0, 2)
 
         kd_codes = [keep.tile([P, KP], U32, name="kd_codes%d" % g, align_bytes=64) for g in range(G)]
         kd_scales = [keep.tile([P, KP], U8, name="kd_scales%d" % g, align_bytes=64) for g in range(G)]
@@ -214,11 +224,16 @@ def tile_attend_gpq_lch_x_kernel(tc, xT, cb, norm, ts, y, wt, offs, out):
             res = ring.tile([P, D], F32, name="res", tag="res")
             dst = res[:].rearrange("r (p t) -> r p t", t=PACK)
             src = sums[i][:].rearrange("r (t p) -> r p t", t=PACK)
-            if i == RT - 1:
-                nc.vector.tensor_copy(out=dst, in_=src)
-            else:
+            rows = slice(i * P, (i + 1) * P)
+            if i < RT - 1:
                 nc.scalar.copy(out=dst, in_=src)
-            nc.sync.dma_start(out=out[i * P:(i + 1) * P, :], in_=res[:])
+                nc.sync.dma_start(out=out[rows, :], in_=res[:])
+            else:
+                for e in range(2):
+                    ps = slice(e * P // 2, (e + 1) * P // 2)
+                    cols = slice(e * D // 2, (e + 1) * D // 2)
+                    nc.vector.tensor_copy(out=dst[:, ps, :], in_=src[:, ps, :])
+                    nc.sync.dma_start(out=out[rows, cols], in_=res[:, cols])
 
         last = PACK - 1
         gather(last, 0, parts=2)
@@ -230,6 +245,8 @@ def tile_attend_gpq_lch_x_kernel(tc, xT, cb, norm, ts, y, wt, offs, out):
         place(last, 1, on_v, low)
         for a in range(PACK):
             scores(0, a)
+        for a in range(0, PACK, 2):
+            turn_y(1, a, 2, 2, 2)
         round_k(last, 0)
         round_k(last, 1)
         quant_kd(1)
@@ -242,14 +259,14 @@ def tile_attend_gpq_lch_x_kernel(tc, xT, cb, norm, ts, y, wt, offs, out):
             tanh(0, i)
         for a in range(PACK):
             residual(1, a)
-        for i in range(RT):
-            weigh(0, i)
-            tanh(1, i)
-        quant_kn(last, 0)
-        quant_h(0, 0, tiles=RT)
-        quant_kn(last - 1, 1, planes=2)
-        for i in range(RT):
-            grad(0, i)
+        for e in range(2):
+            for i in range(2 * e, 2 * e + 2):
+                weigh(0, i)
+                tanh(1, i)
+            quant_kn(last - 1, e, planes=2)
+            quant_h(0, 2 * e, tiles=2)
+            for i in range(2 * e, 2 * e + 2):
+                grad(0, i)
         weigh(1, 0)
         for i in range(RT):
             if i + 1 < RT:

@@ -53,8 +53,8 @@ def tile_attend_gpq_lch_x_kernel(tc, xT, cb, norm, ts, y, wt, offs, out):
         nc.scalar.dma_start(out=wt_col[:], in_=wt.rearrange("(p j) o -> p (j o)", j=PACK))
         nc.scalar.dma_start(out=ts_col[:, :, 0, :], in_=ts[0:1, :].rearrange("o (g p j) -> p (o g) j", g=G, j=PACK))
         nc.scalar.dma_start(out=norm_col[:], in_=norm[0:1, :].rearrange("o (g p j) -> p (o g) j", g=G, j=PACK))
-        nc.sync.dma_start(out=win[0][:], in_=cb_planes[0])
         load_y(0, 0, RT, "y0")
+        nc.sync.dma_start(out=win[0][:], in_=cb_planes[0])
         nc.sync.dma_start(out=win[1][:], in_=cb_planes[1])
         load_y(1, 0, 2, "y1")
         nc.sync.dma_start(out=win[2][:], in_=cb_planes[2])
@@ -111,12 +111,7 @@ def tile_attend_gpq_lch_x_kernel(tc, xT, cb, norm, ts, y, wt, offs, out):
             src = k32[t, g].rearrange("p (m a) -> p a m", a=PACK)
             copy(out=k_d[g][:, tiles, ms, t], in_=src[:, tiles, ms])
 
-        def place_pair(g, copy):
-            src = k_f32[g][:, 0:2, :].rearrange("p t (m a) -> p m a t", a=PACK)
-            copy(out=k_d[g][:, :, :, 0:2].rearrange("p a m t -> p m a t"), in_=src)
-
         pairs = {}
-        k_bank = {}
 
         def round_k(t, g):
             if t < PACK - 1:
@@ -149,6 +144,8 @@ def tile_attend_gpq_lch_x_kernel(tc, xT, cb, norm, ts, y, wt, offs, out):
         nc.scalar.copy(out=x_bf[:], in_=x_raw[:].rearrange("p t r -> p r t"))
         nc.vector.quantize_mx(out=x_codes[:].bitcast(E4), scales=x_scales[:],
                               in_=x_bf[:].rearrange("p r t -> p (r t)"))
+        for a in range(PACK):
+            turn_y(0, a, 1, 0, RT)
         for t in range(PACK - 1):
             for g in range(G):
                 gather(t, g)
@@ -156,18 +153,10 @@ def tile_attend_gpq_lch_x_kernel(tc, xT, cb, norm, ts, y, wt, offs, out):
                 round_k(t, g)
             for g in range(G):
                 turn_k(t, g)
-                if t == 1:
-                    place_pair(g, on_v if g == 0 else on_s)
-            if t == 2:
-                place(t, 0, on_v)
-                place(t, 1, on_v, low)
-                place(t, 1, on_s, high)
-            else:
+                place(t, g, on_v)
+            if t < PACK - 2:
                 for g in range(G):
                     quant_kn(t, g)
-            if t == 0:
-                for a in range(PACK):
-                    turn_y(0, a, 1, 0, RT)
             if t == 1:
                 for a in range(0, PACK, 2):
                     turn_y(1, a, 2, 0, 2)
@@ -181,9 +170,10 @@ def tile_attend_gpq_lch_x_kernel(tc, xT, cb, norm, ts, y, wt, offs, out):
         th = {}
         sums = {}
 
-        def quant_kd(g):
-            nc.vector.quantize_mx(out=kd_codes[g][:].bitcast(E4), scales=kd_scales[g][:],
-                                  in_=k_d[g][:].rearrange("p a m t -> p (a m t)"))
+        def quant_kd(g, tiles=slice(0, PACK)):
+            cols = slice(tiles.start * P, tiles.stop * P)
+            nc.vector.quantize_mx(out=kd_codes[g][:, cols].bitcast(E4), scales=kd_scales[g][:, cols],
+                                  in_=k_d[g][:, tiles, :, :].rearrange("p a m t -> p (a m t)"))
 
         acc = {}
 
@@ -236,13 +226,13 @@ def tile_attend_gpq_lch_x_kernel(tc, xT, cb, norm, ts, y, wt, offs, out):
                     nc.sync.dma_start(out=out[rows, cols], in_=res[:, cols])
 
         last = PACK - 1
-        gather(last, 0, parts=2)
-        place(last, 0, on_s, ms=slice(0, P // 2))
-        place(last, 0, on_s, ms=slice(P // 2, P))
+        gather(last, 0)
+        place(last, 0, on_s, low)
+        place(last, 0, on_s, high)
         gather(last, 1)
-        place(last, 1, on_s, high)
-        quant_kd(0)
-        place(last, 1, on_v, low)
+        quant_kd(0, low)
+        place(last, 1, on_v)
+        quant_kd(0, high)
         for a in range(PACK):
             scores(0, a)
         for a in range(0, PACK, 2):

@@ -33,7 +33,7 @@ def tile_attend_gpq_lch_x_kernel(tc, xT, cb, norm, ts, y, wt, offs, out):
         psum = ctx.enter_context(tc.psum_pool(name="psum", bufs=4))
 
         offsets = keep.tile([P, N // 16], U16, name="offsets")
-        win = [keep.tile([P, C], F32, name="win%d" % t) for t in range(PACK)]
+        win = [keep.tile([P, C], F32, name="win%d" % t, tag="win%d" % t, align_bytes=64) for t in range(PACK)]
         x_raw = keep.tile([P, PACK, R], F32, name="x_raw")
         y_raw = {}
         norm_col = keep.tile([P, G, PACK], F32, name="norm_col", tag="x_bf", align_bytes=64)
@@ -41,25 +41,28 @@ def tile_attend_gpq_lch_x_kernel(tc, xT, cb, norm, ts, y, wt, offs, out):
         wt_col = keep.tile([P, PACK], F32, name="wt_col")
         cb_planes = cb.rearrange("(p t) c -> t p c", t=PACK)
 
-        def load_y(g, first, count, tag):
-            rows = keep.tile([P, count, KP], F32, name=tag + "_y", tag=tag)
-            nc.sync.dma_start(out=rows[:], in_=y[first * P:(first + count) * P, g * KP:(g + 1) * KP].rearrange(
-                "(i p) c -> p i c", p=P))
-            for i in range(count):
-                y_raw[g, first + i] = rows[:, i, :]
+        def load_y(name, first, halves):
+            width = len(halves) * KP
+            rows = keep.tile([P, 2, width], F32, name=name)
+            nc.sync.dma_start(out=rows[:], in_=y[first * P:(first + 2) * P, halves[0] * KP:halves[0] * KP + width]
+                              .rearrange("(i p) c -> p i c", p=P))
+            for i in range(2):
+                for e, g in enumerate(halves):
+                    y_raw[g, first + i] = rows[:, i, e * KP:(e + 1) * KP]
 
         nc.sync.dma_start(out=x_raw[:], in_=xT.rearrange("(p t) r -> p t r", t=PACK))
         nc.sync.dma_start(offsets[:], offs)
         nc.scalar.dma_start(out=wt_col[:], in_=wt.rearrange("(p j) o -> p (j o)", j=PACK))
         nc.scalar.dma_start(out=ts_col[:, :, 0, :], in_=ts[0:1, :].rearrange("o (g p j) -> p (o g) j", g=G, j=PACK))
         nc.scalar.dma_start(out=norm_col[:], in_=norm[0:1, :].rearrange("o (g p j) -> p (o g) j", g=G, j=PACK))
-        load_y(0, 0, RT, "y0")
+        load_y("y_top0", 0, (0,))
         nc.sync.dma_start(out=win[0][:], in_=cb_planes[0])
         nc.sync.dma_start(out=win[1][:], in_=cb_planes[1])
-        load_y(1, 0, 2, "y1")
+        load_y("y_low0", 2, (0,))
         nc.sync.dma_start(out=win[2][:], in_=cb_planes[2])
         nc.sync.dma_start(out=win[3][:], in_=cb_planes[3])
-        load_y(1, 2, 2, "y2")
+        load_y("y_top1", 0, (1,))
+        load_y("y_low1", 2, (1,))
 
         ident = keep.tile([P, P], F32, name="ident")
         make_identity(nc, ident[:])
@@ -94,7 +97,7 @@ def tile_attend_gpq_lch_x_kernel(tc, xT, cb, norm, ts, y, wt, offs, out):
         k_n = keep.tile([P, G, PACK, KP], BF16, name="k_n", align_bytes=64)
         k_n_words = k_n[:].rearrange("m g t c -> m (g t c)").bitcast(F32).rearrange(
             "m (g t p u) -> m g t p u", g=G, t=PACK, u=2)
-        kn_codes = keep.tile([P, G, D], U32, name="kn_codes", align_bytes=64)
+        kn_codes = keep.tile([P, G, D], U32, name="kn_codes", tag="win1", align_bytes=64)
         kn_scales = keep.tile([P, G, D], U8, name="kn_scales", align_bytes=64)
         k_f32 = [keep.tile([P, PACK, KP], F32, name="k_f32_%d" % g) for g in range(G)]
         k32 = {(t, g): k_f32[g][:, t, :] for t in range(PACK) for g in range(G)}
@@ -144,8 +147,8 @@ def tile_attend_gpq_lch_x_kernel(tc, xT, cb, norm, ts, y, wt, offs, out):
         nc.scalar.copy(out=x_bf[:], in_=x_raw[:].rearrange("p t r -> p r t"))
         nc.vector.quantize_mx(out=x_codes[:].bitcast(E4), scales=x_scales[:],
                               in_=x_bf[:].rearrange("p r t -> p (r t)"))
-        for a in range(PACK):
-            turn_y(0, a, 1, 0, RT)
+        for a in range(0, PACK, 2):
+            turn_y(0, a, 2, 0, 2)
         for t in range(PACK - 1):
             for g in range(G):
                 gather(t, g)
@@ -153,13 +156,13 @@ def tile_attend_gpq_lch_x_kernel(tc, xT, cb, norm, ts, y, wt, offs, out):
                 round_k(t, g)
             for g in range(G):
                 turn_k(t, g)
-                place(t, g, on_v)
+                place(t, g, on_s if (t, g) == (PACK - 2, 0) else on_v)
             if t < PACK - 2:
                 for g in range(G):
                     quant_kn(t, g)
             if t == 1:
                 for a in range(0, PACK, 2):
-                    turn_y(1, a, 2, 0, 2)
+                    turn_y(0, a, 2, 2, 2)
 
         kd_codes = [keep.tile([P, KP], U32, name="kd_codes%d" % g, align_bytes=64) for g in range(G)]
         kd_scales = [keep.tile([P, KP], U8, name="kd_scales%d" % g, align_bytes=64) for g in range(G)]
@@ -236,23 +239,30 @@ def tile_attend_gpq_lch_x_kernel(tc, xT, cb, norm, ts, y, wt, offs, out):
         for a in range(PACK):
             scores(0, a)
         for a in range(0, PACK, 2):
-            turn_y(1, a, 2, 2, 2)
-        round_k(last, 0)
-        round_k(last, 1)
+            turn_y(1, a, 2, 0, 2)
+        turn_y(1, 0, 2, 2, 2)
         quant_kd(1)
         for a in range(PACK):
             residual(0, a)
+            if a < 2:
+                scores(1, a)
+        turn_y(1, 2, 2, 2, 2)
+        for a in range(2, PACK):
             scores(1, a)
-        for g in range(G):
-            turn_k(last, g)
         for i in range(RT):
             tanh(0, i)
-        for a in range(PACK):
-            residual(1, a)
+        for g in range(G):
+            round_k(last, g)
+        for g in range(G):
+            turn_k(last, g)
         for e in range(2):
+            for a in range(2 * e, 2 * e + 2):
+                residual(1, a)
             for i in range(2 * e, 2 * e + 2):
                 weigh(0, i)
-                tanh(1, i)
+        for i in range(RT):
+            tanh(1, i)
+        for e in range(2):
             quant_kn(last - 1, e, planes=2)
             quant_h(0, 2 * e, tiles=2)
             for i in range(2 * e, 2 * e + 2):

@@ -30,147 +30,153 @@ def tile_attend_gpq_lch_x_kernel(tc, xT, cb, norm, ts, y, wt, offs, out):
     with ExitStack() as ctx:
         keep = ctx.enter_context(tc.tile_pool(name="keep", bufs=1))
         ring = ctx.enter_context(tc.tile_pool(name="ring", bufs=4))
-        psum = ctx.enter_context(tc.psum_pool(name="psum", bufs=4))
+        shared = ctx.enter_context(tc.tile_pool(name="shared", bufs=1))
+        psum = ctx.enter_context(tc.psum_pool(name="psum", bufs=1))
+
+        def bank(b, shape):
+            return psum.tile(shape, F32, name="bank%d" % b, tag="bank%d" % b)
 
         offsets = keep.tile([P, N // 16], U16, name="offsets")
         win = [keep.tile([P, C], F32, name="win%d" % t, tag="win%d" % t, align_bytes=64) for t in range(PACK)]
         x_raw = keep.tile([P, PACK, R], F32, name="x_raw")
         y_raw = {}
-        norm_col = keep.tile([P, G, PACK], F32, name="norm_col", tag="x_bf", align_bytes=64)
-        ts_col = keep.tile([P, G, 1, PACK], F32, name="ts_col")
+        norm_col = keep.tile([P, G, PACK], F32, name="norm_col")
+        ts_col = keep.tile([P, G, PACK], F32, name="ts_col")
         wt_col = keep.tile([P, PACK], F32, name="wt_col")
         cb_planes = cb.rearrange("(p t) c -> t p c", t=PACK)
 
-        def load_y(name, first, halves):
-            width = len(halves) * KP
-            rows = keep.tile([P, 2, width], F32, name=name)
-            nc.sync.dma_start(out=rows[:], in_=y[first * P:(first + 2) * P, halves[0] * KP:halves[0] * KP + width]
+        def load_y(g, half):
+            rows = keep.tile([P, 2, KP], F32, name="y%d_%d" % (g, half))
+            nc.sync.dma_start(out=rows[:], in_=y[half * 2 * P:(half + 1) * 2 * P, g * KP:(g + 1) * KP]
                               .rearrange("(i p) c -> p i c", p=P))
-            for i in range(2):
-                for e, g in enumerate(halves):
-                    y_raw[g, first + i] = rows[:, i, e * KP:(e + 1) * KP]
+            y_raw[g, half] = rows
 
-        nc.sync.dma_start(out=x_raw[:], in_=xT.rearrange("(p t) r -> p t r", t=PACK))
-        nc.sync.dma_start(offsets[:], offs)
-        nc.scalar.dma_start(out=wt_col[:], in_=wt.rearrange("(p j) o -> p (j o)", j=PACK))
-        nc.scalar.dma_start(out=ts_col[:, :, 0, :], in_=ts[0:1, :].rearrange("o (g p j) -> p (o g) j", g=G, j=PACK))
-        nc.scalar.dma_start(out=norm_col[:], in_=norm[0:1, :].rearrange("o (g p j) -> p (o g) j", g=G, j=PACK))
-        load_y("y_top0", 0, (0,))
+        nc.sync.dma_start(out=wt_col[:], in_=wt.rearrange("(p j) o -> p (j o)", j=PACK))
+        nc.sync.dma_start(out=ts_col[:], in_=ts[0:1, :].rearrange("o (g p j) -> p (o g) j", g=G, j=PACK))
+        nc.sync.dma_start(out=norm_col[:], in_=norm[0:1, :].rearrange("o (g p j) -> p (o g) j", g=G, j=PACK))
         nc.sync.dma_start(out=win[0][:], in_=cb_planes[0])
+        nc.sync.dma_start(offsets[:], offs)
+        nc.sync.dma_start(out=x_raw[:], in_=xT.rearrange("(p t) r -> p t r", t=PACK))
         nc.sync.dma_start(out=win[1][:], in_=cb_planes[1])
-        load_y("y_low0", 2, (0,))
         nc.sync.dma_start(out=win[2][:], in_=cb_planes[2])
+        load_y(0, 0)
         nc.sync.dma_start(out=win[3][:], in_=cb_planes[3])
-        load_y("y_top1", 0, (1,))
-        load_y("y_low1", 2, (1,))
+        load_y(0, 1)
+        load_y(1, 0)
+        load_y(1, 1)
 
         ident = keep.tile([P, P], F32, name="ident")
         make_identity(nc, ident[:])
 
-        def spread(col, row):
-            bank = psum.tile([P, PACK, P], F32, name="turn", tag="turn")
+        def spread(b, col):
+            turned = bank(b, [P, PACK, P])
             for j in range(PACK):
-                nc.tensor.transpose(bank[:, j, :], col[:, j:j + 1].to_broadcast([P, P]), ident[:])
-            nc.scalar.copy(out=row.rearrange("m (p j) -> m p j", j=PACK), in_=bank[:].rearrange("m j p -> m p j"))
+                nc.tensor.transpose(turned[:, j, :], col[:, j:j + 1].to_broadcast([P, P]), ident[:])
+            return turned
 
-        wt_row = keep.tile([P, R, 1], F32, name="wt_row")
-        spread(wt_col[:], wt_row[:, :, 0])
+        wt_row = keep.tile([P, R], F32, name="wt_row", tag="wt_row")
+        nc.scalar.copy(out=wt_row[:].rearrange("q (p j) -> q p j", j=PACK),
+                       in_=spread(0, wt_col[:])[:].rearrange("q j p -> q p j"))
         norm_row = keep.tile([P, G, KP], F32, name="norm_row")
         for g in range(G):
-            spread(norm_col[:, g, :], norm_row[:, g, :])
-        weight = [keep.tile([P, R, PACK], F32, name="weight%d" % g) for g in range(G)]
+            nc.scalar.copy(out=norm_row[:, g, :].rearrange("q (p j) -> q p j", j=PACK),
+                           in_=spread(1 + g, norm_col[:, g, :])[:].rearrange("q j p -> q p j"))
+        weight = [keep.tile([P, PACK, R], F32, name="weight%d" % g) for g in range(G)]
         for g in range(G):
-            nc.vector.tensor_tensor(weight[g][:], wt_row[:].to_broadcast([P, R, PACK]),
-                                    ts_col[:, g, :, :].to_broadcast([P, R, PACK]), MULT)
+            for a in range(PACK):
+                nc.vector.tensor_scalar(weight[g][:, a, :], wt_row[:], ts_col[:, g, a:a + 1], None, MULT)
 
-        yT = [keep.tile([P, PACK, R], F32, name="yT%d" % g) for g in range(G)]
+        yT = {0: keep.tile([P, PACK, R], F32, name="yT0", tag="yT0", align_bytes=64)}
 
-        def turn_y(g, first_a, count_a, first_i, count_i):
-            bank = psum.tile([P, count_a, count_i, P], F32, name="turn", tag="turn")
-            for a in range(count_a):
-                for i in range(count_i):
-                    nc.tensor.transpose(bank[:, a, i, :], y_raw[g, first_i + i][:, first_a + a:KP:PACK], ident[:])
-            nc.scalar.copy(out=yT[g][:, first_a:first_a + count_a, first_i * P:(first_i + count_i) * P],
-                           in_=bank[:].rearrange("m a i p -> m a (i p)"))
+        def turn_y(b, g, half, pair):
+            turned = bank(b, [P, 2, 2, P])
+            for e in range(2):
+                for i in range(2):
+                    nc.tensor.transpose(turned[:, e, i, :], y_raw[g, half][:, i, 2 * pair + e:KP:PACK], ident[:])
+            nc.scalar.copy(out=yT[g][:, 2 * pair:2 * pair + 2, half * 2 * P:(half + 1) * 2 * P],
+                           in_=turned[:].rearrange("m e i p -> m e (i p)"))
 
-        k_d = [keep.tile([P, PACK, P, PACK], BF16, name="k_d%d" % g, tag="k_d%d" % g, align_bytes=64) for g in range(G)]
+        def turn_low_y(a):
+            turned = bank(a, [P, 2, P])
+            for i in range(2):
+                nc.tensor.transpose(turned[:, i, :], y_raw[0, 1][:, i, a:KP:PACK], ident[:])
+            nc.scalar.copy(out=yT[0][:, a, 2 * P:], in_=turned[:].rearrange("m i p -> m (i p)"))
+
+        def turn_late_y(b, a):
+            turned = bank(b, [P, RT, P])
+            for i in range(RT):
+                nc.tensor.transpose(turned[:, i, :], y_raw[1, i // 2][:, i % 2, a:KP:PACK], ident[:])
+            nc.scalar.copy(out=yT[1][:, a, :], in_=turned[:].rearrange("m i p -> m (i p)"))
+
+        early_pairs = [keep.tile([P, PACK - 1, 2, P, 2], BF16, name="pairs%d" % g, align_bytes=64) for g in range(G)]
+        pairs = {(t, g): early_pairs[g][:, t] for t in range(PACK - 1) for g in range(G)}
+        k_d = [keep.tile([P, PACK, P, PACK], BF16, name="k_d%d" % g, align_bytes=64) for g in range(G)]
         k_n = keep.tile([P, G, PACK, KP], BF16, name="k_n", align_bytes=64)
         k_n_words = k_n[:].rearrange("m g t c -> m (g t c)").bitcast(F32).rearrange(
             "m (g t p u) -> m g t p u", g=G, t=PACK, u=2)
-        kn_codes = keep.tile([P, G, D], U32, name="kn_codes", tag="win1", align_bytes=64)
+        kn_codes = keep.tile([P, G, D], U32, name="kn_codes", tag="win2", align_bytes=64)
         kn_scales = keep.tile([P, G, D], U8, name="kn_scales", align_bytes=64)
-        k_f32 = [keep.tile([P, PACK, KP], F32, name="k_f32_%d" % g) for g in range(G)]
-        k32 = {(t, g): k_f32[g][:, t, :] for t in range(PACK) for g in range(G)}
+        picked = {}
 
-        def gather(t, g, parts=1):
-            width = KP // parts
-            for c in range(parts):
-                first = (g * KP + c * width) // 16
-                nc.vector.tensor_tensor(k32[t, g][:, c * width:(c + 1) * width],
-                                        win[t][:].indirect(offsets[:, first:first + width // 16]),
-                                        norm_row[:, g, c * width:(c + 1) * width], MULT)
-
-        def place(t, g, copy, tiles=slice(0, PACK), ms=slice(0, P)):
-            src = k32[t, g].rearrange("p (m a) -> p a m", a=PACK)
-            copy(out=k_d[g][:, tiles, ms, t], in_=src[:, tiles, ms])
-
-        pairs = {}
+        def gather(t, g):
+            if (t, g) == (0, 0):
+                picked[t, g] = keep.tile([P, KP], F32, name="picked_first", tag="wt_row")
+            else:
+                picked[t, g] = ring.tile([P, KP], F32, name="picked", tag="picked")
+            first = g * KP // 16
+            nc.vector.tensor_tensor(picked[t, g][:], win[t][:].indirect(offsets[:, first:first + KP // 16]),
+                                    norm_row[:, g, :], MULT)
 
         def round_k(t, g):
-            if t < PACK - 1:
-                pairs[t, g] = ring.tile([P, KP], BF16, name="pairs", tag="pairs")
-            elif g == 0:
-                late_pairs = keep.tile([P, G, KP], BF16, name="late_pairs", tag="k_d0", align_bytes=64)
-                for e in range(G):
-                    pairs[t, e] = late_pairs[:, e, :]
-            nc.scalar.copy(out=pairs[t, g][:].rearrange("p (u m e) -> p u m e", u=2, e=2),
-                           in_=k32[t, g].rearrange("p (m u e) -> p u m e", u=2, e=2))
+            nc.scalar.copy(out=pairs[t, g],
+                           in_=picked[t, g][:].rearrange("p (m u e) -> p u m e", u=2, e=2))
 
-        def turn_k(t, g):
-            bank = psum.tile([P, 2, P], F32, name="turn", tag="turn")
-            words = pairs[t, g][:].bitcast(F32)
-            for u in range(2):
-                nc.tensor.transpose(bank[:, u, :], words[:, u * P:(u + 1) * P], ident[:])
-            nc.scalar.copy(out=k_n_words[:, g, t, :, :], in_=bank[:].rearrange("m u p -> m p u"))
+        def place_one(t, g, copy, tiles=slice(0, PACK)):
+            copy(out=k_d[g][:, tiles, :, t], in_=picked[t, g][:].rearrange("p (m a) -> p a m", a=PACK)[:, tiles, :])
 
-        def quant_kn(t, g, planes=1):
+        def turn_k(b, t):
+            turned = bank(b, [P, G, 2, P])
+            for g in range(G):
+                words = pairs[t, g].rearrange("p u m e -> p (u m e)").bitcast(F32)
+                for u in range(2):
+                    nc.tensor.transpose(turned[:, g, u, :], words[:, u * P:(u + 1) * P], ident[:])
+            nc.scalar.copy(out=k_n_words[:, :, t, :, :], in_=turned[:].rearrange("m g u p -> m g p u"))
+
+        def quant_kn(g, t, planes=1):
             cols = slice(t * P, (t + planes) * P)
             nc.vector.quantize_mx(out=kn_codes[:, g, cols].bitcast(E4), scales=kn_scales[:, g, cols],
                                   in_=k_n[:, g, t:t + planes, :].rearrange("m t c -> m (t c)"))
 
-        x_bf = keep.tile([P, R, PACK], BF16, name="x_bf", tag="x_bf", align_bytes=64)
+        x_bf = keep.tile([P, R, PACK], BF16, name="x_bf", align_bytes=64)
         x_codes = keep.tile([P, R], U32, name="x_codes", align_bytes=64)
         x_scales = keep.tile([P, R], U8, name="x_scales", align_bytes=64)
 
         on_v, on_s = nc.vector.tensor_copy, nc.scalar.copy
-        low, high = slice(0, 2), slice(2, 4)
-        nc.scalar.copy(out=x_bf[:], in_=x_raw[:].rearrange("p t r -> p r t"))
-        nc.vector.quantize_mx(out=x_codes[:].bitcast(E4), scales=x_scales[:],
-                              in_=x_bf[:].rearrange("p r t -> p (r t)"))
-        for a in range(0, PACK, 2):
-            turn_y(0, a, 2, 0, 2)
         for t in range(PACK - 1):
             for g in range(G):
                 gather(t, g)
             for g in range(G):
                 round_k(t, g)
-            for g in range(G):
-                turn_k(t, g)
-                place(t, g, on_s if (t, g) == (PACK - 2, 0) else on_v)
-            if t < PACK - 2:
-                for g in range(G):
-                    quant_kn(t, g)
-            if t == 1:
-                for a in range(0, PACK, 2):
-                    turn_y(0, a, 2, 2, 2)
+                place_one(t, g, on_v)
+            turn_k(3 + t, t)
+            if t == 0:
+                nc.scalar.copy(out=x_bf[:].rearrange("p (c i) t -> p c t i", i=2),
+                               in_=x_raw[:].rearrange("p t (c i) -> p c t i", i=2))
+                nc.vector.quantize_mx(out=x_codes[:].bitcast(E4), scales=x_scales[:],
+                                      in_=x_bf[:].rearrange("p r t -> p (r t)"))
+        for g in range(G):
+            quant_kn(g, 0, planes=2)
+        for pair in range(2):
+            turn_y(pair, 0, 0, pair)
 
-        kd_codes = [keep.tile([P, KP], U32, name="kd_codes%d" % g, align_bytes=64) for g in range(G)]
+        kd_codes = {0: keep.tile([P, KP], U32, name="kd_codes0", align_bytes=64)}
         kd_scales = [keep.tile([P, KP], U8, name="kd_scales%d" % g, align_bytes=64) for g in range(G)]
-        z = [keep.tile([P, PACK, R], F32, name="z%d" % g) for g in range(G)]
+        z = [shared.tile([P, PACK, R], F32, name="z0", offset=0, align_bytes=64), keep.tile([P, PACK, R], F32, name="z1")]
+        th = [keep.tile([P, PACK, R], F32, name="th%d" % g) for g in range(G)]
         h_bf = [keep.tile([P, R, PACK], BF16, name="h_bf%d" % g, align_bytes=64) for g in range(G)]
         h_codes = [keep.tile([P, R], U32, name="h_codes%d" % g, align_bytes=64) for g in range(G)]
         h_scales = [keep.tile([P, R], U8, name="h_scales%d" % g, align_bytes=64) for g in range(G)]
-        th = {}
+        acc = {}
         sums = {}
 
         def quant_kd(g, tiles=slice(0, PACK)):
@@ -178,37 +184,34 @@ def tile_attend_gpq_lch_x_kernel(tc, xT, cb, norm, ts, y, wt, offs, out):
             nc.vector.quantize_mx(out=kd_codes[g][:, cols].bitcast(E4), scales=kd_scales[g][:, cols],
                                   in_=k_d[g][:, tiles, :, :].rearrange("p a m t -> p (a m t)"))
 
-        acc = {}
-
-        def scores(g, a):
-            acc[g, a] = psum.tile([P, R], F32, name="acc", tag="acc")
+        def scores(b, g, a):
+            acc[g, a] = bank(b, [P, R])
             cols = slice(a * P, (a + 1) * P)
             nc.tensor.matmul_mx(out=acc[g, a][:], lhsT=kd_codes[g][:, cols].bitcast(E4),
                                 lhsT_scale=kd_scales[g][:, cols],
                                 rhs=x_codes[:].bitcast(E4), rhs_scale=x_scales[:], start=True, stop=True)
 
         def residual(g, a):
-            nc.vector.scalar_tensor_tensor(out=z[g][:, a, :], in0=acc[g, a][:], scalar=ts_col[:, g, 0, a:a + 1],
+            nc.vector.scalar_tensor_tensor(out=z[g][:, a, :], in0=acc[g, a][:], scalar=ts_col[:, g, a:a + 1],
                                            in1=yT[g][:, a, :], op0=MULT, op1=SUB)
+            nc.scalar.activation(out=th[g][:, a, :], in_=z[g][:, a, :], func=TANH)
 
-        def tanh(g, i):
-            th[g, i] = ring.tile([P, P, PACK], F32, name="th", tag="th", bufs=G * RT)
-            nc.scalar.activation(out=th[g, i][:], in_=z[g][:, :, i * P:(i + 1) * P].rearrange("m a r -> m r a"),
-                                 func=TANH)
-
-        def weigh(g, i):
-            rows = slice(i * P, (i + 1) * P)
-            nc.vector.tensor_tensor(h_bf[g][:, rows, :], th[g, i][:], weight[g][:, rows, :], MULT)
+        def weigh(g, i, tiles=1):
+            rows = slice(i * P, (i + tiles) * P)
+            walk = "m a (c i) -> m c a i"
+            nc.vector.tensor_tensor(h_bf[g][:, rows, :].rearrange("m (c i) a -> m c a i", i=2),
+                                    th[g][:, :, rows].rearrange(walk, i=2),
+                                    weight[g][:, :, rows].rearrange(walk, i=2), MULT)
 
         def quant_h(g, i, tiles=1):
             rows = slice(i * P, (i + tiles) * P)
             nc.vector.quantize_mx(out=h_codes[g][:, rows].bitcast(E5), scales=h_scales[g][:, rows],
                                   in_=h_bf[g][:, rows, :].rearrange("m r a -> m (r a)"))
 
-        def grad(g, i):
+        def grad(g, i, b=None):
             rows = slice(i * P, (i + 1) * P)
             if g == 0:
-                sums[i] = psum.tile([P, D], F32, name="acc", tag="acc")
+                sums[i] = bank(b, [P, D])
             nc.tensor.matmul_mx(out=sums[i][:], lhsT=h_codes[g][:, rows].bitcast(E5), lhsT_scale=h_scales[g][:, rows],
                                 rhs=kn_codes[:, g, :].bitcast(E4), rhs_scale=kn_scales[:, g, :],
                                 start=(g == 0), stop=(g == G - 1))
@@ -230,43 +233,42 @@ def tile_attend_gpq_lch_x_kernel(tc, xT, cb, norm, ts, y, wt, offs, out):
 
         last = PACK - 1
         gather(last, 0)
-        place(last, 0, on_s, low)
-        place(last, 0, on_s, high)
+        for u in range(2):
+            place_one(last, 0, on_s, slice(2 * u, 2 * u + 2))
         gather(last, 1)
-        quant_kd(0, low)
-        place(last, 1, on_v)
-        quant_kd(0, high)
         for a in range(PACK):
-            scores(0, a)
-        for a in range(0, PACK, 2):
-            turn_y(1, a, 2, 0, 2)
-        turn_y(1, 0, 2, 2, 2)
-        quant_kd(1)
+            turn_low_y(a)
+        for u in range(2):
+            quant_kd(0, slice(2 * u, 2 * u + 2))
+        for u in range(2):
+            place_one(last, 1, on_v, slice(2 * u, 2 * u + 2))
+        for a in range(PACK):
+            scores(a, 0, a)
         for a in range(PACK):
             residual(0, a)
-            if a < 2:
-                scores(1, a)
-        turn_y(1, 2, 2, 2, 2)
-        for a in range(2, PACK):
-            scores(1, a)
-        for i in range(RT):
-            tanh(0, i)
+        kd_codes[1] = keep.tile([P, KP], U32, name="kd_codes1", tag="yT0", align_bytes=64)
+        quant_kd(1)
+        yT[1] = shared.tile([P, PACK, R], F32, name="yT1", offset=G * 2 * KP, align_bytes=64)
+        for a in range(PACK):
+            if a == 2:
+                for b in range(PACK):
+                    scores(4 + b, 1, b)
+            turn_late_y(a, a)
         for g in range(G):
+            late_pairs = shared.tile([P, 2, P, 2], BF16, name="late_pairs%d" % g, offset=g * 2 * KP, align_bytes=64)
+            pairs[last, g] = late_pairs[:]
             round_k(last, g)
-        for g in range(G):
-            turn_k(last, g)
+        turn_k(2, last)
         for e in range(2):
-            for a in range(2 * e, 2 * e + 2):
-                residual(1, a)
-            for i in range(2 * e, 2 * e + 2):
-                weigh(0, i)
-        for i in range(RT):
-            tanh(1, i)
+            weigh(0, 2 * e, tiles=2)
+        for a in range(PACK):
+            residual(1, a)
         for e in range(2):
-            quant_kn(last - 1, e, planes=2)
             quant_h(0, 2 * e, tiles=2)
-            for i in range(2 * e, 2 * e + 2):
-                grad(0, i)
+        for g in range(G):
+            quant_kn(g, last - 1, planes=2)
+        for i in range(RT):
+            grad(0, i, (0, 1, 4, 5)[i])
         weigh(1, 0)
         for i in range(RT):
             if i + 1 < RT:

@@ -23,6 +23,7 @@ PACK = 4
 KP = P * PACK
 G = N // KP
 RT = R // P
+HALF = R // 2
 
 
 def tile_attend_gpq_lch_x_kernel(tc, xT, cb, norm, ts, y, wt, offs, out):
@@ -30,7 +31,6 @@ def tile_attend_gpq_lch_x_kernel(tc, xT, cb, norm, ts, y, wt, offs, out):
     with ExitStack() as ctx:
         keep = ctx.enter_context(tc.tile_pool(name="keep", bufs=1))
         ring = ctx.enter_context(tc.tile_pool(name="ring", bufs=4))
-        shared = ctx.enter_context(tc.tile_pool(name="shared", bufs=1))
         psum = ctx.enter_context(tc.psum_pool(name="psum", bufs=1))
 
         def bank(b, shape):
@@ -59,11 +59,10 @@ def tile_attend_gpq_lch_x_kernel(tc, xT, cb, norm, ts, y, wt, offs, out):
         nc.sync.dma_start(out=x_raw[:], in_=xT.rearrange("(p t) r -> p t r", t=PACK))
         nc.sync.dma_start(out=win[1][:], in_=cb_planes[1])
         nc.sync.dma_start(out=win[2][:], in_=cb_planes[2])
-        load_y(0, 0)
         nc.sync.dma_start(out=win[3][:], in_=cb_planes[3])
-        load_y(0, 1)
-        load_y(1, 0)
-        load_y(1, 1)
+        for g in range(G):
+            for half in range(2):
+                load_y(g, half)
 
         ident = keep.tile([P, P], F32, name="ident")
         make_identity(nc, ident[:])
@@ -93,23 +92,11 @@ def tile_attend_gpq_lch_x_kernel(tc, xT, cb, norm, ts, y, wt, offs, out):
             for e in range(2):
                 for i in range(2):
                     nc.tensor.transpose(turned[:, e, i, :], y_raw[g, half][:, i, 2 * pair + e:KP:PACK], ident[:])
-            nc.scalar.copy(out=yT[g][:, 2 * pair:2 * pair + 2, half * 2 * P:(half + 1) * 2 * P],
+            nc.scalar.copy(out=yT[g][:, 2 * pair:2 * pair + 2, half * HALF:(half + 1) * HALF],
                            in_=turned[:].rearrange("m e i p -> m e (i p)"))
 
-        def turn_low_y(a):
-            turned = bank(a, [P, 2, P])
-            for i in range(2):
-                nc.tensor.transpose(turned[:, i, :], y_raw[0, 1][:, i, a:KP:PACK], ident[:])
-            nc.scalar.copy(out=yT[0][:, a, 2 * P:], in_=turned[:].rearrange("m i p -> m (i p)"))
-
-        def turn_late_y(b, a):
-            turned = bank(b, [P, RT, P])
-            for i in range(RT):
-                nc.tensor.transpose(turned[:, i, :], y_raw[1, i // 2][:, i % 2, a:KP:PACK], ident[:])
-            nc.scalar.copy(out=yT[1][:, a, :], in_=turned[:].rearrange("m i p -> m (i p)"))
-
-        early_pairs = [keep.tile([P, PACK - 1, 2, P, 2], BF16, name="pairs%d" % g, align_bytes=64) for g in range(G)]
-        pairs = {(t, g): early_pairs[g][:, t] for t in range(PACK - 1) for g in range(G)}
+        pair_planes = [keep.tile([P, PACK, 2, P, 2], BF16, name="pairs%d" % g, align_bytes=64) for g in range(G)]
+        pairs = {(t, g): pair_planes[g][:, t] for t in range(PACK) for g in range(G)}
         k_d = [keep.tile([P, PACK, P, PACK], BF16, name="k_d%d" % g, align_bytes=64) for g in range(G)]
         k_n = keep.tile([P, G, PACK, KP], BF16, name="k_n", align_bytes=64)
         k_n_words = k_n[:].rearrange("m g t c -> m (g t c)").bitcast(F32).rearrange(
@@ -130,6 +117,10 @@ def tile_attend_gpq_lch_x_kernel(tc, xT, cb, norm, ts, y, wt, offs, out):
         def round_k(t, g):
             nc.scalar.copy(out=pairs[t, g],
                            in_=picked[t, g][:].rearrange("p (m u e) -> p u m e", u=2, e=2))
+
+        def place_pair(g, copy):
+            copy(out=k_d[g][:, :, :, 0:2].rearrange("p (u e) m t -> p u e m t", e=2),
+                 in_=pair_planes[g][:, 0:2].rearrange("p t u m e -> p u e m t"))
 
         def place_one(t, g, copy, tiles=slice(0, PACK)):
             copy(out=k_d[g][:, tiles, :, t], in_=picked[t, g][:].rearrange("p (m a) -> p a m", a=PACK)[:, tiles, :])
@@ -157,21 +148,28 @@ def tile_attend_gpq_lch_x_kernel(tc, xT, cb, norm, ts, y, wt, offs, out):
                 gather(t, g)
             for g in range(G):
                 round_k(t, g)
-                place_one(t, g, on_v)
+            if t == 2:
+                for g in range(G):
+                    quant_kn(g, 0, planes=2)
             turn_k(3 + t, t)
+            for g in range(G):
+                if t == 1:
+                    place_pair(g, on_v)
+                if t == 2:
+                    if g == 0:
+                        place_one(t, g, on_s, slice(0, 2))
+                        place_one(t, g, on_v, slice(2, 4))
+                    else:
+                        place_one(t, g, on_v)
             if t == 0:
                 nc.scalar.copy(out=x_bf[:].rearrange("p (c i) t -> p c t i", i=2),
                                in_=x_raw[:].rearrange("p t (c i) -> p c t i", i=2))
                 nc.vector.quantize_mx(out=x_codes[:].bitcast(E4), scales=x_scales[:],
                                       in_=x_bf[:].rearrange("p r t -> p (r t)"))
-        for g in range(G):
-            quant_kn(g, 0, planes=2)
-        for pair in range(2):
-            turn_y(pair, 0, 0, pair)
 
         kd_codes = {0: keep.tile([P, KP], U32, name="kd_codes0", align_bytes=64)}
         kd_scales = [keep.tile([P, KP], U8, name="kd_scales%d" % g, align_bytes=64) for g in range(G)]
-        z = [shared.tile([P, PACK, R], F32, name="z0", offset=0, align_bytes=64), keep.tile([P, PACK, R], F32, name="z1")]
+        z = [keep.tile([P, PACK, R], F32, name="z%d" % g, tag="z%d" % g) for g in range(G)]
         th = [keep.tile([P, PACK, R], F32, name="th%d" % g) for g in range(G)]
         h_bf = [keep.tile([P, R, PACK], BF16, name="h_bf%d" % g, align_bytes=64) for g in range(G)]
         h_codes = [keep.tile([P, R], U32, name="h_codes%d" % g, align_bytes=64) for g in range(G)]
@@ -184,17 +182,25 @@ def tile_attend_gpq_lch_x_kernel(tc, xT, cb, norm, ts, y, wt, offs, out):
             nc.vector.quantize_mx(out=kd_codes[g][:, cols].bitcast(E4), scales=kd_scales[g][:, cols],
                                   in_=k_d[g][:, tiles, :, :].rearrange("p a m t -> p (a m t)"))
 
-        def scores(b, g, a):
-            acc[g, a] = bank(b, [P, R])
-            cols = slice(a * P, (a + 1) * P)
-            nc.tensor.matmul_mx(out=acc[g, a][:], lhsT=kd_codes[g][:, cols].bitcast(E4),
-                                lhsT_scale=kd_scales[g][:, cols],
-                                rhs=x_codes[:].bitcast(E4), rhs_scale=x_scales[:], start=True, stop=True)
+        def scores(b, g, half, pair):
+            acc[g, half, pair] = bank(b, [P, 2, HALF])
+            rows = slice(half * HALF, (half + 1) * HALF)
+            for e in range(2):
+                cols = slice((2 * pair + e) * P, (2 * pair + e + 1) * P)
+                nc.tensor.matmul_mx(out=acc[g, half, pair][:, e, :], lhsT=kd_codes[g][:, cols].bitcast(E4),
+                                    lhsT_scale=kd_scales[g][:, cols], rhs=x_codes[:, rows].bitcast(E4),
+                                    rhs_scale=x_scales[:, rows], start=True, stop=True)
 
-        def residual(g, a):
-            nc.vector.scalar_tensor_tensor(out=z[g][:, a, :], in0=acc[g, a][:], scalar=ts_col[:, g, a:a + 1],
-                                           in1=yT[g][:, a, :], op0=MULT, op1=SUB)
-            nc.scalar.activation(out=th[g][:, a, :], in_=z[g][:, a, :], func=TANH)
+        def residual(g, half):
+            rows = slice(half * HALF, (half + 1) * HALF)
+            for a in range(PACK):
+                nc.vector.scalar_tensor_tensor(out=z[g][:, a, rows], in0=acc[g, half, a // 2][:, a % 2, :],
+                                               scalar=ts_col[:, g, a:a + 1], in1=yT[g][:, a, rows],
+                                               op0=MULT, op1=SUB)
+
+        def tanh(g, i):
+            rows = slice(i * P, (i + 1) * P)
+            nc.scalar.activation(out=th[g][:, :, rows], in_=z[g][:, :, rows], func=TANH)
 
         def weigh(g, i, tiles=1):
             rows = slice(i * P, (i + tiles) * P)
@@ -233,42 +239,46 @@ def tile_attend_gpq_lch_x_kernel(tc, xT, cb, norm, ts, y, wt, offs, out):
 
         last = PACK - 1
         gather(last, 0)
-        for u in range(2):
-            place_one(last, 0, on_s, slice(2 * u, 2 * u + 2))
+        place_one(last, 0, on_s, slice(0, 2))
         gather(last, 1)
-        for a in range(PACK):
-            turn_low_y(a)
-        for u in range(2):
-            quant_kd(0, slice(2 * u, 2 * u + 2))
+        for half in range(2):
+            for pair in range(2):
+                turn_y(2 * half + pair, 0, half, pair)
+            round_k(last, half)
+        quant_kd(0, slice(0, 2))
+        place_one(last, 0, on_v, slice(2, 4))
+        quant_kd(0, slice(2, 4))
         for u in range(2):
             place_one(last, 1, on_v, slice(2 * u, 2 * u + 2))
-        for a in range(PACK):
-            scores(a, 0, a)
-        for a in range(PACK):
-            residual(0, a)
+        for half in range(2):
+            for pair in range(2):
+                scores(2 * half + pair, 0, half, pair)
+            residual(0, half)
+            for i in range(2 * half, 2 * half + 2):
+                tanh(0, i)
         kd_codes[1] = keep.tile([P, KP], U32, name="kd_codes1", tag="yT0", align_bytes=64)
         quant_kd(1)
-        yT[1] = shared.tile([P, PACK, R], F32, name="yT1", offset=G * 2 * KP, align_bytes=64)
-        for a in range(PACK):
-            if a == 2:
-                for b in range(PACK):
-                    scores(4 + b, 1, b)
-            turn_late_y(a, a)
-        for g in range(G):
-            late_pairs = shared.tile([P, 2, P, 2], BF16, name="late_pairs%d" % g, offset=g * 2 * KP, align_bytes=64)
-            pairs[last, g] = late_pairs[:]
-            round_k(last, g)
-        turn_k(2, last)
-        for e in range(2):
-            weigh(0, 2 * e, tiles=2)
-        for a in range(PACK):
-            residual(1, a)
-        for e in range(2):
-            quant_h(0, 2 * e, tiles=2)
+        yT[1] = keep.tile([P, PACK, R], F32, name="yT1", tag="z0")
+        for half in range(2):
+            for pair in range(2):
+                turn_y(4 + 2 * half + pair, 1, half, pair)
+            if half == 0:
+                turn_k(last, last)
+            for pair in range(2):
+                scores(4 + 2 * half + pair, 1, half, pair)
+            weigh(0, 2 * half, tiles=2)
+        residual(1, 0)
+        for i in range(2):
+            tanh(1, i)
         for g in range(G):
             quant_kn(g, last - 1, planes=2)
-        for i in range(RT):
-            grad(0, i, (0, 1, 4, 5)[i])
+        for half in range(2):
+            quant_h(0, 2 * half, tiles=2)
+            for i in range(2 * half, 2 * half + 2):
+                grad(0, i, i)
+        residual(1, 1)
+        for i in range(2, RT):
+            tanh(1, i)
         weigh(1, 0)
         for i in range(RT):
             if i + 1 < RT:

@@ -259,13 +259,13 @@ def tile_attend_gpq_lch_x_kernel(tc, xT, cb, norm, ts, y, wt, offs, out):
         kd_codes[1] = keep.tile([P, KP], U32, name="kd_codes1", tag="yT0", align_bytes=64)
         quant_kd(1)
         yT[1] = keep.tile([P, PACK, R], F32, name="yT1", tag="z0")
-        for half in range(2):
+        for half, banks in enumerate(((0, 1), (3, 2))):
             for pair in range(2):
-                turn_y(4 + 2 * half + pair, 1, half, pair)
+                turn_y(banks[pair], 1, half, pair)
             if half == 0:
-                turn_k(last, last)
+                turn_k(2, last)
             for pair in range(2):
-                scores(4 + 2 * half + pair, 1, half, pair)
+                scores(banks[pair], 1, half, pair)
             weigh(0, 2 * half, tiles=2)
         residual(1, 0)
         for i in range(2):
@@ -275,7 +275,7 @@ def tile_attend_gpq_lch_x_kernel(tc, xT, cb, norm, ts, y, wt, offs, out):
         for half in range(2):
             quant_h(0, 2 * half, tiles=2)
             for i in range(2 * half, 2 * half + 2):
-                grad(0, i, i)
+                grad(0, i, 4 + i)
         residual(1, 1)
         for i in range(2, RT):
             tanh(1, i)

@@ -33,36 +33,40 @@ def tile_attend_gpq_lch_x_kernel(tc, xT, cb, norm, ts, y, wt, offs, out):
         ring = ctx.enter_context(tc.tile_pool(name="ring", bufs=4))
         psum = ctx.enter_context(tc.psum_pool(name="psum", bufs=1))
 
-        def bank(b, shape):
-            return psum.tile(shape, F32, name="bank%d" % b, tag="bank%d" % b)
+        def bank(b, shape, dtype=F32):
+            return psum.tile(shape, dtype, name="bank%d" % b, tag="bank%d" % b)
 
         offsets = keep.tile([P, N // 16], U16, name="offsets")
         win = [keep.tile([P, C], F32, name="win%d" % t, tag="win%d" % t, align_bytes=64) for t in range(PACK)]
-        x_raw = keep.tile([P, PACK, R], F32, name="x_raw")
-        y_raw = {}
+        x_raw = [keep.tile([P, PACK, HALF], F32, name="x_raw%d" % hf, tag="x_raw%d" % hf) for hf in range(2)]
+        y_raw = {(g, hf): keep.tile([P, 2, KP], F32, name="y%d_%d" % (g, hf)) for g in range(G) for hf in range(2)}
         norm_col = keep.tile([P, G, PACK], F32, name="norm_col")
         ts_col = keep.tile([P, G, PACK], F32, name="ts_col")
         wt_col = keep.tile([P, PACK], F32, name="wt_col")
         cb_planes = cb.rearrange("(p t) c -> t p c", t=PACK)
+        x_planes = xT.rearrange("(p t) r -> p t r", t=PACK)
 
-        def load_y(g, half):
-            rows = keep.tile([P, 2, KP], F32, name="y%d_%d" % (g, half))
-            nc.sync.dma_start(out=rows[:], in_=y[half * 2 * P:(half + 1) * 2 * P, g * KP:(g + 1) * KP]
+        def load_x(hf):
+            nc.sync.dma_start(out=x_raw[hf][:], in_=x_planes[:, :, hf * HALF:(hf + 1) * HALF])
+
+        def load_y(g, hf):
+            nc.sync.dma_start(out=y_raw[g, hf][:], in_=y[hf * HALF:(hf + 1) * HALF, g * KP:(g + 1) * KP]
                               .rearrange("(i p) c -> p i c", p=P))
-            y_raw[g, half] = rows
 
-        nc.sync.dma_start(out=wt_col[:], in_=wt.rearrange("(p j) o -> p (j o)", j=PACK))
-        nc.sync.dma_start(out=ts_col[:], in_=ts[0:1, :].rearrange("o (g p j) -> p (o g) j", g=G, j=PACK))
         nc.sync.dma_start(out=norm_col[:], in_=norm[0:1, :].rearrange("o (g p j) -> p (o g) j", g=G, j=PACK))
         nc.sync.dma_start(out=win[0][:], in_=cb_planes[0])
         nc.sync.dma_start(offsets[:], offs)
-        nc.sync.dma_start(out=x_raw[:], in_=xT.rearrange("(p t) r -> p t r", t=PACK))
+        nc.sync.dma_start(out=wt_col[:], in_=wt.rearrange("(p j) o -> p (j o)", j=PACK))
+        nc.sync.dma_start(out=ts_col[:], in_=ts[0:1, :].rearrange("o (g p j) -> p (o g) j", g=G, j=PACK))
         nc.sync.dma_start(out=win[1][:], in_=cb_planes[1])
         nc.sync.dma_start(out=win[2][:], in_=cb_planes[2])
+        load_y(0, 0)
         nc.sync.dma_start(out=win[3][:], in_=cb_planes[3])
-        for g in range(G):
-            for half in range(2):
-                load_y(g, half)
+        load_y(1, 0)
+        load_x(0)
+        load_y(0, 1)
+        load_x(1)
+        load_y(1, 1)
 
         ident = keep.tile([P, P], F32, name="ident")
         make_identity(nc, ident[:])
@@ -73,161 +77,124 @@ def tile_attend_gpq_lch_x_kernel(tc, xT, cb, norm, ts, y, wt, offs, out):
                 nc.tensor.transpose(turned[:, j, :], col[:, j:j + 1].to_broadcast([P, P]), ident[:])
             return turned
 
-        wt_row = keep.tile([P, R], F32, name="wt_row", tag="wt_row")
-        nc.scalar.copy(out=wt_row[:].rearrange("q (p j) -> q p j", j=PACK),
-                       in_=spread(0, wt_col[:])[:].rearrange("q j p -> q p j"))
         norm_row = keep.tile([P, G, KP], F32, name="norm_row")
         for g in range(G):
             nc.scalar.copy(out=norm_row[:, g, :].rearrange("q (p j) -> q p j", j=PACK),
                            in_=spread(1 + g, norm_col[:, g, :])[:].rearrange("q j p -> q p j"))
-        weight = [keep.tile([P, PACK, R], F32, name="weight%d" % g) for g in range(G)]
-        for g in range(G):
+        wt_row = keep.tile([P, R], F32, name="wt_row", tag="wt_row")
+        nc.scalar.copy(out=wt_row[:].rearrange("q (p j) -> q p j", j=PACK),
+                       in_=spread(2, wt_col[:])[:].rearrange("q j p -> q p j"))
+
+        last = PACK - 1
+        k_d = [keep.tile([P, PACK, P, PACK], BF16, name="k_d%d" % g, tag="k_d%d" % g, align_bytes=64) for g in range(G)]
+        k_n = [keep.tile([P, last, P, PACK], BF16, name="k_n%d" % g, align_bytes=64) for g in range(G)]
+        kn_codes = keep.tile([P, G, D], U32, name="kn_codes", tag="win2", align_bytes=64)
+        kn_scales = keep.tile([P, G, D], U8, name="kn_scales", align_bytes=64)
+        kd_codes = {}
+        kd_scales = [keep.tile([P, KP], U8, name="kd_scales%d" % g, align_bytes=64) for g in range(G)]
+        picked_planes = [keep.tile([P, PACK, KP], F32, name="picked%d" % g) for g in range(G)]
+        picked = {(t, g): picked_planes[g][:, t, :] for t in range(PACK) for g in range(G)}
+
+        def gather(t, g):
+            first = g * KP // 16
+            nc.vector.tensor_tensor(picked[t, g], win[t][:].indirect(offsets[:, first:first + KP // 16]),
+                                    norm_row[:, g, :], MULT)
+
+        def place(g, planes, copy, slots=slice(0, PACK)):
+            copy(out=k_d[g][:, slots, :, planes],
+                 in_=picked_planes[g][:, planes, :].rearrange("p t (m a) -> p a m t", a=PACK)[:, slots])
+
+        def turn_k(t, g):
+            turned = bank(6 + g, [P, PACK, P])
             for a in range(PACK):
-                nc.vector.tensor_scalar(weight[g][:, a, :], wt_row[:], ts_col[:, g, a:a + 1], None, MULT)
+                nc.tensor.transpose(turned[:, a, :], picked[t, g][:, a:KP:PACK], ident[:])
+            nc.scalar.copy(out=k_n[g][:, t], in_=turned[:].rearrange("m a p -> m p a"))
 
-        yT = {0: keep.tile([P, PACK, R], F32, name="yT0", tag="yT0", align_bytes=64)}
+        def quant_kn(g, planes, src):
+            cols = slice(planes.start * P, planes.stop * P)
+            nc.vector.quantize_mx(out=kn_codes[:, g, cols].bitcast(E4), scales=kn_scales[:, g, cols], in_=src)
 
-        def turn_y(b, g, half, pair):
+        def quant_kd(g, tag):
+            kd_codes[g] = keep.tile([P, KP], U32, name="kd_codes%d" % g, tag=tag, align_bytes=64)
+            nc.vector.quantize_mx(out=kd_codes[g][:].bitcast(E4), scales=kd_scales[g][:],
+                                  in_=k_d[g][:].rearrange("p a m t -> p (a m t)"))
+
+        x_bf, x_codes, x_scales, yT, acc, z, th, h_bf, h_codes, h_scales, sums = ({} for e in range(11))
+
+        def round_x(hf, tag):
+            x_bf[hf] = keep.tile([P, HALF, PACK], BF16, name="x_bf%d" % hf, tag=tag, align_bytes=64)
+            nc.scalar.copy(out=x_bf[hf][:].rearrange("p (c i) t -> p c t i", i=2),
+                           in_=x_raw[hf][:].rearrange("p t (c i) -> p c t i", i=2))
+
+        def quant_x(hf):
+            x_codes[hf] = keep.tile([P, HALF], U32, name="x_codes%d" % hf, align_bytes=64)
+            x_scales[hf] = keep.tile([P, HALF], U8, name="x_scales%d" % hf, align_bytes=64)
+            nc.vector.quantize_mx(out=x_codes[hf][:].bitcast(E4), scales=x_scales[hf][:],
+                                  in_=x_bf[hf][:].rearrange("p r t -> p (r t)"))
+
+        def turn_y(b, g, hf, pair):
+            if pair == 0:
+                tag = "x_raw0" if (g, hf) == (1, 0) else "yT%d_%d" % (g, hf)
+                yT[g, hf] = keep.tile([P, PACK, HALF], F32, name="yT%d_%d" % (g, hf), tag=tag)
             turned = bank(b, [P, 2, 2, P])
             for e in range(2):
                 for i in range(2):
-                    nc.tensor.transpose(turned[:, e, i, :], y_raw[g, half][:, i, 2 * pair + e:KP:PACK], ident[:])
-            nc.scalar.copy(out=yT[g][:, 2 * pair:2 * pair + 2, half * HALF:(half + 1) * HALF],
-                           in_=turned[:].rearrange("m e i p -> m e (i p)"))
+                    nc.tensor.transpose(turned[:, e, i, :], y_raw[g, hf][:, i, 2 * pair + e:KP:PACK], ident[:])
+            nc.scalar.copy(out=yT[g, hf][:, 2 * pair:2 * pair + 2, :], in_=turned[:].rearrange("m e i p -> m e (i p)"))
 
-        pair_planes = [keep.tile([P, PACK, 2, P, 2], BF16, name="pairs%d" % g, align_bytes=64) for g in range(G)]
-        pairs = {(t, g): pair_planes[g][:, t] for t in range(PACK) for g in range(G)}
-        k_d = [keep.tile([P, PACK, P, PACK], BF16, name="k_d%d" % g, align_bytes=64) for g in range(G)]
-        k_n = keep.tile([P, G, PACK, KP], BF16, name="k_n", align_bytes=64)
-        k_n_words = k_n[:].rearrange("m g t c -> m (g t c)").bitcast(F32).rearrange(
-            "m (g t p u) -> m g t p u", g=G, t=PACK, u=2)
-        kn_codes = keep.tile([P, G, D], U32, name="kn_codes", tag="win2", align_bytes=64)
-        kn_scales = keep.tile([P, G, D], U8, name="kn_scales", align_bytes=64)
-        picked = {}
-
-        def gather(t, g):
-            if (t, g) == (0, 0):
-                picked[t, g] = keep.tile([P, KP], F32, name="picked_first", tag="wt_row")
-            else:
-                picked[t, g] = ring.tile([P, KP], F32, name="picked", tag="picked")
-            first = g * KP // 16
-            nc.vector.tensor_tensor(picked[t, g][:], win[t][:].indirect(offsets[:, first:first + KP // 16]),
-                                    norm_row[:, g, :], MULT)
-
-        def round_k(t, g):
-            nc.scalar.copy(out=pairs[t, g],
-                           in_=picked[t, g][:].rearrange("p (m u e) -> p u m e", u=2, e=2))
-
-        def place_pair(g, copy):
-            copy(out=k_d[g][:, :, :, 0:2].rearrange("p (u e) m t -> p u e m t", e=2),
-                 in_=pair_planes[g][:, 0:2].rearrange("p t u m e -> p u e m t"))
-
-        def place_one(t, g, copy, tiles=slice(0, PACK)):
-            copy(out=k_d[g][:, tiles, :, t], in_=picked[t, g][:].rearrange("p (m a) -> p a m", a=PACK)[:, tiles, :])
-
-        def turn_k(b, t):
-            turned = bank(b, [P, G, 2, P])
-            for g in range(G):
-                words = pairs[t, g].rearrange("p u m e -> p (u m e)").bitcast(F32)
-                for u in range(2):
-                    nc.tensor.transpose(turned[:, g, u, :], words[:, u * P:(u + 1) * P], ident[:])
-            nc.scalar.copy(out=k_n_words[:, :, t, :, :], in_=turned[:].rearrange("m g u p -> m g p u"))
-
-        def quant_kn(g, t, planes=1):
-            cols = slice(t * P, (t + planes) * P)
-            nc.vector.quantize_mx(out=kn_codes[:, g, cols].bitcast(E4), scales=kn_scales[:, g, cols],
-                                  in_=k_n[:, g, t:t + planes, :].rearrange("m t c -> m (t c)"))
-
-        x_bf = keep.tile([P, R, PACK], BF16, name="x_bf", align_bytes=64)
-        x_codes = keep.tile([P, R], U32, name="x_codes", align_bytes=64)
-        x_scales = keep.tile([P, R], U8, name="x_scales", align_bytes=64)
-
-        on_v, on_s = nc.vector.tensor_copy, nc.scalar.copy
-        for t in range(PACK - 1):
-            for g in range(G):
-                gather(t, g)
-            for g in range(G):
-                round_k(t, g)
-            if t == 2:
-                for g in range(G):
-                    quant_kn(g, 0, planes=2)
-            turn_k(3 + t, t)
-            for g in range(G):
-                if t == 1:
-                    place_pair(g, on_v)
-                if t == 2:
-                    if g == 0:
-                        place_one(t, g, on_s, slice(0, 2))
-                        place_one(t, g, on_v, slice(2, 4))
-                    else:
-                        place_one(t, g, on_v)
-            if t == 0:
-                nc.scalar.copy(out=x_bf[:].rearrange("p (c i) t -> p c t i", i=2),
-                               in_=x_raw[:].rearrange("p t (c i) -> p c t i", i=2))
-                nc.vector.quantize_mx(out=x_codes[:].bitcast(E4), scales=x_scales[:],
-                                      in_=x_bf[:].rearrange("p r t -> p (r t)"))
-
-        kd_codes = {0: keep.tile([P, KP], U32, name="kd_codes0", align_bytes=64)}
-        kd_scales = [keep.tile([P, KP], U8, name="kd_scales%d" % g, align_bytes=64) for g in range(G)]
-        z = [keep.tile([P, PACK, R], F32, name="z%d" % g, tag="z%d" % g) for g in range(G)]
-        th = [keep.tile([P, PACK, R], F32, name="th%d" % g) for g in range(G)]
-        h_bf = [keep.tile([P, R, PACK], BF16, name="h_bf%d" % g, align_bytes=64) for g in range(G)]
-        h_codes = [keep.tile([P, R], U32, name="h_codes%d" % g, align_bytes=64) for g in range(G)]
-        h_scales = [keep.tile([P, R], U8, name="h_scales%d" % g, align_bytes=64) for g in range(G)]
-        acc = {}
-        sums = {}
-
-        def quant_kd(g, tiles=slice(0, PACK)):
-            cols = slice(tiles.start * P, tiles.stop * P)
-            nc.vector.quantize_mx(out=kd_codes[g][:, cols].bitcast(E4), scales=kd_scales[g][:, cols],
-                                  in_=k_d[g][:, tiles, :, :].rearrange("p a m t -> p (a m t)"))
-
-        def scores(b, g, half, pair):
-            acc[g, half, pair] = bank(b, [P, 2, HALF])
-            rows = slice(half * HALF, (half + 1) * HALF)
+        def scores(b, g, hf, pair):
+            acc[g, hf, pair] = bank(b, [P, 2, HALF])
             for e in range(2):
                 cols = slice((2 * pair + e) * P, (2 * pair + e + 1) * P)
-                nc.tensor.matmul_mx(out=acc[g, half, pair][:, e, :], lhsT=kd_codes[g][:, cols].bitcast(E4),
-                                    lhsT_scale=kd_scales[g][:, cols], rhs=x_codes[:, rows].bitcast(E4),
-                                    rhs_scale=x_scales[:, rows], start=True, stop=True)
+                nc.tensor.matmul_mx(out=acc[g, hf, pair][:, e, :], lhsT=kd_codes[g][:, cols].bitcast(E4),
+                                    lhsT_scale=kd_scales[g][:, cols], rhs=x_codes[hf][:].bitcast(E4),
+                                    rhs_scale=x_scales[hf][:], start=True, stop=True)
 
-        def residual(g, half):
-            rows = slice(half * HALF, (half + 1) * HALF)
+        def residual(g, hf):
+            z[g, hf] = keep.tile([P, PACK, HALF], F32, name="z%d_%d" % (g, hf), tag="z%d_%d" % (g, hf), align_bytes=64)
             for a in range(PACK):
-                nc.vector.scalar_tensor_tensor(out=z[g][:, a, rows], in0=acc[g, half, a // 2][:, a % 2, :],
-                                               scalar=ts_col[:, g, a:a + 1], in1=yT[g][:, a, rows],
+                nc.vector.scalar_tensor_tensor(out=z[g, hf][:, a, :], in0=acc[g, hf, a // 2][:, a % 2, :],
+                                               scalar=ts_col[:, g, a:a + 1], in1=yT[g, hf][:, a, :],
                                                op0=MULT, op1=SUB)
 
-        def tanh(g, i):
-            rows = slice(i * P, (i + 1) * P)
-            nc.scalar.activation(out=th[g][:, :, rows], in_=z[g][:, :, rows], func=TANH)
+        def tanh(g, hf):
+            th[g, hf] = keep.tile([P, PACK, HALF], F32, name="th%d_%d" % (g, hf))
+            for i in range(2):
+                rows = slice(i * P, (i + 1) * P)
+                nc.scalar.activation(out=th[g, hf][:, :, rows], in_=z[g, hf][:, :, rows], func=TANH)
 
-        def weigh(g, i, tiles=1):
-            rows = slice(i * P, (i + tiles) * P)
+        def weigh(g, hf, first, tiles):
+            if first == 0:
+                h_bf[g, hf] = keep.tile([P, HALF, PACK], BF16, name="h_bf%d_%d" % (g, hf), align_bytes=64)
+                h_codes[g, hf] = keep.tile([P, HALF], U32, name="h_codes%d_%d" % (g, hf), align_bytes=64)
+                h_scales[g, hf] = keep.tile([P, HALF], U8, name="h_scales%d_%d" % (g, hf), align_bytes=64)
+            rows = slice(first * P, (first + tiles) * P)
+            whole = slice(hf * HALF + rows.start, hf * HALF + rows.stop)
             walk = "m a (c i) -> m c a i"
-            nc.vector.tensor_tensor(h_bf[g][:, rows, :].rearrange("m (c i) a -> m c a i", i=2),
-                                    th[g][:, :, rows].rearrange(walk, i=2),
-                                    weight[g][:, :, rows].rearrange(walk, i=2), MULT)
+            nc.vector.tensor_tensor(h_bf[g, hf][:, rows, :].rearrange("m (c i) a -> m c a i", i=2),
+                                    th[g, hf][:, :, rows].rearrange(walk, i=2),
+                                    weight[g][:, :, whole].rearrange(walk, i=2), MULT)
 
-        def quant_h(g, i, tiles=1):
-            rows = slice(i * P, (i + tiles) * P)
-            nc.vector.quantize_mx(out=h_codes[g][:, rows].bitcast(E5), scales=h_scales[g][:, rows],
-                                  in_=h_bf[g][:, rows, :].rearrange("m r a -> m (r a)"))
+        def quant_h(g, hf, first, tiles):
+            rows = slice(first * P, (first + tiles) * P)
+            nc.vector.quantize_mx(out=h_codes[g, hf][:, rows].bitcast(E5), scales=h_scales[g, hf][:, rows],
+                                  in_=h_bf[g, hf][:, rows, :].rearrange("m r a -> m (r a)"))
 
-        def grad(g, i, b=None):
+        def grad(g, hf, i, b=None):
             rows = slice(i * P, (i + 1) * P)
             if g == 0:
-                sums[i] = bank(b, [P, D])
-            nc.tensor.matmul_mx(out=sums[i][:], lhsT=h_codes[g][:, rows].bitcast(E5), lhsT_scale=h_scales[g][:, rows],
+                sums[hf, i] = bank(b, [P, D])
+            nc.tensor.matmul_mx(out=sums[hf, i][:], lhsT=h_codes[g, hf][:, rows].bitcast(E5),
+                                lhsT_scale=h_scales[g, hf][:, rows],
                                 rhs=kn_codes[:, g, :].bitcast(E4), rhs_scale=kn_scales[:, g, :],
                                 start=(g == 0), stop=(g == G - 1))
 
-        def finish(i):
+        def finish(hf, i):
             res = ring.tile([P, D], F32, name="res", tag="res")
             dst = res[:].rearrange("r (p t) -> r p t", t=PACK)
-            src = sums[i][:].rearrange("r (t p) -> r p t", t=PACK)
-            rows = slice(i * P, (i + 1) * P)
-            if i < RT - 1:
+            src = sums[hf, i][:].rearrange("r (t p) -> r p t", t=PACK)
+            rows = slice(hf * HALF + i * P, hf * HALF + (i + 1) * P)
+            if (hf, i) != (1, 1):
                 nc.scalar.copy(out=dst, in_=src)
                 nc.sync.dma_start(out=out[rows, :], in_=res[:])
             else:
@@ -237,52 +204,92 @@ def tile_attend_gpq_lch_x_kernel(tc, xT, cb, norm, ts, y, wt, offs, out):
                     nc.vector.tensor_copy(out=dst[:, ps, :], in_=src[:, ps, :])
                     nc.sync.dma_start(out=out[rows, cols], in_=res[:, cols])
 
-        last = PACK - 1
-        gather(last, 0)
-        place_one(last, 0, on_s, slice(0, 2))
-        gather(last, 1)
-        for half in range(2):
-            for pair in range(2):
-                turn_y(2 * half + pair, 0, half, pair)
-            round_k(last, half)
-        quant_kd(0, slice(0, 2))
-        place_one(last, 0, on_v, slice(2, 4))
-        quant_kd(0, slice(2, 4))
-        for u in range(2):
-            place_one(last, 1, on_v, slice(2 * u, 2 * u + 2))
-        for half in range(2):
-            for pair in range(2):
-                scores(2 * half + pair, 0, half, pair)
-            residual(0, half)
-            for i in range(2 * half, 2 * half + 2):
-                tanh(0, i)
-        kd_codes[1] = keep.tile([P, KP], U32, name="kd_codes1", tag="yT0", align_bytes=64)
-        quant_kd(1)
-        yT[1] = keep.tile([P, PACK, R], F32, name="yT1", tag="z0")
-        for half, banks in enumerate(((0, 1), (3, 2))):
-            for pair in range(2):
-                turn_y(banks[pair], 1, half, pair)
-            if half == 0:
-                turn_k(2, last)
-            for pair in range(2):
-                scores(banks[pair], 1, half, pair)
-            weigh(0, 2 * half, tiles=2)
-        residual(1, 0)
-        for i in range(2):
-            tanh(1, i)
+        def turn_last_plane(b, tag):
+            pairs = keep.tile([P, G, 2, P, 2], BF16, name="pairs", tag=tag, align_bytes=64)
+            for g in range(G):
+                nc.scalar.copy(out=pairs[:, g], in_=picked[last, g].rearrange("p (m u e) -> p u m e", u=2, e=2))
+            words = pairs[:].rearrange("p g u m e -> p (g u m e)").bitcast(F32)
+            turned = bank(b, [P, G, 2, P])
+            for g in range(G):
+                for u in range(2):
+                    nc.tensor.transpose(turned[:, g, u, :], words[:, (2 * g + u) * P:(2 * g + u + 1) * P], ident[:])
+            k_n_last = keep.tile([P, G, KP], BF16, name="k_n_last", align_bytes=64)
+            nc.scalar.copy(out=k_n_last[:].rearrange("m g c -> m (g c)").bitcast(F32)
+                           .rearrange("m (g p u) -> m g p u", g=G, u=2), in_=turned[:].rearrange("m g u p -> m g p u"))
+            return k_n_last
+
+        on_v, on_s = nc.vector.tensor_copy, nc.scalar.copy
+        for t in range(2):
+            for g in range(G):
+                gather(t, g)
+                turn_k(t, g)
+        weight = [keep.tile([P, PACK, R], F32, name="weight%d" % g, tag="win%d" % g, align_bytes=64) for g in range(G)]
         for g in range(G):
-            quant_kn(g, last - 1, planes=2)
-        for half in range(2):
-            quant_h(0, 2 * half, tiles=2)
-            for i in range(2 * half, 2 * half + 2):
-                grad(0, i, 4 + i)
-        residual(1, 1)
-        for i in range(2, RT):
-            tanh(1, i)
-        weigh(1, 0)
-        for i in range(RT):
-            if i + 1 < RT:
-                weigh(1, i + 1)
-            quant_h(1, i)
-            grad(1, i)
-            finish(i)
+            for a in range(PACK):
+                nc.vector.tensor_scalar(weight[g][:, a, :], wt_row[:], ts_col[:, g, a:a + 1], None, MULT)
+        place(0, slice(0, 2), on_s)
+        place(1, slice(0, 2), on_v)
+        gather(2, 0)
+        place(0, slice(2, 3), on_s)
+        gather(2, 1)
+        place(1, slice(2, 3), on_v)
+        for g in range(G):
+            quant_kn(g, slice(0, 2), k_n[g][:, 0:2].rearrange("m t p a -> m (t p a)"))
+        for g in range(G):
+            turn_k(2, g)
+            quant_kn(g, slice(2, 3), k_n[g][:, 2].rearrange("m p a -> m (p a)"))
+        for pair in range(2):
+            turn_y(pair, 0, 0, pair)
+
+        gather(last, 0)
+        place(0, slice(last, PACK), on_s, slice(0, 2))
+        place(0, slice(last, PACK), on_v, slice(2, 4))
+        quant_kd(0, "kd_codes0")
+        round_x(0, "x_bf0")
+        gather(last, 1)
+        quant_x(0)
+        place(1, slice(last, PACK), on_v)
+        quant_kd(1, "x_bf0")
+        for g in range(G):
+            for pair in range(2):
+                scores(2 + 2 * g + pair, g, 0, pair)
+        for pair in range(2):
+            turn_y(pair, 1, 0, pair)
+        round_x(1, "x_bf1")
+        turn_y(6, 0, 1, 0)
+        for g in range(G):
+            residual(g, 0)
+            tanh(g, 0)
+        k_n_last = turn_last_plane(7, "k_d1")
+        turn_y(2, 0, 1, 1)
+        turn_y(3, 1, 1, 0)
+        turn_y(4, 1, 1, 1)
+        weigh(0, 0, 0, 2)
+        quant_x(1)
+        quant_h(0, 0, 0, 2)
+        weigh(1, 0, 0, 2)
+        for g in range(G):
+            quant_kn(g, slice(last, PACK), k_n_last[:, g, :])
+        quant_h(1, 0, 0, 2)
+        for g, banks in enumerate(((0, 1), (5, 2))):
+            for pair in range(2):
+                scores(banks[pair], g, 1, pair)
+        for g in range(G):
+            for i in range(2):
+                grad(g, 0, i, 6 + i)
+        for g in range(G):
+            residual(g, 1)
+            tanh(g, 1)
+        for i in range(2):
+            finish(0, i)
+        weigh(0, 1, 0, 2)
+        weigh(1, 1, 0, 1)
+        quant_h(0, 1, 0, 2)
+        for i in range(2):
+            grad(0, 1, i, 3 + i)
+        for i in range(2):
+            if i == 0:
+                weigh(1, 1, 1, 1)
+            quant_h(1, 1, i, 1)
+            grad(1, 1, i)
+            finish(1, i)

@@ -30,26 +30,32 @@ def tile_attend_gpq_lch_x_kernel(tc, xT, cb, norm, ts, y, wt, offs, out):
     nc = tc.nc
     with ExitStack() as ctx:
         keep = ctx.enter_context(tc.tile_pool(name="keep", bufs=1))
-        ring = ctx.enter_context(tc.tile_pool(name="ring", bufs=4))
+        wide = ctx.enter_context(tc.tile_pool(name="wide", bufs=1))
         psum = ctx.enter_context(tc.psum_pool(name="psum", bufs=1))
 
         def bank(b, shape, dtype=F32):
             return psum.tile(shape, dtype, name="bank%d" % b, tag="bank%d" % b)
 
         offsets = keep.tile([P, N // 16], U16, name="offsets")
-        win = [keep.tile([P, C], F32, name="win%d" % t, tag="win%d" % t, align_bytes=64) for t in range(PACK)]
-        x_raw = [keep.tile([P, PACK, HALF], F32, name="x_raw%d" % hf, tag="x_raw%d" % hf) for hf in range(2)]
-        y_raw = {(g, hf): keep.tile([P, 2, KP], F32, name="y%d_%d" % (g, hf)) for g in range(G) for hf in range(2)}
+        window_bytes, piece_bytes = 4 * C, 4 * PACK * HALF
+
+        def on_window(t, piece, shape, dtype, name):
+            return wide.tile(shape, dtype, name=name, offset=t * window_bytes + piece * piece_bytes, align_bytes=64)
+
+        win = [on_window(t, 0, [P, C], F32, "win%d" % t) for t in range(PACK)]
+        x_raw, y_raw = {}, {}
         norm_col = keep.tile([P, G, PACK], F32, name="norm_col")
         ts_col = keep.tile([P, G, PACK], F32, name="ts_col")
         wt_col = keep.tile([P, PACK], F32, name="wt_col")
         cb_planes = cb.rearrange("(p t) c -> t p c", t=PACK)
         x_planes = xT.rearrange("(p t) r -> p t r", t=PACK)
 
-        def load_x(hf):
+        def load_x(hf, tile):
+            x_raw[hf] = tile
             nc.sync.dma_start(out=x_raw[hf][:], in_=x_planes[:, :, hf * HALF:(hf + 1) * HALF])
 
-        def load_y(g, hf):
+        def load_y(g, hf, tile):
+            y_raw[g, hf] = tile
             nc.sync.dma_start(out=y_raw[g, hf][:], in_=y[hf * HALF:(hf + 1) * HALF, g * KP:(g + 1) * KP]
                               .rearrange("(i p) c -> p i c", p=P))
 
@@ -58,15 +64,11 @@ def tile_attend_gpq_lch_x_kernel(tc, xT, cb, norm, ts, y, wt, offs, out):
         nc.sync.dma_start(offsets[:], offs)
         nc.sync.dma_start(out=wt_col[:], in_=wt.rearrange("(p j) o -> p (j o)", j=PACK))
         nc.sync.dma_start(out=ts_col[:], in_=ts[0:1, :].rearrange("o (g p j) -> p (o g) j", g=G, j=PACK))
+        load_y(0, 0, keep.tile([P, 2, KP], F32, name="y_first"))
         nc.sync.dma_start(out=win[1][:], in_=cb_planes[1])
+        load_y(1, 0, keep.tile([P, 2, KP], F32, name="y_second"))
         nc.sync.dma_start(out=win[2][:], in_=cb_planes[2])
-        load_y(0, 0)
         nc.sync.dma_start(out=win[3][:], in_=cb_planes[3])
-        load_y(1, 0)
-        load_x(0)
-        load_y(0, 1)
-        load_x(1)
-        load_y(1, 1)
 
         ident = keep.tile([P, P], F32, name="ident")
         make_identity(nc, ident[:])
@@ -83,12 +85,15 @@ def tile_attend_gpq_lch_x_kernel(tc, xT, cb, norm, ts, y, wt, offs, out):
                            in_=spread(1 + g, norm_col[:, g, :])[:].rearrange("q j p -> q p j"))
         wt_row = keep.tile([P, R], F32, name="wt_row", tag="wt_row")
         nc.scalar.copy(out=wt_row[:].rearrange("q (p j) -> q p j", j=PACK),
-                       in_=spread(2, wt_col[:])[:].rearrange("q j p -> q p j"))
+                       in_=spread(6, wt_col[:])[:].rearrange("q j p -> q p j"))
 
         last = PACK - 1
         k_d = [keep.tile([P, PACK, P, PACK], BF16, name="k_d%d" % g, tag="k_d%d" % g, align_bytes=64) for g in range(G)]
-        k_n = [keep.tile([P, last, P, PACK], BF16, name="k_n%d" % g, align_bytes=64) for g in range(G)]
-        kn_codes = keep.tile([P, G, D], U32, name="kn_codes", tag="win2", align_bytes=64)
+        k_n_early = [keep.tile([P, last - g, P, PACK], BF16, name="k_n%d" % g, align_bytes=64) for g in range(G)]
+        k_n_late = keep.tile([P, 3, P, PACK], BF16, name="k_n_late", align_bytes=64)
+        k_n = {(t, g): k_n_early[g][:, t] for g in range(G) for t in range(last - g)}
+        k_n[2, 1] = k_n_late[:, 1]
+        kn_codes = on_window(2, 0, [P, G, D], U32, "kn_codes")
         kn_scales = keep.tile([P, G, D], U8, name="kn_scales", align_bytes=64)
         kd_codes = {}
         kd_scales = [keep.tile([P, KP], U8, name="kd_scales%d" % g, align_bytes=64) for g in range(G)]
@@ -108,7 +113,7 @@ def tile_attend_gpq_lch_x_kernel(tc, xT, cb, norm, ts, y, wt, offs, out):
             turned = bank(6 + g, [P, PACK, P])
             for a in range(PACK):
                 nc.tensor.transpose(turned[:, a, :], picked[t, g][:, a:KP:PACK], ident[:])
-            nc.scalar.copy(out=k_n[g][:, t], in_=turned[:].rearrange("m a p -> m p a"))
+            nc.scalar.copy(out=k_n[t, g], in_=turned[:].rearrange("m a p -> m p a"))
 
         def quant_kn(g, planes, src):
             cols = slice(planes.start * P, planes.stop * P)
@@ -126,16 +131,16 @@ def tile_attend_gpq_lch_x_kernel(tc, xT, cb, norm, ts, y, wt, offs, out):
             nc.scalar.copy(out=x_bf[hf][:].rearrange("p (c i) t -> p c t i", i=2),
                            in_=x_raw[hf][:].rearrange("p t (c i) -> p c t i", i=2))
 
-        def quant_x(hf):
-            x_codes[hf] = keep.tile([P, HALF], U32, name="x_codes%d" % hf, align_bytes=64)
+        def quant_x(hf, tag):
+            x_codes[hf] = keep.tile([P, HALF], U32, name="x_codes%d" % hf, tag=tag, align_bytes=64)
             x_scales[hf] = keep.tile([P, HALF], U8, name="x_scales%d" % hf, align_bytes=64)
             nc.vector.quantize_mx(out=x_codes[hf][:].bitcast(E4), scales=x_scales[hf][:],
                                   in_=x_bf[hf][:].rearrange("p r t -> p (r t)"))
 
         def turn_y(b, g, hf, pair):
             if pair == 0:
-                tag = "x_raw0" if (g, hf) == (1, 0) else "yT%d_%d" % (g, hf)
-                yT[g, hf] = keep.tile([P, PACK, HALF], F32, name="yT%d_%d" % (g, hf), tag=tag)
+                tag = ("yT%d", "z%d_0")[hf] % g
+                yT[g, hf] = keep.tile([P, PACK, HALF], F32, name="yT%d_%d" % (g, hf), tag=tag, align_bytes=64)
             turned = bank(b, [P, 2, 2, P])
             for e in range(2):
                 for i in range(2):
@@ -150,15 +155,15 @@ def tile_attend_gpq_lch_x_kernel(tc, xT, cb, norm, ts, y, wt, offs, out):
                                     lhsT_scale=kd_scales[g][:, cols], rhs=x_codes[hf][:].bitcast(E4),
                                     rhs_scale=x_scales[hf][:], start=True, stop=True)
 
-        def residual(g, hf):
-            z[g, hf] = keep.tile([P, PACK, HALF], F32, name="z%d_%d" % (g, hf), tag="z%d_%d" % (g, hf), align_bytes=64)
+        def residual(g, hf, tag):
+            z[g, hf] = keep.tile([P, PACK, HALF], F32, name="z%d_%d" % (g, hf), tag=tag, align_bytes=64)
             for a in range(PACK):
                 nc.vector.scalar_tensor_tensor(out=z[g, hf][:, a, :], in0=acc[g, hf, a // 2][:, a % 2, :],
                                                scalar=ts_col[:, g, a:a + 1], in1=yT[g, hf][:, a, :],
                                                op0=MULT, op1=SUB)
 
         def tanh(g, hf):
-            th[g, hf] = keep.tile([P, PACK, HALF], F32, name="th%d_%d" % (g, hf))
+            th[g, hf] = keep.tile([P, PACK, HALF], F32, name="th%d_%d" % (g, hf), tag="th%d_%d" % (g, hf), align_bytes=64)
             for i in range(2):
                 rows = slice(i * P, (i + 1) * P)
                 nc.scalar.activation(out=th[g, hf][:, :, rows], in_=z[g, hf][:, :, rows], func=TANH)
@@ -173,7 +178,7 @@ def tile_attend_gpq_lch_x_kernel(tc, xT, cb, norm, ts, y, wt, offs, out):
             walk = "m a (c i) -> m c a i"
             nc.vector.tensor_tensor(h_bf[g, hf][:, rows, :].rearrange("m (c i) a -> m c a i", i=2),
                                     th[g, hf][:, :, rows].rearrange(walk, i=2),
-                                    weight[g][:, :, whole].rearrange(walk, i=2), MULT)
+                                    weight[:, g, :, whole].rearrange(walk, i=2), MULT)
 
         def quant_h(g, hf, first, tiles):
             rows = slice(first * P, (first + tiles) * P)
@@ -189,8 +194,8 @@ def tile_attend_gpq_lch_x_kernel(tc, xT, cb, norm, ts, y, wt, offs, out):
                                 rhs=kn_codes[:, g, :].bitcast(E4), rhs_scale=kn_scales[:, g, :],
                                 start=(g == 0), stop=(g == G - 1))
 
-        def finish(hf, i):
-            res = ring.tile([P, D], F32, name="res", tag="res")
+        def finish(hf, i, tag):
+            res = keep.tile([P, D], F32, name="res%d_%d" % (hf, i), tag=tag, align_bytes=64)
             dst = res[:].rearrange("r (p t) -> r p t", t=PACK)
             src = sums[hf, i][:].rearrange("r (t p) -> r p t", t=PACK)
             rows = slice(hf * HALF + i * P, hf * HALF + (i + 1) * P)
@@ -213,20 +218,29 @@ def tile_attend_gpq_lch_x_kernel(tc, xT, cb, norm, ts, y, wt, offs, out):
             for g in range(G):
                 for u in range(2):
                     nc.tensor.transpose(turned[:, g, u, :], words[:, (2 * g + u) * P:(2 * g + u + 1) * P], ident[:])
-            k_n_last = keep.tile([P, G, KP], BF16, name="k_n_last", align_bytes=64)
-            nc.scalar.copy(out=k_n_last[:].rearrange("m g c -> m (g c)").bitcast(F32)
-                           .rearrange("m (g p u) -> m g p u", g=G, u=2), in_=turned[:].rearrange("m g u p -> m g p u"))
-            return k_n_last
+            late_words = k_n_late[:].rearrange("m s p a -> m (s p a)").bitcast(F32).rearrange(
+                "m (s p u) -> m s p u", s=3, u=2)
+            nc.scalar.copy(out=late_words[:, 0:3:2], in_=turned[:].rearrange("m g u p -> m g p u"))
 
         on_v, on_s = nc.vector.tensor_copy, nc.scalar.copy
-        for t in range(2):
-            for g in range(G):
-                gather(t, g)
-                turn_k(t, g)
-        weight = [keep.tile([P, PACK, R], F32, name="weight%d" % g, tag="win%d" % g, align_bytes=64) for g in range(G)]
+        for g in range(G):
+            gather(0, g)
+            turn_k(0, g)
+        weight = on_window(0, 0, [P, G, PACK, R], F32, "weight")
         for g in range(G):
             for a in range(PACK):
-                nc.vector.tensor_scalar(weight[g][:, a, :], wt_row[:], ts_col[:, g, a:a + 1], None, MULT)
+                nc.vector.tensor_scalar(weight[:, g, a, :], wt_row[:], ts_col[:, g, a:a + 1], None, MULT)
+        for pair in range(2):
+            turn_y(pair, 0, 0, pair)
+        for g in range(G):
+            gather(1, g)
+            turn_k(1, g)
+        load_x(0, on_window(1, 0, [P, PACK, HALF], F32, "x0"))
+        load_x(1, on_window(1, 1, [P, PACK, HALF], F32, "x1"))
+        load_y(0, 1, on_window(1, 2, [P, 2, KP], F32, "y01"))
+        load_y(1, 1, on_window(1, 3, [P, 2, KP], F32, "y11"))
+        for pair in range(2):
+            turn_y(pair, 1, 0, pair)
         place(0, slice(0, 2), on_s)
         place(1, slice(0, 2), on_v)
         gather(2, 0)
@@ -234,62 +248,59 @@ def tile_attend_gpq_lch_x_kernel(tc, xT, cb, norm, ts, y, wt, offs, out):
         gather(2, 1)
         place(1, slice(2, 3), on_v)
         for g in range(G):
-            quant_kn(g, slice(0, 2), k_n[g][:, 0:2].rearrange("m t p a -> m (t p a)"))
+            quant_kn(g, slice(0, 2), k_n_early[g][:, 0:2].rearrange("m t p a -> m (t p a)"))
         for g in range(G):
             turn_k(2, g)
-            quant_kn(g, slice(2, 3), k_n[g][:, 2].rearrange("m p a -> m (p a)"))
-        for pair in range(2):
-            turn_y(pair, 0, 0, pair)
+        quant_kn(0, slice(2, 3), k_n[2, 0].rearrange("m p a -> m (p a)"))
 
         gather(last, 0)
         place(0, slice(last, PACK), on_s, slice(0, 2))
-        place(0, slice(last, PACK), on_v, slice(2, 4))
-        quant_kd(0, "kd_codes0")
-        round_x(0, "x_bf0")
         gather(last, 1)
-        quant_x(0)
-        place(1, slice(last, PACK), on_v)
+        place(0, slice(last, PACK), on_v, slice(2, 4))
+        round_x(0, "x_bf0")
+        quant_kd(0, "kd_codes0")
+        place(1, slice(last, PACK), on_s, slice(0, 2))
+        place(1, slice(last, PACK), on_v, slice(2, 4))
+        quant_x(0, "x_codes0")
         quant_kd(1, "x_bf0")
         for g in range(G):
             for pair in range(2):
                 scores(2 + 2 * g + pair, g, 0, pair)
-        for pair in range(2):
-            turn_y(pair, 1, 0, pair)
         round_x(1, "x_bf1")
-        turn_y(6, 0, 1, 0)
         for g in range(G):
-            residual(g, 0)
+            residual(g, 0, "z%d_0" % g)
             tanh(g, 0)
-        k_n_last = turn_last_plane(7, "k_d1")
-        turn_y(2, 0, 1, 1)
-        turn_y(3, 1, 1, 0)
-        turn_y(4, 1, 1, 1)
+        turn_last_plane(4, "k_d1")
+        for g in range(G):
+            for pair in range(2):
+                turn_y(2 * g + pair, g, 1, pair)
         weigh(0, 0, 0, 2)
-        quant_x(1)
+        quant_x(1, "th0_0")
         quant_h(0, 0, 0, 2)
         weigh(1, 0, 0, 2)
-        for g in range(G):
-            quant_kn(g, slice(last, PACK), k_n_last[:, g, :])
+        quant_kn(0, slice(last, PACK), k_n_late[:, 0].rearrange("m p a -> m (p a)"))
+        quant_kn(1, slice(2, PACK), k_n_late[:, 1:3].rearrange("m s p a -> m (s p a)"))
         quant_h(1, 0, 0, 2)
-        for g, banks in enumerate(((0, 1), (5, 2))):
+        for g, banks in enumerate(((5, 4), (0, 1))):
             for pair in range(2):
                 scores(banks[pair], g, 1, pair)
         for g in range(G):
             for i in range(2):
                 grad(g, 0, i, 6 + i)
-        for g in range(G):
-            residual(g, 1)
-            tanh(g, 1)
+        residual(0, 1, "th1_0")
+        tanh(0, 1)
+        residual(1, 1, "z1_1")
+        tanh(1, 1)
         for i in range(2):
-            finish(0, i)
+            finish(0, i, ("th1_0", "z1_1")[i])
         weigh(0, 1, 0, 2)
         weigh(1, 1, 0, 1)
         quant_h(0, 1, 0, 2)
         for i in range(2):
-            grad(0, 1, i, 3 + i)
+            grad(0, 1, i, 2 + i)
         for i in range(2):
             if i == 0:
                 weigh(1, 1, 1, 1)
             quant_h(1, 1, i, 1)
             grad(1, 1, i)
-            finish(1, i)
+            finish(1, i, "res%d" % i)

@@ -15,6 +15,7 @@ U8 = mybir.dt.uint8
 E4 = mybir.dt.float8_e4m3fn_x4
 E5 = mybir.dt.float8_e5m2_x4
 MULT = mybir.AluOpType.mult
+ADD = mybir.AluOpType.add
 SUB = mybir.AluOpType.subtract
 TANH = mybir.ActivationFunctionType.Tanh
 
@@ -40,7 +41,8 @@ def tile_attend_gpq_lch_x_kernel(tc, xT, cb, norm, ts, y, wt, offs, out):
         window_bytes, piece_bytes = 4 * C, 4 * PACK * HALF
 
         def on_window(t, piece, shape, dtype, name):
-            return wide.tile(shape, dtype, name=name, offset=t * window_bytes + piece * piece_bytes, align_bytes=64)
+            offset = t * window_bytes + int(piece * piece_bytes)
+            return wide.tile(shape, dtype, name=name, offset=offset, align_bytes=64)
 
         win = [on_window(t, 0, [P, C], F32, "win%d" % t) for t in range(PACK)]
         x_raw, y_raw = {}, {}
@@ -90,7 +92,7 @@ def tile_attend_gpq_lch_x_kernel(tc, xT, cb, norm, ts, y, wt, offs, out):
         last = PACK - 1
         k_d = [keep.tile([P, PACK, P, PACK], BF16, name="k_d%d" % g, tag="k_d%d" % g, align_bytes=64) for g in range(G)]
         k_n_early = [keep.tile([P, last - g, P, PACK], BF16, name="k_n%d" % g, align_bytes=64) for g in range(G)]
-        k_n_late = keep.tile([P, 3, P, PACK], BF16, name="k_n_late", align_bytes=64)
+        k_n_late = on_window(2, 1, [P, 3, P, PACK], BF16, "k_n_late")
         k_n = {(t, g): k_n_early[g][:, t] for g in range(G) for t in range(last - g)}
         k_n[2, 1] = k_n_late[:, 1]
         kn_codes = on_window(2, 0, [P, G, D], U32, "kn_codes")
@@ -139,8 +141,11 @@ def tile_attend_gpq_lch_x_kernel(tc, xT, cb, norm, ts, y, wt, offs, out):
 
         def turn_y(b, g, hf, pair):
             if pair == 0:
-                tag = ("yT%d", "z%d_0")[hf] % g
-                yT[g, hf] = keep.tile([P, PACK, HALF], F32, name="yT%d_%d" % (g, hf), tag=tag, align_bytes=64)
+                if (g, hf) == (0, 1):
+                    yT[g, hf] = on_window(1, 1, [P, PACK, HALF], F32, "yT0_1")
+                else:
+                    tag = ("yT%d", "z%d_0")[hf] % g
+                    yT[g, hf] = keep.tile([P, PACK, HALF], F32, name="yT%d_%d" % (g, hf), tag=tag, align_bytes=64)
             turned = bank(b, [P, 2, 2, P])
             for e in range(2):
                 for i in range(2):
@@ -155,8 +160,8 @@ def tile_attend_gpq_lch_x_kernel(tc, xT, cb, norm, ts, y, wt, offs, out):
                                     lhsT_scale=kd_scales[g][:, cols], rhs=x_codes[hf][:].bitcast(E4),
                                     rhs_scale=x_scales[hf][:], start=True, stop=True)
 
-        def residual(g, hf, tag):
-            z[g, hf] = keep.tile([P, PACK, HALF], F32, name="z%d_%d" % (g, hf), tag=tag, align_bytes=64)
+        def residual(g, hf, tile):
+            z[g, hf] = tile
             for a in range(PACK):
                 nc.vector.scalar_tensor_tensor(out=z[g, hf][:, a, :], in0=acc[g, hf, a // 2][:, a % 2, :],
                                                scalar=ts_col[:, g, a:a + 1], in1=yT[g, hf][:, a, :],
@@ -171,8 +176,6 @@ def tile_attend_gpq_lch_x_kernel(tc, xT, cb, norm, ts, y, wt, offs, out):
         def weigh(g, hf, first, tiles):
             if first == 0:
                 h_bf[g, hf] = keep.tile([P, HALF, PACK], BF16, name="h_bf%d_%d" % (g, hf), align_bytes=64)
-                h_codes[g, hf] = keep.tile([P, HALF], U32, name="h_codes%d_%d" % (g, hf), align_bytes=64)
-                h_scales[g, hf] = keep.tile([P, HALF], U8, name="h_scales%d_%d" % (g, hf), align_bytes=64)
             rows = slice(first * P, (first + tiles) * P)
             whole = slice(hf * HALF + rows.start, hf * HALF + rows.stop)
             walk = "m a (c i) -> m c a i"
@@ -181,6 +184,9 @@ def tile_attend_gpq_lch_x_kernel(tc, xT, cb, norm, ts, y, wt, offs, out):
                                     weight[:, g, :, whole].rearrange(walk, i=2), MULT)
 
         def quant_h(g, hf, first, tiles):
+            if first == 0:
+                h_codes[g, hf] = keep.tile([P, HALF], U32, name="h_codes%d_%d" % (g, hf), align_bytes=64)
+                h_scales[g, hf] = keep.tile([P, HALF], U8, name="h_scales%d_%d" % (g, hf), align_bytes=64)
             rows = slice(first * P, (first + tiles) * P)
             nc.vector.quantize_mx(out=h_codes[g, hf][:, rows].bitcast(E5), scales=h_scales[g, hf][:, rows],
                                   in_=h_bf[g, hf][:, rows, :].rearrange("m r a -> m (r a)"))
@@ -210,14 +216,14 @@ def tile_attend_gpq_lch_x_kernel(tc, xT, cb, norm, ts, y, wt, offs, out):
                     nc.sync.dma_start(out=out[rows, cols], in_=res[:, cols])
 
         def turn_last_plane(b, tag):
-            pairs = keep.tile([P, G, 2, P, 2], BF16, name="pairs", tag=tag, align_bytes=64)
+            pairs = keep.tile([P, G, KP], BF16, name="pairs", tag=tag, align_bytes=64)
             for g in range(G):
-                nc.scalar.copy(out=pairs[:, g], in_=picked[last, g].rearrange("p (m u e) -> p u m e", u=2, e=2))
-            words = pairs[:].rearrange("p g u m e -> p (g u m e)").bitcast(F32)
+                nc.gpsimd.tensor_scalar(pairs[:, g], picked[last, g], 1.0, 0.0, MULT, ADD)
+            words = pairs[:].rearrange("p g c -> p (g c)").bitcast(F32).rearrange("p (g w) -> p g w", g=G)
             turned = bank(b, [P, G, 2, P])
             for g in range(G):
                 for u in range(2):
-                    nc.tensor.transpose(turned[:, g, u, :], words[:, (2 * g + u) * P:(2 * g + u + 1) * P], ident[:])
+                    nc.tensor.transpose(turned[:, g, u, :], words[:, g, u:2 * P:2], ident[:])
             late_words = k_n_late[:].rearrange("m s p a -> m (s p a)").bitcast(F32).rearrange(
                 "m (s p u) -> m s p u", s=3, u=2)
             nc.scalar.copy(out=late_words[:, 0:3:2], in_=turned[:].rearrange("m g u p -> m g p u"))
@@ -229,16 +235,21 @@ def tile_attend_gpq_lch_x_kernel(tc, xT, cb, norm, ts, y, wt, offs, out):
         weight = on_window(0, 0, [P, G, PACK, R], F32, "weight")
         for g in range(G):
             for a in range(PACK):
-                nc.vector.tensor_scalar(weight[:, g, a, :], wt_row[:], ts_col[:, g, a:a + 1], None, MULT)
+                rows = slice(g * HALF, R)
+                nc.vector.tensor_scalar(weight[:, g, a, rows], wt_row[:, rows], ts_col[:, g, a:a + 1], None, MULT)
+        weight_woven = keep.tile([P, HALF, PACK], F32, name="weight_woven")
+        nc.vector.tensor_tensor(weight_woven[:],
+                                wt_row[:, 0:HALF].rearrange("q (r o) -> q r o", o=1).to_broadcast([P, HALF, PACK]),
+                                ts_col[:, 1:2, :].to_broadcast([P, HALF, PACK]), MULT)
         for pair in range(2):
             turn_y(pair, 0, 0, pair)
         for g in range(G):
             gather(1, g)
             turn_k(1, g)
-        load_x(0, on_window(1, 0, [P, PACK, HALF], F32, "x0"))
-        load_x(1, on_window(1, 1, [P, PACK, HALF], F32, "x1"))
-        load_y(0, 1, on_window(1, 2, [P, 2, KP], F32, "y01"))
-        load_y(1, 1, on_window(1, 3, [P, 2, KP], F32, "y11"))
+        load_y(0, 1, on_window(1, 0, [P, 2, KP], F32, "y01"))
+        load_x(0, on_window(1, 1, [P, PACK, HALF], F32, "x0"))
+        load_y(1, 1, on_window(1, 2, [P, 2, KP], F32, "y11"))
+        load_x(1, on_window(1, 3, [P, PACK, HALF], F32, "x1"))
         for pair in range(2):
             turn_y(pair, 1, 0, pair)
         place(0, slice(0, 2), on_s)
@@ -259,45 +270,52 @@ def tile_attend_gpq_lch_x_kernel(tc, xT, cb, norm, ts, y, wt, offs, out):
         place(0, slice(last, PACK), on_v, slice(2, 4))
         round_x(0, "x_bf0")
         quant_kd(0, "kd_codes0")
-        place(1, slice(last, PACK), on_s, slice(0, 2))
-        place(1, slice(last, PACK), on_v, slice(2, 4))
+        place(1, slice(last, PACK), on_v)
         quant_x(0, "x_codes0")
         quant_kd(1, "x_bf0")
         for g in range(G):
             for pair in range(2):
                 scores(2 + 2 * g + pair, g, 0, pair)
+        for pair in range(2):
+            turn_y(pair, 0, 1, pair)
         round_x(1, "x_bf1")
         for g in range(G):
-            residual(g, 0, "z%d_0" % g)
-            tanh(g, 0)
-        turn_last_plane(4, "k_d1")
-        for g in range(G):
-            for pair in range(2):
-                turn_y(2 * g + pair, g, 1, pair)
+            residual(g, 0, keep.tile([P, PACK, HALF], F32, name="z%d_0" % g, tag="z%d_0" % g, align_bytes=64))
+        tanh(0, 0)
+        th_woven = keep.tile([P, HALF, PACK], F32, name="th_woven")
+        for i in range(2):
+            rows = slice(i * P, (i + 1) * P)
+            nc.scalar.activation(out=th_woven[:, rows, :].rearrange("m (c i) a -> m c a i", i=2),
+                                 in_=z[1, 0][:, :, rows].rearrange("m a (c i) -> m c a i", i=2), func=TANH)
+        turn_last_plane(2, "k_d1")
+        turn_y(6, 1, 1, 0)
+        turn_y(3, 1, 1, 1)
+        quant_x(1, "x_codes1")
         weigh(0, 0, 0, 2)
-        quant_x(1, "th0_0")
         quant_h(0, 0, 0, 2)
-        weigh(1, 0, 0, 2)
         quant_kn(0, slice(last, PACK), k_n_late[:, 0].rearrange("m p a -> m (p a)"))
         quant_kn(1, slice(2, PACK), k_n_late[:, 1:3].rearrange("m s p a -> m (s p a)"))
-        quant_h(1, 0, 0, 2)
-        for g, banks in enumerate(((5, 4), (0, 1))):
+        h_bf[1, 0] = on_window(2, 1, [P, HALF, PACK], BF16, "h_bf1_0")
+        nc.gpsimd.tensor_tensor(h_bf[1, 0][:], th_woven[:], weight_woven[:], MULT)
+        for g, banks in enumerate(((0, 1), (4, 5))):
             for pair in range(2):
                 scores(banks[pair], g, 1, pair)
-        for g in range(G):
-            for i in range(2):
-                grad(g, 0, i, 6 + i)
-        residual(0, 1, "th1_0")
-        tanh(0, 1)
-        residual(1, 1, "z1_1")
-        tanh(1, 1)
         for i in range(2):
-            finish(0, i, ("th1_0", "z1_1")[i])
+            grad(0, 0, i, (7, 2)[i])
+        residual(0, 1, on_window(2, 1.5, [P, PACK, HALF], F32, "z0_1"))
+        tanh(0, 1)
+        residual(1, 1, keep.tile([P, PACK, HALF], F32, name="z1_1", tag="z1_1", align_bytes=64))
+        tanh(1, 1)
+        quant_h(1, 0, 0, 2)
+        for i in range(2):
+            grad(1, 0, i)
+        for i in range(2):
+            finish(0, i, ("res_first", "z1_1")[i])
         weigh(0, 1, 0, 2)
         weigh(1, 1, 0, 1)
         quant_h(0, 1, 0, 2)
         for i in range(2):
-            grad(0, 1, i, 2 + i)
+            grad(0, 1, i, (6, 3)[i])
         for i in range(2):
             if i == 0:
                 weigh(1, 1, 1, 1)

@@ -66,9 +66,10 @@ def tile_attend_gpq_lch_x_kernel(tc, xT, cb, norm, ts, y, wt, offs, out):
         nc.sync.dma_start(offsets[:], offs)
         nc.sync.dma_start(out=wt_col[:], in_=wt.rearrange("(p j) o -> p (j o)", j=PACK))
         nc.sync.dma_start(out=ts_col[:], in_=ts[0:1, :].rearrange("o (g p j) -> p (o g) j", g=G, j=PACK))
-        load_y(0, 0, keep.tile([P, 2, KP], F32, name="y_first"))
+        y_early = [keep.tile([P, N], F32, name="y_early%d" % i) for i in range(2)]
+        nc.sync.dma_start(out=y_early[0][:], in_=y[0:P, :])
         nc.sync.dma_start(out=win[1][:], in_=cb_planes[1])
-        load_y(1, 0, keep.tile([P, 2, KP], F32, name="y_second"))
+        nc.sync.dma_start(out=y_early[1][:], in_=y[P:HALF, :])
         nc.sync.dma_start(out=win[2][:], in_=cb_planes[2])
         nc.sync.dma_start(out=win[3][:], in_=cb_planes[3])
 
@@ -91,10 +92,9 @@ def tile_attend_gpq_lch_x_kernel(tc, xT, cb, norm, ts, y, wt, offs, out):
 
         last = PACK - 1
         k_d = [keep.tile([P, PACK, P, PACK], BF16, name="k_d%d" % g, tag="k_d%d" % g, align_bytes=64) for g in range(G)]
-        k_n_early = [keep.tile([P, last - g, P, PACK], BF16, name="k_n%d" % g, align_bytes=64) for g in range(G)]
-        k_n_late = on_window(2, 1, [P, 3, P, PACK], BF16, "k_n_late")
-        k_n = {(t, g): k_n_early[g][:, t] for g in range(G) for t in range(last - g)}
-        k_n[2, 1] = k_n_late[:, 1]
+        k_n_early = keep.tile([P, G, 2, 2, P // 2, PACK], BF16, name="k_n_early", align_bytes=64)
+        k_n_late = on_window(2, 1, [P, G, 2, 2, P // 2, PACK], BF16, "k_n_late")
+        k_n = (k_n_early, k_n_late)
         kn_codes = on_window(2, 0, [P, G, D], U32, "kn_codes")
         kn_scales = keep.tile([P, G, D], U8, name="kn_scales", align_bytes=64)
         kd_codes = {}
@@ -115,11 +115,14 @@ def tile_attend_gpq_lch_x_kernel(tc, xT, cb, norm, ts, y, wt, offs, out):
             turned = bank(6 + g, [P, PACK, P])
             for a in range(PACK):
                 nc.tensor.transpose(turned[:, a, :], picked[t, g][:, a:KP:PACK], ident[:])
-            nc.scalar.copy(out=k_n[t, g], in_=turned[:].rearrange("m a p -> m p a"))
+            nc.scalar.copy(out=k_n[t // 2][:, g, :, t % 2], in_=turned[:].rearrange("m a (h p) -> m h p a", h=2))
 
-        def quant_kn(g, planes, src):
-            cols = slice(planes.start * P, planes.stop * P)
-            nc.vector.quantize_mx(out=kn_codes[:, g, cols].bitcast(E4), scales=kn_scales[:, g, cols], in_=src)
+        def quant_kn(g, planes):
+            within = slice(planes.start % 2, (planes.stop - 1) % 2 + 1)
+            for h in range(2):
+                cols = slice(h * D // 2 + planes.start * P // 2, h * D // 2 + planes.stop * P // 2)
+                nc.vector.quantize_mx(out=kn_codes[:, g, cols].bitcast(E4), scales=kn_scales[:, g, cols],
+                                      in_=k_n[planes.start // 2][:, g, h, within].rearrange("m t p a -> m (t p a)"))
 
         def quant_kd(g, tag):
             kd_codes[g] = keep.tile([P, KP], U32, name="kd_codes%d" % g, tag=tag, align_bytes=64)
@@ -141,16 +144,23 @@ def tile_attend_gpq_lch_x_kernel(tc, xT, cb, norm, ts, y, wt, offs, out):
 
         def turn_y(b, g, hf, pair):
             if pair == 0:
-                if (g, hf) == (0, 1):
+                if g == 0:
                     yT[g, hf] = on_window(1, 1, [P, PACK, HALF], F32, "yT0_1")
                 else:
-                    tag = ("yT%d", "z%d_0")[hf] % g
-                    yT[g, hf] = keep.tile([P, PACK, HALF], F32, name="yT%d_%d" % (g, hf), tag=tag, align_bytes=64)
+                    yT[g, hf] = keep.tile([P, PACK, HALF], F32, name="yT1_1", tag="z1_0", align_bytes=64)
             turned = bank(b, [P, 2, 2, P])
             for e in range(2):
                 for i in range(2):
                     nc.tensor.transpose(turned[:, e, i, :], y_raw[g, hf][:, i, 2 * pair + e:KP:PACK], ident[:])
             nc.scalar.copy(out=yT[g, hf][:, 2 * pair:2 * pair + 2, :], in_=turned[:].rearrange("m e i p -> m e (i p)"))
+
+        def turn_early_y(g, i):
+            if i == 0:
+                yT[g, 0] = keep.tile([P, PACK, HALF], F32, name="yT%d_0" % g, tag="yT%d" % g, align_bytes=64)
+            turned = bank(g, [P, PACK, P])
+            for a in range(PACK):
+                nc.tensor.transpose(turned[:, a, :], y_early[i][:, g * KP + a:(g + 1) * KP:PACK], ident[:])
+            nc.scalar.copy(out=yT[g, 0][:, :, i * P:(i + 1) * P], in_=turned[:])
 
         def scores(b, g, hf, pair):
             acc[g, hf, pair] = bank(b, [P, 2, HALF])
@@ -173,13 +183,13 @@ def tile_attend_gpq_lch_x_kernel(tc, xT, cb, norm, ts, y, wt, offs, out):
                 rows = slice(i * P, (i + 1) * P)
                 nc.scalar.activation(out=th[g, hf][:, :, rows], in_=z[g, hf][:, :, rows], func=TANH)
 
-        def weigh(g, hf, first, tiles):
-            if first == 0:
-                h_bf[g, hf] = keep.tile([P, HALF, PACK], BF16, name="h_bf%d_%d" % (g, hf), align_bytes=64)
+        def weigh(g, hf, first, tiles, tag):
+            h_bf[g, hf, first] = keep.tile([P, tiles * P, PACK], BF16, name="h_bf%d_%d_%d" % (g, hf, first), tag=tag,
+                                           align_bytes=64)
             rows = slice(first * P, (first + tiles) * P)
             whole = slice(hf * HALF + rows.start, hf * HALF + rows.stop)
             walk = "m a (c i) -> m c a i"
-            nc.vector.tensor_tensor(h_bf[g, hf][:, rows, :].rearrange("m (c i) a -> m c a i", i=2),
+            nc.vector.tensor_tensor(h_bf[g, hf, first][:].rearrange("m (c i) a -> m c a i", i=2),
                                     th[g, hf][:, :, rows].rearrange(walk, i=2),
                                     weight[:, g, :, whole].rearrange(walk, i=2), MULT)
 
@@ -189,30 +199,32 @@ def tile_attend_gpq_lch_x_kernel(tc, xT, cb, norm, ts, y, wt, offs, out):
                 h_scales[g, hf] = keep.tile([P, HALF], U8, name="h_scales%d_%d" % (g, hf), align_bytes=64)
             rows = slice(first * P, (first + tiles) * P)
             nc.vector.quantize_mx(out=h_codes[g, hf][:, rows].bitcast(E5), scales=h_scales[g, hf][:, rows],
-                                  in_=h_bf[g, hf][:, rows, :].rearrange("m r a -> m (r a)"))
+                                  in_=h_bf[g, hf, first][:].rearrange("m r a -> m (r a)"))
 
-        def grad(g, hf, i, b=None):
+        def grad(g, hf, i, banks=None):
             rows = slice(i * P, (i + 1) * P)
             if g == 0:
-                sums[hf, i] = bank(b, [P, D])
-            nc.tensor.matmul_mx(out=sums[hf, i][:], lhsT=h_codes[g, hf][:, rows].bitcast(E5),
-                                lhsT_scale=h_scales[g, hf][:, rows],
-                                rhs=kn_codes[:, g, :].bitcast(E4), rhs_scale=kn_scales[:, g, :],
-                                start=(g == 0), stop=(g == G - 1))
+                sums[hf, i] = [bank(b, [P, D // len(banks)]) for b in banks]
+            width = D // len(sums[hf, i])
+            for h, total in enumerate(sums[hf, i]):
+                cols = slice(h * width, (h + 1) * width)
+                nc.tensor.matmul_mx(out=total[:], lhsT=h_codes[g, hf][:, rows].bitcast(E5),
+                                    lhsT_scale=h_scales[g, hf][:, rows],
+                                    rhs=kn_codes[:, g, cols].bitcast(E4), rhs_scale=kn_scales[:, g, cols],
+                                    start=(g == 0), stop=(g == G - 1))
 
         def finish(hf, i, tag):
             res = keep.tile([P, D], F32, name="res%d_%d" % (hf, i), tag=tag, align_bytes=64)
-            dst = res[:].rearrange("r (p t) -> r p t", t=PACK)
-            src = sums[hf, i][:].rearrange("r (t p) -> r p t", t=PACK)
             rows = slice(hf * HALF + i * P, hf * HALF + (i + 1) * P)
-            if (hf, i) != (1, 1):
-                nc.scalar.copy(out=dst, in_=src)
+            if len(sums[hf, i]) == 1:
+                nc.scalar.copy(out=res[:].rearrange("r (h p t) -> r h p t", h=2, t=PACK),
+                               in_=sums[hf, i][0][:].rearrange("r (h t p) -> r h p t", h=2, t=PACK))
                 nc.sync.dma_start(out=out[rows, :], in_=res[:])
             else:
-                for e in range(2):
-                    ps = slice(e * P // 2, (e + 1) * P // 2)
-                    cols = slice(e * D // 2, (e + 1) * D // 2)
-                    nc.vector.tensor_copy(out=dst[:, ps, :], in_=src[:, ps, :])
+                for h, copy in enumerate((nc.vector.tensor_copy, nc.scalar.copy)):
+                    cols = slice(h * D // 2, (h + 1) * D // 2)
+                    copy(out=res[:, cols].rearrange("r (p t) -> r p t", t=PACK),
+                         in_=sums[hf, i][h][:].rearrange("r (t p) -> r p t", t=PACK))
                     nc.sync.dma_start(out=out[rows, cols], in_=res[:, cols])
 
         def turn_last_plane(b, tag):
@@ -224,9 +236,9 @@ def tile_attend_gpq_lch_x_kernel(tc, xT, cb, norm, ts, y, wt, offs, out):
             for g in range(G):
                 for u in range(2):
                     nc.tensor.transpose(turned[:, g, u, :], words[:, g, u:2 * P:2], ident[:])
-            late_words = k_n_late[:].rearrange("m s p a -> m (s p a)").bitcast(F32).rearrange(
-                "m (s p u) -> m s p u", s=3, u=2)
-            nc.scalar.copy(out=late_words[:, 0:3:2], in_=turned[:].rearrange("m g u p -> m g p u"))
+            late_words = k_n_late[:].rearrange("m g h t p a -> m (g h t p a)").bitcast(F32).rearrange(
+                "m (g h t p u) -> m g h t p u", g=G, h=2, t=2, u=2)
+            nc.scalar.copy(out=late_words[:, :, :, 1], in_=turned[:].rearrange("m g u (h p) -> m g h p u", h=2))
 
         on_v, on_s = nc.vector.tensor_copy, nc.scalar.copy
         for g in range(G):
@@ -241,8 +253,8 @@ def tile_attend_gpq_lch_x_kernel(tc, xT, cb, norm, ts, y, wt, offs, out):
         nc.vector.tensor_tensor(weight_woven[:],
                                 wt_row[:, 0:HALF].rearrange("q (r o) -> q r o", o=1).to_broadcast([P, HALF, PACK]),
                                 ts_col[:, 1:2, :].to_broadcast([P, HALF, PACK]), MULT)
-        for pair in range(2):
-            turn_y(pair, 0, 0, pair)
+        for g in range(G):
+            turn_early_y(g, 0)
         for g in range(G):
             gather(1, g)
             turn_k(1, g)
@@ -250,8 +262,8 @@ def tile_attend_gpq_lch_x_kernel(tc, xT, cb, norm, ts, y, wt, offs, out):
         load_x(0, on_window(1, 1, [P, PACK, HALF], F32, "x0"))
         load_y(1, 1, on_window(1, 2, [P, 2, KP], F32, "y11"))
         load_x(1, on_window(1, 3, [P, PACK, HALF], F32, "x1"))
-        for pair in range(2):
-            turn_y(pair, 1, 0, pair)
+        for g in range(G):
+            turn_early_y(g, 1)
         place(0, slice(0, 2), on_s)
         place(1, slice(0, 2), on_v)
         gather(2, 0)
@@ -259,10 +271,10 @@ def tile_attend_gpq_lch_x_kernel(tc, xT, cb, norm, ts, y, wt, offs, out):
         gather(2, 1)
         place(1, slice(2, 3), on_v)
         for g in range(G):
-            quant_kn(g, slice(0, 2), k_n_early[g][:, 0:2].rearrange("m t p a -> m (t p a)"))
+            quant_kn(g, slice(0, 2))
         for g in range(G):
             turn_k(2, g)
-        quant_kn(0, slice(2, 3), k_n[2, 0].rearrange("m p a -> m (p a)"))
+        quant_kn(0, slice(2, 3))
 
         gather(last, 0)
         place(0, slice(last, PACK), on_s, slice(0, 2))
@@ -282,26 +294,26 @@ def tile_attend_gpq_lch_x_kernel(tc, xT, cb, norm, ts, y, wt, offs, out):
         for g in range(G):
             residual(g, 0, keep.tile([P, PACK, HALF], F32, name="z%d_0" % g, tag="z%d_0" % g, align_bytes=64))
         tanh(0, 0)
+        turn_last_plane(2, "k_d1")
         th_woven = keep.tile([P, HALF, PACK], F32, name="th_woven")
         for i in range(2):
             rows = slice(i * P, (i + 1) * P)
             nc.scalar.activation(out=th_woven[:, rows, :].rearrange("m (c i) a -> m c a i", i=2),
                                  in_=z[1, 0][:, :, rows].rearrange("m a (c i) -> m c a i", i=2), func=TANH)
-        turn_last_plane(2, "k_d1")
         turn_y(6, 1, 1, 0)
-        turn_y(3, 1, 1, 1)
-        quant_x(1, "x_codes1")
-        weigh(0, 0, 0, 2)
+        turn_y(5, 1, 1, 1)
+        quant_x(1, "yT1")
+        weigh(0, 0, 0, 2, "h_first")
         quant_h(0, 0, 0, 2)
-        quant_kn(0, slice(last, PACK), k_n_late[:, 0].rearrange("m p a -> m (p a)"))
-        quant_kn(1, slice(2, PACK), k_n_late[:, 1:3].rearrange("m s p a -> m (s p a)"))
-        h_bf[1, 0] = on_window(2, 1, [P, HALF, PACK], BF16, "h_bf1_0")
-        nc.gpsimd.tensor_tensor(h_bf[1, 0][:], th_woven[:], weight_woven[:], MULT)
-        for g, banks in enumerate(((0, 1), (4, 5))):
+        quant_kn(0, slice(last, PACK))
+        quant_kn(1, slice(2, PACK))
+        h_bf[1, 0, 0] = on_window(2, 1, [P, HALF, PACK], BF16, "h_bf1_0")
+        nc.gpsimd.tensor_tensor(h_bf[1, 0, 0][:], th_woven[:], weight_woven[:], MULT)
+        for g, banks in enumerate(((0, 1), (3, 4))):
             for pair in range(2):
                 scores(banks[pair], g, 1, pair)
         for i in range(2):
-            grad(0, 0, i, (7, 2)[i])
+            grad(0, 0, i, ((7,), (2,))[i])
         residual(0, 1, on_window(2, 1.5, [P, PACK, HALF], F32, "z0_1"))
         tanh(0, 1)
         residual(1, 1, keep.tile([P, PACK, HALF], F32, name="z1_1", tag="z1_1", align_bytes=64))
@@ -311,14 +323,16 @@ def tile_attend_gpq_lch_x_kernel(tc, xT, cb, norm, ts, y, wt, offs, out):
             grad(1, 0, i)
         for i in range(2):
             finish(0, i, ("res_first", "z1_1")[i])
-        weigh(0, 1, 0, 2)
-        weigh(1, 1, 0, 1)
-        quant_h(0, 1, 0, 2)
         for i in range(2):
-            grad(0, 1, i, (6, 3)[i])
+            weigh(0, 1, i, 1, "h_tile%d" % i)
+        quant_h(0, 1, 0, 1)
+        grad(0, 1, 0, (6,))
+        weigh(1, 1, 0, 1, "h_tile2")
+        quant_h(0, 1, 1, 1)
+        grad(0, 1, 1, (5, 0))
         for i in range(2):
-            if i == 0:
-                weigh(1, 1, 1, 1)
             quant_h(1, 1, i, 1)
             grad(1, 1, i)
             finish(1, i, "res%d" % i)
+            if i == 0:
+                weigh(1, 1, 1, 1, "h_tile1")

@@ -69,8 +69,8 @@ def tile_attend_gpq_lch_x_kernel(tc, xT, cb, norm, ts, y, wt, offs, out):
         y_early = [keep.tile([P, N], F32, name="y_early%d" % i) for i in range(2)]
         nc.sync.dma_start(out=y_early[0][:], in_=y[0:P, :])
         nc.sync.dma_start(out=win[1][:], in_=cb_planes[1])
-        nc.sync.dma_start(out=y_early[1][:], in_=y[P:HALF, :])
         nc.sync.dma_start(out=win[2][:], in_=cb_planes[2])
+        nc.sync.dma_start(out=y_early[1][:], in_=y[P:HALF, :])
         nc.sync.dma_start(out=win[3][:], in_=cb_planes[3])
 
         ident = keep.tile([P, P], F32, name="ident")
@@ -144,23 +144,18 @@ def tile_attend_gpq_lch_x_kernel(tc, xT, cb, norm, ts, y, wt, offs, out):
 
         def turn_y(b, g, hf, pair):
             if pair == 0:
-                if g == 0:
-                    yT[g, hf] = on_window(1, 1, [P, PACK, HALF], F32, "yT0_1")
-                else:
-                    yT[g, hf] = keep.tile([P, PACK, HALF], F32, name="yT1_1", tag="z1_0", align_bytes=64)
+                yT[g, hf] = on_window(1, 1, [P, PACK, HALF], F32, "yT0_1")
             turned = bank(b, [P, 2, 2, P])
             for e in range(2):
                 for i in range(2):
                     nc.tensor.transpose(turned[:, e, i, :], y_raw[g, hf][:, i, 2 * pair + e:KP:PACK], ident[:])
             nc.scalar.copy(out=yT[g, hf][:, 2 * pair:2 * pair + 2, :], in_=turned[:].rearrange("m e i p -> m e (i p)"))
 
-        def turn_early_y(g, i):
-            if i == 0:
-                yT[g, 0] = keep.tile([P, PACK, HALF], F32, name="yT%d_0" % g, tag="yT%d" % g, align_bytes=64)
-            turned = bank(g, [P, PACK, P])
+        def turn_y_tile(b, g, hf, i, rows):
+            turned = bank(b, [P, PACK, P])
             for a in range(PACK):
-                nc.tensor.transpose(turned[:, a, :], y_early[i][:, g * KP + a:(g + 1) * KP:PACK], ident[:])
-            nc.scalar.copy(out=yT[g, 0][:, :, i * P:(i + 1) * P], in_=turned[:])
+                nc.tensor.transpose(turned[:, a, :], rows[:, a:KP:PACK], ident[:])
+            nc.scalar.copy(out=yT[g, hf][:, :, i * P:(i + 1) * P], in_=turned[:])
 
         def scores(b, g, hf, pair):
             acc[g, hf, pair] = bank(b, [P, 2, HALF])
@@ -254,26 +249,29 @@ def tile_attend_gpq_lch_x_kernel(tc, xT, cb, norm, ts, y, wt, offs, out):
                                 wt_row[:, 0:HALF].rearrange("q (r o) -> q r o", o=1).to_broadcast([P, HALF, PACK]),
                                 ts_col[:, 1:2, :].to_broadcast([P, HALF, PACK]), MULT)
         for g in range(G):
-            turn_early_y(g, 0)
+            yT[g, 0] = keep.tile([P, PACK, HALF], F32, name="yT%d_0" % g, tag="yT%d" % g, align_bytes=64)
+            turn_y_tile(g, g, 0, 0, y_early[0][:, g * KP:(g + 1) * KP])
         for g in range(G):
             gather(1, g)
             turn_k(1, g)
         load_y(0, 1, on_window(1, 0, [P, 2, KP], F32, "y01"))
         load_x(0, on_window(1, 1, [P, PACK, HALF], F32, "x0"))
-        load_y(1, 1, on_window(1, 2, [P, 2, KP], F32, "y11"))
+        y_last = [on_window(1, 2 + i / 2, [P, KP], F32, "y_last%d" % i) for i in range(2)]
+        nc.sync.dma_start(out=y_last[0][:], in_=y[HALF:HALF + P, KP:N])
         load_x(1, on_window(1, 3, [P, PACK, HALF], F32, "x1"))
-        for g in range(G):
-            turn_early_y(g, 1)
+        nc.sync.dma_start(out=y_last[1][:], in_=y[HALF + P:R, KP:N])
         place(0, slice(0, 2), on_s)
         place(1, slice(0, 2), on_v)
         gather(2, 0)
         place(0, slice(2, 3), on_s)
+        turn_k(2, 0)
         gather(2, 1)
         place(1, slice(2, 3), on_v)
         for g in range(G):
             quant_kn(g, slice(0, 2))
+        turn_k(2, 1)
         for g in range(G):
-            turn_k(2, g)
+            turn_y_tile(g, g, 0, 1, y_early[1][:, g * KP:(g + 1) * KP])
         quant_kn(0, slice(2, 3))
 
         gather(last, 0)
@@ -300,8 +298,9 @@ def tile_attend_gpq_lch_x_kernel(tc, xT, cb, norm, ts, y, wt, offs, out):
             rows = slice(i * P, (i + 1) * P)
             nc.scalar.activation(out=th_woven[:, rows, :].rearrange("m (c i) a -> m c a i", i=2),
                                  in_=z[1, 0][:, :, rows].rearrange("m a (c i) -> m c a i", i=2), func=TANH)
-        turn_y(6, 1, 1, 0)
-        turn_y(5, 1, 1, 1)
+        yT[1, 1] = keep.tile([P, PACK, HALF], F32, name="yT1_1", tag="z1_0", align_bytes=64)
+        for i, b in enumerate((6, 5)):
+            turn_y_tile(b, 1, 1, i, y_last[i][:])
         quant_x(1, "yT1")
         weigh(0, 0, 0, 2, "h_first")
         quant_h(0, 0, 0, 2)

@@ -296,8 +296,8 @@ def tile_attend_gpq_lch_x_kernel(tc, xT, cb, norm, ts, y, wt, offs, out):
         th_woven = keep.tile([P, HALF, PACK], F32, name="th_woven")
         for i in range(2):
             rows = slice(i * P, (i + 1) * P)
-            nc.scalar.activation(out=th_woven[:, rows, :].rearrange("m (c i) a -> m c a i", i=2),
-                                 in_=z[1, 0][:, :, rows].rearrange("m a (c i) -> m c a i", i=2), func=TANH)
+            nc.scalar.activation(out=th_woven[:, rows, :], in_=z[1, 0][:, :, rows].rearrange("m a r -> m r a"),
+                                 func=TANH)
         yT[1, 1] = keep.tile([P, PACK, HALF], F32, name="yT1_1", tag="z1_0", align_bytes=64)
         for i, b in enumerate((6, 5)):
             turn_y_tile(b, 1, 1, i, y_last[i][:])

@@ -99,30 +99,39 @@ def tile_attend_gpq_lch_x_kernel(tc, xT, cb, norm, ts, y, wt, offs, out):
         kn_scales = keep.tile([P, G, D], U8, name="kn_scales", align_bytes=64)
         kd_codes = {}
         kd_scales = [keep.tile([P, KP], U8, name="kd_scales%d" % g, align_bytes=64) for g in range(G)]
-        picked_planes = [keep.tile([P, PACK, KP], F32, name="picked%d" % g) for g in range(G)]
-        picked = {(t, g): picked_planes[g][:, t, :] for t in range(PACK) for g in range(G)}
+        picked = keep.tile([P, PACK, G, KP], F32, name="picked")
 
         def gather(t, g):
             first = g * KP // 16
-            nc.vector.tensor_tensor(picked[t, g], win[t][:].indirect(offsets[:, first:first + KP // 16]),
+            nc.vector.tensor_tensor(picked[:, t, g], win[t][:].indirect(offsets[:, first:first + KP // 16]),
                                     norm_row[:, g, :], MULT)
 
         def place(g, planes, copy, slots=slice(0, PACK)):
             copy(out=k_d[g][:, slots, :, planes],
-                 in_=picked_planes[g][:, planes, :].rearrange("p t (m a) -> p a m t", a=PACK)[:, slots])
+                 in_=picked[:, planes, g].rearrange("p t (m a) -> p a m t", a=PACK)[:, slots])
 
-        def turn_k(t, g):
-            turned = bank(6 + g, [P, PACK, P])
-            for a in range(PACK):
-                nc.tensor.transpose(turned[:, a, :], picked[t, g][:, a:KP:PACK], ident[:])
-            nc.scalar.copy(out=k_n[t // 2][:, g, :, t % 2], in_=turned[:].rearrange("m a (h p) -> m h p a", h=2))
+        def turn_k(b, t, rounded):
+            words = rounded[:].rearrange("p g c -> p (g c)").bitcast(F32).rearrange("p (g w) -> p g w", g=G)
+            turned = bank(b, [P, G, 2, P])
+            for g in range(G):
+                for u in range(2):
+                    nc.tensor.transpose(turned[:, g, u, :], words[:, g, u:2 * P:2], ident[:])
+            dst = k_n[t // 2][:].rearrange("m g h t p a -> m (g h t p a)").bitcast(F32).rearrange(
+                "m (g h t p u) -> m g h t p u", g=G, h=2, t=2, u=2)
+            nc.scalar.copy(out=dst[:, :, :, t % 2], in_=turned[:].rearrange("m g u (h p) -> m g h p u", h=2))
 
-        def quant_kn(g, planes):
-            within = slice(planes.start % 2, (planes.stop - 1) % 2 + 1)
-            for h in range(2):
-                cols = slice(h * D // 2 + planes.start * P // 2, h * D // 2 + planes.stop * P // 2)
-                nc.vector.quantize_mx(out=kn_codes[:, g, cols].bitcast(E4), scales=kn_scales[:, g, cols],
-                                      in_=k_n[planes.start // 2][:, g, h, within].rearrange("m t p a -> m (t p a)"))
+        def turn_early_k(b, t):
+            rounded = keep.tile([P, G, KP], BF16, name="rounded%d" % t)
+            for g in range(G):
+                nc.scalar.copy(out=rounded[:, g], in_=picked[:, t, g])
+            turn_k(b, t, rounded)
+
+        def quant_kn(u):
+            for g in range(G):
+                for h in range(2):
+                    cols = slice(h * D // 2 + u * P, h * D // 2 + (u + 1) * P)
+                    nc.vector.quantize_mx(out=kn_codes[:, g, cols].bitcast(E4), scales=kn_scales[:, g, cols],
+                                          in_=k_n[u][:, g, h].rearrange("m t p a -> m (t p a)"))
 
         def quant_kd(g, tag):
             kd_codes[g] = keep.tile([P, KP], U32, name="kd_codes%d" % g, tag=tag, align_bytes=64)
@@ -131,8 +140,8 @@ def tile_attend_gpq_lch_x_kernel(tc, xT, cb, norm, ts, y, wt, offs, out):
 
         x_bf, x_codes, x_scales, yT, acc, z, th, h_bf, h_codes, h_scales, sums = ({} for e in range(11))
 
-        def round_x(hf, tag):
-            x_bf[hf] = keep.tile([P, HALF, PACK], BF16, name="x_bf%d" % hf, tag=tag, align_bytes=64)
+        def round_x(hf, tile):
+            x_bf[hf] = tile
             nc.scalar.copy(out=x_bf[hf][:].rearrange("p (c i) t -> p c t i", i=2),
                            in_=x_raw[hf][:].rearrange("p t (c i) -> p c t i", i=2))
 
@@ -143,8 +152,6 @@ def tile_attend_gpq_lch_x_kernel(tc, xT, cb, norm, ts, y, wt, offs, out):
                                   in_=x_bf[hf][:].rearrange("p r t -> p (r t)"))
 
         def turn_y(b, g, hf, pair):
-            if pair == 0:
-                yT[g, hf] = on_window(1, 1, [P, PACK, HALF], F32, "yT0_1")
             turned = bank(b, [P, 2, 2, P])
             for e in range(2):
                 for i in range(2):
@@ -222,23 +229,10 @@ def tile_attend_gpq_lch_x_kernel(tc, xT, cb, norm, ts, y, wt, offs, out):
                          in_=sums[hf, i][h][:].rearrange("r (t p) -> r p t", t=PACK))
                     nc.sync.dma_start(out=out[rows, cols], in_=res[:, cols])
 
-        def turn_last_plane(b, tag):
-            pairs = keep.tile([P, G, KP], BF16, name="pairs", tag=tag, align_bytes=64)
-            for g in range(G):
-                nc.gpsimd.tensor_scalar(pairs[:, g], picked[last, g], 1.0, 0.0, MULT, ADD)
-            words = pairs[:].rearrange("p g c -> p (g c)").bitcast(F32).rearrange("p (g w) -> p g w", g=G)
-            turned = bank(b, [P, G, 2, P])
-            for g in range(G):
-                for u in range(2):
-                    nc.tensor.transpose(turned[:, g, u, :], words[:, g, u:2 * P:2], ident[:])
-            late_words = k_n_late[:].rearrange("m g h t p a -> m (g h t p a)").bitcast(F32).rearrange(
-                "m (g h t p u) -> m g h t p u", g=G, h=2, t=2, u=2)
-            nc.scalar.copy(out=late_words[:, :, :, 1], in_=turned[:].rearrange("m g u (h p) -> m g h p u", h=2))
-
         on_v, on_s = nc.vector.tensor_copy, nc.scalar.copy
         for g in range(G):
             gather(0, g)
-            turn_k(0, g)
+        turn_early_k(6, 0)
         weight = on_window(0, 0, [P, G, PACK, R], F32, "weight")
         for g in range(G):
             for a in range(PACK):
@@ -253,32 +247,28 @@ def tile_attend_gpq_lch_x_kernel(tc, xT, cb, norm, ts, y, wt, offs, out):
             turn_y_tile(g, g, 0, 0, y_early[0][:, g * KP:(g + 1) * KP])
         for g in range(G):
             gather(1, g)
-            turn_k(1, g)
         load_y(0, 1, on_window(1, 0, [P, 2, KP], F32, "y01"))
-        load_x(0, on_window(1, 1, [P, PACK, HALF], F32, "x0"))
-        y_last = [on_window(1, 2 + i / 2, [P, KP], F32, "y_last%d" % i) for i in range(2)]
-        nc.sync.dma_start(out=y_last[0][:], in_=y[HALF:HALF + P, KP:N])
-        load_x(1, on_window(1, 3, [P, PACK, HALF], F32, "x1"))
-        nc.sync.dma_start(out=y_last[1][:], in_=y[HALF + P:R, KP:N])
+        for hf in range(2):
+            load_x(hf, on_window(1, 1 + hf, [P, PACK, HALF], F32, "x%d" % hf))
+        load_y(1, 1, on_window(1, 3, [P, 2, KP], F32, "y11"))
+        turn_early_k(6, 1)
         place(0, slice(0, 2), on_s)
         place(1, slice(0, 2), on_v)
-        gather(2, 0)
-        place(0, slice(2, 3), on_s)
-        turn_k(2, 0)
-        gather(2, 1)
+        for g in range(G):
+            gather(2, g)
+        place(0, slice(2, 3), on_s, slice(0, 2))
+        place(0, slice(2, 3), on_v, slice(2, 4))
         place(1, slice(2, 3), on_v)
         for g in range(G):
-            quant_kn(g, slice(0, 2))
-        turn_k(2, 1)
-        for g in range(G):
             turn_y_tile(g, g, 0, 1, y_early[1][:, g * KP:(g + 1) * KP])
-        quant_kn(0, slice(2, 3))
+        turn_early_k(0, 2)
+        quant_kn(0)
 
         gather(last, 0)
         place(0, slice(last, PACK), on_s, slice(0, 2))
         gather(last, 1)
         place(0, slice(last, PACK), on_v, slice(2, 4))
-        round_x(0, "x_bf0")
+        round_x(0, keep.tile([P, HALF, PACK], BF16, name="x_bf0", tag="x_bf0", align_bytes=64))
         quant_kd(0, "kd_codes0")
         place(1, slice(last, PACK), on_v)
         quant_x(0, "x_codes0")
@@ -286,33 +276,35 @@ def tile_attend_gpq_lch_x_kernel(tc, xT, cb, norm, ts, y, wt, offs, out):
         for g in range(G):
             for pair in range(2):
                 scores(2 + 2 * g + pair, g, 0, pair)
+        round_x(1, keep.tile([P, HALF, PACK], BF16, name="x_bf1", align_bytes=64))
+        yT[0, 1] = on_window(1, 2, [P, PACK, HALF], F32, "yT0_1")
         for pair in range(2):
-            turn_y(pair, 0, 1, pair)
-        round_x(1, "x_bf1")
+            turn_y(6 + pair, 0, 1, pair)
+        rounded = keep.tile([P, G, KP], BF16, name="rounded3", tag="k_d1", align_bytes=64)
+        nc.gpsimd.tensor_scalar(rounded[:], picked[:, last], 1.0, 0.0, MULT, ADD)
         for g in range(G):
             residual(g, 0, keep.tile([P, PACK, HALF], F32, name="z%d_0" % g, tag="z%d_0" % g, align_bytes=64))
         tanh(0, 0)
-        turn_last_plane(2, "k_d1")
+        turn_k(2, last, rounded)
         th_woven = keep.tile([P, HALF, PACK], F32, name="th_woven")
         for i in range(2):
             rows = slice(i * P, (i + 1) * P)
             nc.scalar.activation(out=th_woven[:, rows, :], in_=z[1, 0][:, :, rows].rearrange("m a r -> m r a"),
                                  func=TANH)
         yT[1, 1] = keep.tile([P, PACK, HALF], F32, name="yT1_1", tag="z1_0", align_bytes=64)
-        for i, b in enumerate((6, 5)):
-            turn_y_tile(b, 1, 1, i, y_last[i][:])
+        turn_y(4, 1, 1, 0)
         quant_x(1, "yT1")
-        weigh(0, 0, 0, 2, "h_first")
-        quant_h(0, 0, 0, 2)
-        quant_kn(0, slice(last, PACK))
-        quant_kn(1, slice(2, PACK))
-        h_bf[1, 0, 0] = on_window(2, 1, [P, HALF, PACK], BF16, "h_bf1_0")
-        nc.gpsimd.tensor_tensor(h_bf[1, 0, 0][:], th_woven[:], weight_woven[:], MULT)
-        for g, banks in enumerate(((0, 1), (3, 4))):
+        for g, banks in enumerate(((6, 7), (3, 0))):
             for pair in range(2):
                 scores(banks[pair], g, 1, pair)
+        turn_y(2, 1, 1, 1)
+        weigh(0, 0, 0, 2, "h_first")
+        quant_kn(1)
+        quant_h(0, 0, 0, 2)
+        h_bf[1, 0, 0] = on_window(2, 1, [P, HALF, PACK], BF16, "h_bf1_0")
+        nc.gpsimd.tensor_tensor(h_bf[1, 0, 0][:], th_woven[:], weight_woven[:], MULT)
         for i in range(2):
-            grad(0, 0, i, ((7,), (2,))[i])
+            grad(0, 0, i, ((1,), (5,))[i])
         residual(0, 1, on_window(2, 1.5, [P, PACK, HALF], F32, "z0_1"))
         tanh(0, 1)
         residual(1, 1, keep.tile([P, PACK, HALF], F32, name="z1_1", tag="z1_1", align_bytes=64))
@@ -325,10 +317,10 @@ def tile_attend_gpq_lch_x_kernel(tc, xT, cb, norm, ts, y, wt, offs, out):
         for i in range(2):
             weigh(0, 1, i, 1, "h_tile%d" % i)
         quant_h(0, 1, 0, 1)
-        grad(0, 1, 0, (6,))
+        grad(0, 1, 0, (4,))
         weigh(1, 1, 0, 1, "h_tile2")
         quant_h(0, 1, 1, 1)
-        grad(0, 1, 1, (5, 0))
+        grad(0, 1, 1, (2, 6))
         for i in range(2):
             quant_h(1, 1, i, 1)
             grad(1, 1, i)

@@ -61,16 +61,17 @@ def tile_attend_gpq_lch_x_kernel(tc, xT, cb, norm, ts, y, wt, offs, out):
             nc.sync.dma_start(out=y_raw[g, hf][:], in_=y[hf * HALF:(hf + 1) * HALF, g * KP:(g + 1) * KP]
                               .rearrange("(i p) c -> p i c", p=P))
 
-        nc.sync.dma_start(out=norm_col[:], in_=norm[0:1, :].rearrange("o (g p j) -> p (o g) j", g=G, j=PACK))
-        nc.sync.dma_start(out=win[0][:], in_=cb_planes[0])
-        nc.sync.dma_start(offsets[:], offs)
+        y_early = [keep.tile([P, N], F32, name="y_early%d" % i) for i in range(2)]
+        nc.sync.dma_start(out=win[0][:, 0:N], in_=cb_planes[0][:, 0:N])
         nc.sync.dma_start(out=wt_col[:], in_=wt.rearrange("(p j) o -> p (j o)", j=PACK))
         nc.sync.dma_start(out=ts_col[:], in_=ts[0:1, :].rearrange("o (g p j) -> p (o g) j", g=G, j=PACK))
-        y_early = [keep.tile([P, N], F32, name="y_early%d" % i) for i in range(2)]
-        nc.sync.dma_start(out=y_early[0][:], in_=y[0:P, :])
+        nc.sync.dma_start(out=norm_col[:], in_=norm[0:1, :].rearrange("o (g p j) -> p (o g) j", g=G, j=PACK))
+        nc.sync.dma_start(offsets[:], offs)
+        nc.sync.dma_start(out=win[0][:, N:C], in_=cb_planes[0][:, N:C])
         nc.sync.dma_start(out=win[1][:], in_=cb_planes[1])
         nc.sync.dma_start(out=win[2][:], in_=cb_planes[2])
-        nc.sync.dma_start(out=y_early[1][:], in_=y[P:HALF, :])
+        for i in range(2):
+            nc.sync.dma_start(out=y_early[i][:], in_=y[i * P:(i + 1) * P, :])
         nc.sync.dma_start(out=win[3][:], in_=cb_planes[3])
 
         ident = keep.tile([P, P], F32, name="ident")
@@ -82,19 +83,29 @@ def tile_attend_gpq_lch_x_kernel(tc, xT, cb, norm, ts, y, wt, offs, out):
                 nc.tensor.transpose(turned[:, j, :], col[:, j:j + 1].to_broadcast([P, P]), ident[:])
             return turned
 
+        wt_row = keep.tile([P, R], F32, name="wt_row", tag="wt_row")
+        nc.scalar.copy(out=wt_row[:].rearrange("q (p j) -> q p j", j=PACK),
+                       in_=spread(6, wt_col[:])[:].rearrange("q j p -> q p j"))
         norm_row = keep.tile([P, G, KP], F32, name="norm_row")
         for g in range(G):
             nc.scalar.copy(out=norm_row[:, g, :].rearrange("q (p j) -> q p j", j=PACK),
                            in_=spread(1 + g, norm_col[:, g, :])[:].rearrange("q j p -> q p j"))
-        wt_row = keep.tile([P, R], F32, name="wt_row", tag="wt_row")
-        nc.scalar.copy(out=wt_row[:].rearrange("q (p j) -> q p j", j=PACK),
-                       in_=spread(6, wt_col[:])[:].rearrange("q j p -> q p j"))
+        weight = keep.tile([P, G, PACK, R], F32, name="weight")
+        for g in range(G):
+            for a in range(PACK):
+                rows = slice(g * HALF, R)
+                nc.vector.tensor_scalar(weight[:, g, a, rows], wt_row[:, rows], ts_col[:, g, a:a + 1], None, MULT)
+        weight_woven = keep.tile([P, HALF, PACK], F32, name="weight_woven")
+        nc.vector.tensor_tensor(weight_woven[:],
+                                wt_row[:, 0:HALF].rearrange("q (r o) -> q r o", o=1).to_broadcast([P, HALF, PACK]),
+                                ts_col[:, 1:2, :].to_broadcast([P, HALF, PACK]), MULT)
 
         last = PACK - 1
         k_d = [keep.tile([P, PACK, P, PACK], BF16, name="k_d%d" % g, tag="k_d%d" % g, align_bytes=64) for g in range(G)]
         k_n_early = keep.tile([P, G, 2, 2, P // 2, PACK], BF16, name="k_n_early", align_bytes=64)
-        k_n_late = on_window(2, 1, [P, G, 2, 2, P // 2, PACK], BF16, "k_n_late")
-        k_n = (k_n_early, k_n_late)
+        k_n_third = keep.tile([P, G, 2, 1, P // 2, PACK], BF16, name="k_n_third", align_bytes=64)
+        k_n_last = on_window(2, 1.25, [P, G, 2, 1, P // 2, PACK], BF16, "k_n_last")
+        k_n = (k_n_early, k_n_early, k_n_third, k_n_last)
         kn_codes = on_window(2, 0, [P, G, D], U32, "kn_codes")
         kn_scales = keep.tile([P, G, D], U8, name="kn_scales", align_bytes=64)
         kd_codes = {}
@@ -116,9 +127,10 @@ def tile_attend_gpq_lch_x_kernel(tc, xT, cb, norm, ts, y, wt, offs, out):
             for g in range(G):
                 for u in range(2):
                     nc.tensor.transpose(turned[:, g, u, :], words[:, g, u:2 * P:2], ident[:])
-            dst = k_n[t // 2][:].rearrange("m g h t p a -> m (g h t p a)").bitcast(F32).rearrange(
-                "m (g h t p u) -> m g h t p u", g=G, h=2, t=2, u=2)
-            nc.scalar.copy(out=dst[:, :, :, t % 2], in_=turned[:].rearrange("m g u (h p) -> m g h p u", h=2))
+            planes = k_n[t].shape[3]
+            dst = k_n[t][:].rearrange("m g h t p a -> m (g h t p a)").bitcast(F32).rearrange(
+                "m (g h t p u) -> m g h t p u", g=G, h=2, t=planes, u=2)
+            nc.scalar.copy(out=dst[:, :, :, t % planes], in_=turned[:].rearrange("m g u (h p) -> m g h p u", h=2))
 
         def turn_early_k(b, t):
             rounded = keep.tile([P, G, KP], BF16, name="rounded%d" % t)
@@ -126,19 +138,20 @@ def tile_attend_gpq_lch_x_kernel(tc, xT, cb, norm, ts, y, wt, offs, out):
                 nc.scalar.copy(out=rounded[:, g], in_=picked[:, t, g])
             turn_k(b, t, rounded)
 
-        def quant_kn(u):
+        def quant_kn(t):
             for g in range(G):
                 for h in range(2):
-                    cols = slice(h * D // 2 + u * P, h * D // 2 + (u + 1) * P)
+                    start = h * D // 2 + t * P // 2
+                    cols = slice(start, start + k_n[t].shape[3] * P // 2)
                     nc.vector.quantize_mx(out=kn_codes[:, g, cols].bitcast(E4), scales=kn_scales[:, g, cols],
-                                          in_=k_n[u][:, g, h].rearrange("m t p a -> m (t p a)"))
+                                          in_=k_n[t][:, g, h].rearrange("m t p a -> m (t p a)"))
 
         def quant_kd(g, tag):
             kd_codes[g] = keep.tile([P, KP], U32, name="kd_codes%d" % g, tag=tag, align_bytes=64)
             nc.vector.quantize_mx(out=kd_codes[g][:].bitcast(E4), scales=kd_scales[g][:],
                                   in_=k_d[g][:].rearrange("p a m t -> p (a m t)"))
 
-        x_bf, x_codes, x_scales, yT, acc, z, th, h_bf, h_codes, h_scales, sums = ({} for e in range(11))
+        x_bf, x_codes, x_scales, yT, acc, z, th, h_bf, h_codes, h_scales, sums, upper = ({} for e in range(12))
 
         def round_x(hf, tile):
             x_bf[hf] = tile
@@ -151,18 +164,18 @@ def tile_attend_gpq_lch_x_kernel(tc, xT, cb, norm, ts, y, wt, offs, out):
             nc.vector.quantize_mx(out=x_codes[hf][:].bitcast(E4), scales=x_scales[hf][:],
                                   in_=x_bf[hf][:].rearrange("p r t -> p (r t)"))
 
-        def turn_y(b, g, hf, pair):
+        def turn_y(b, g, hf, pair, dst):
             turned = bank(b, [P, 2, 2, P])
             for e in range(2):
                 for i in range(2):
                     nc.tensor.transpose(turned[:, e, i, :], y_raw[g, hf][:, i, 2 * pair + e:KP:PACK], ident[:])
-            nc.scalar.copy(out=yT[g, hf][:, 2 * pair:2 * pair + 2, :], in_=turned[:].rearrange("m e i p -> m e (i p)"))
+            nc.scalar.copy(out=dst, in_=turned[:].rearrange("m e i p -> m e (i p)"))
 
         def turn_y_tile(b, g, hf, i, rows):
             turned = bank(b, [P, PACK, P])
             for a in range(PACK):
                 nc.tensor.transpose(turned[:, a, :], rows[:, a:KP:PACK], ident[:])
-            nc.scalar.copy(out=yT[g, hf][:, :, i * P:(i + 1) * P], in_=turned[:])
+            nc.scalar.copy(out=upper[g][:, :, i * P:(i + 1) * P], in_=turned[:])
 
         def scores(b, g, hf, pair):
             acc[g, hf, pair] = bank(b, [P, 2, HALF])
@@ -176,7 +189,7 @@ def tile_attend_gpq_lch_x_kernel(tc, xT, cb, norm, ts, y, wt, offs, out):
             z[g, hf] = tile
             for a in range(PACK):
                 nc.vector.scalar_tensor_tensor(out=z[g, hf][:, a, :], in0=acc[g, hf, a // 2][:, a % 2, :],
-                                               scalar=ts_col[:, g, a:a + 1], in1=yT[g, hf][:, a, :],
+                                               scalar=ts_col[:, g, a:a + 1], in1=yT[g, hf][a],
                                                op0=MULT, op1=SUB)
 
         def tanh(g, hf):
@@ -233,36 +246,31 @@ def tile_attend_gpq_lch_x_kernel(tc, xT, cb, norm, ts, y, wt, offs, out):
         for g in range(G):
             gather(0, g)
         turn_early_k(6, 0)
-        weight = on_window(0, 0, [P, G, PACK, R], F32, "weight")
         for g in range(G):
-            for a in range(PACK):
-                rows = slice(g * HALF, R)
-                nc.vector.tensor_scalar(weight[:, g, a, rows], wt_row[:, rows], ts_col[:, g, a:a + 1], None, MULT)
-        weight_woven = keep.tile([P, HALF, PACK], F32, name="weight_woven")
-        nc.vector.tensor_tensor(weight_woven[:],
-                                wt_row[:, 0:HALF].rearrange("q (r o) -> q r o", o=1).to_broadcast([P, HALF, PACK]),
-                                ts_col[:, 1:2, :].to_broadcast([P, HALF, PACK]), MULT)
-        for g in range(G):
-            yT[g, 0] = keep.tile([P, PACK, HALF], F32, name="yT%d_0" % g, tag="yT%d" % g, align_bytes=64)
-            turn_y_tile(g, g, 0, 0, y_early[0][:, g * KP:(g + 1) * KP])
+            place(g, slice(0, 1), on_v)
         for g in range(G):
             gather(1, g)
         load_y(0, 1, on_window(1, 0, [P, 2, KP], F32, "y01"))
-        for hf in range(2):
-            load_x(hf, on_window(1, 1 + hf, [P, PACK, HALF], F32, "x%d" % hf))
+        load_x(0, on_window(1, 1, [P, PACK, HALF], F32, "x0"))
         load_y(1, 1, on_window(1, 3, [P, 2, KP], F32, "y11"))
+        load_x(1, on_window(1, 2, [P, PACK, HALF], F32, "x1"))
         turn_early_k(6, 1)
-        place(0, slice(0, 2), on_s)
-        place(1, slice(0, 2), on_v)
+        for g in range(G):
+            place(g, slice(1, 2), on_v)
         for g in range(G):
             gather(2, g)
         place(0, slice(2, 3), on_s, slice(0, 2))
         place(0, slice(2, 3), on_v, slice(2, 4))
         place(1, slice(2, 3), on_v)
         for g in range(G):
-            turn_y_tile(g, g, 0, 1, y_early[1][:, g * KP:(g + 1) * KP])
-        turn_early_k(0, 2)
+            upper[g] = keep.tile([P, PACK, HALF], F32, name="yT%d_0" % g, tag="yT%d" % g, align_bytes=64)
+            yT[g, 0] = [upper[g][:, a, :] for a in range(PACK)]
+            turn_y_tile(g, g, 0, 0, y_early[0][:, g * KP:(g + 1) * KP])
+        turn_early_k(5, 2)
         quant_kn(0)
+        quant_kn(2)
+        for g in range(G):
+            turn_y_tile(g, g, 0, 1, y_early[1][:, g * KP:(g + 1) * KP])
 
         gather(last, 0)
         place(0, slice(last, PACK), on_s, slice(0, 2))
@@ -276,10 +284,13 @@ def tile_attend_gpq_lch_x_kernel(tc, xT, cb, norm, ts, y, wt, offs, out):
         for g in range(G):
             for pair in range(2):
                 scores(2 + 2 * g + pair, g, 0, pair)
-        round_x(1, keep.tile([P, HALF, PACK], BF16, name="x_bf1", align_bytes=64))
-        yT[0, 1] = on_window(1, 2, [P, PACK, HALF], F32, "yT0_1")
+        lower = on_window(1, 1, [P, PACK, HALF], F32, "yT0_1")
+        yT[0, 1] = [lower[:, a, :] for a in range(PACK)]
         for pair in range(2):
-            turn_y(6 + pair, 0, 1, pair)
+            turn_y(6 + pair, 0, 1, pair, lower[:, 2 * pair:2 * pair + 2, :])
+        last_first = keep.tile([P, 2, HALF], F32, name="yT1_1a", align_bytes=64)
+        turn_y(0, 1, 1, 0, last_first[:])
+        round_x(1, keep.tile([P, HALF, PACK], BF16, name="x_bf1", align_bytes=64))
         rounded = keep.tile([P, G, KP], BF16, name="rounded3", tag="k_d1", align_bytes=64)
         nc.gpsimd.tensor_scalar(rounded[:], picked[:, last], 1.0, 0.0, MULT, ADD)
         for g in range(G):
@@ -291,15 +302,15 @@ def tile_attend_gpq_lch_x_kernel(tc, xT, cb, norm, ts, y, wt, offs, out):
             rows = slice(i * P, (i + 1) * P)
             nc.scalar.activation(out=th_woven[:, rows, :], in_=z[1, 0][:, :, rows].rearrange("m a r -> m r a"),
                                  func=TANH)
-        yT[1, 1] = keep.tile([P, PACK, HALF], F32, name="yT1_1", tag="z1_0", align_bytes=64)
-        turn_y(4, 1, 1, 0)
+        last_second = keep.tile([P, 2, HALF], F32, name="yT1_1b", tag="z1_0", align_bytes=64)
+        yT[1, 1] = [half[:, e, :] for half in (last_first, last_second) for e in range(2)]
+        turn_y(4, 1, 1, 1, last_second[:])
         quant_x(1, "yT1")
         for g, banks in enumerate(((6, 7), (3, 0))):
             for pair in range(2):
                 scores(banks[pair], g, 1, pair)
-        turn_y(2, 1, 1, 1)
         weigh(0, 0, 0, 2, "h_first")
-        quant_kn(1)
+        quant_kn(last)
         quant_h(0, 0, 0, 2)
         h_bf[1, 0, 0] = on_window(2, 1, [P, HALF, PACK], BF16, "h_bf1_0")
         nc.gpsimd.tensor_tensor(h_bf[1, 0, 0][:], th_woven[:], weight_woven[:], MULT)

@@ -56,12 +56,10 @@ def tile_attend_gpq_lch_x_kernel(tc, xT, cb, norm, ts, y, wt, offs, out):
             x_raw[hf] = tile
             nc.sync.dma_start(out=x_raw[hf][:], in_=x_planes[:, :, hf * HALF:(hf + 1) * HALF])
 
-        def load_y(g, hf, tile):
-            y_raw[g, hf] = tile
-            nc.sync.dma_start(out=y_raw[g, hf][:], in_=y[hf * HALF:(hf + 1) * HALF, g * KP:(g + 1) * KP]
-                              .rearrange("(i p) c -> p i c", p=P))
+        def load_y(i, tile):
+            y_raw[i] = tile
+            nc.sync.dma_start(out=tile[:], in_=y[i * P:(i + 1) * P, :])
 
-        y_early = [keep.tile([P, N], F32, name="y_early%d" % i) for i in range(2)]
         nc.sync.dma_start(out=win[0][:, 0:N], in_=cb_planes[0][:, 0:N])
         nc.sync.dma_start(out=wt_col[:], in_=wt.rearrange("(p j) o -> p (j o)", j=PACK))
         nc.sync.dma_start(out=ts_col[:], in_=ts[0:1, :].rearrange("o (g p j) -> p (o g) j", g=G, j=PACK))
@@ -71,7 +69,7 @@ def tile_attend_gpq_lch_x_kernel(tc, xT, cb, norm, ts, y, wt, offs, out):
         nc.sync.dma_start(out=win[1][:], in_=cb_planes[1])
         nc.sync.dma_start(out=win[2][:], in_=cb_planes[2])
         for i in range(2):
-            nc.sync.dma_start(out=y_early[i][:], in_=y[i * P:(i + 1) * P, :])
+            load_y(i, keep.tile([P, N], F32, name="y_early%d" % i))
         nc.sync.dma_start(out=win[3][:], in_=cb_planes[3])
 
         ident = keep.tile([P, P], F32, name="ident")
@@ -151,7 +149,7 @@ def tile_attend_gpq_lch_x_kernel(tc, xT, cb, norm, ts, y, wt, offs, out):
             nc.vector.quantize_mx(out=kd_codes[g][:].bitcast(E4), scales=kd_scales[g][:],
                                   in_=k_d[g][:].rearrange("p a m t -> p (a m t)"))
 
-        x_bf, x_codes, x_scales, yT, acc, z, th, h_bf, h_codes, h_scales, sums, upper = ({} for e in range(12))
+        x_bf, x_codes, x_scales, yT, acc, z, th, h_bf, h_codes, h_scales, sums = ({} for e in range(11))
 
         def round_x(hf, tile):
             x_bf[hf] = tile
@@ -164,32 +162,25 @@ def tile_attend_gpq_lch_x_kernel(tc, xT, cb, norm, ts, y, wt, offs, out):
             nc.vector.quantize_mx(out=x_codes[hf][:].bitcast(E4), scales=x_scales[hf][:],
                                   in_=x_bf[hf][:].rearrange("p r t -> p (r t)"))
 
-        def turn_y(b, g, hf, pair, dst):
-            turned = bank(b, [P, 2, 2, P])
-            for e in range(2):
-                for i in range(2):
-                    nc.tensor.transpose(turned[:, e, i, :], y_raw[g, hf][:, i, 2 * pair + e:KP:PACK], ident[:])
-            nc.scalar.copy(out=dst, in_=turned[:].rearrange("m e i p -> m e (i p)"))
-
-        def turn_y_tile(b, g, hf, i, rows):
+        def turn_y(b, g, i):
             turned = bank(b, [P, PACK, P])
             for a in range(PACK):
-                nc.tensor.transpose(turned[:, a, :], rows[:, a:KP:PACK], ident[:])
-            nc.scalar.copy(out=upper[g][:, :, i * P:(i + 1) * P], in_=turned[:])
+                nc.tensor.transpose(turned[:, a, :], y_raw[i][:, g * KP + a:(g + 1) * KP:PACK], ident[:])
+            nc.scalar.copy(out=yT[g, i // 2][:, :, i % 2 * P:(i % 2 + 1) * P], in_=turned[:])
 
-        def scores(b, g, hf, pair):
-            acc[g, hf, pair] = bank(b, [P, 2, HALF])
-            for e in range(2):
-                cols = slice((2 * pair + e) * P, (2 * pair + e + 1) * P)
-                nc.tensor.matmul_mx(out=acc[g, hf, pair][:, e, :], lhsT=kd_codes[g][:, cols].bitcast(E4),
+        def scores(g, hf, banks):
+            for a, b in enumerate(banks):
+                acc[g, hf, a] = bank(b, [P, HALF])
+                cols = slice(a * P, (a + 1) * P)
+                nc.tensor.matmul_mx(out=acc[g, hf, a][:], lhsT=kd_codes[g][:, cols].bitcast(E4),
                                     lhsT_scale=kd_scales[g][:, cols], rhs=x_codes[hf][:].bitcast(E4),
                                     rhs_scale=x_scales[hf][:], start=True, stop=True)
 
         def residual(g, hf, tile):
             z[g, hf] = tile
             for a in range(PACK):
-                nc.vector.scalar_tensor_tensor(out=z[g, hf][:, a, :], in0=acc[g, hf, a // 2][:, a % 2, :],
-                                               scalar=ts_col[:, g, a:a + 1], in1=yT[g, hf][a],
+                nc.vector.scalar_tensor_tensor(out=z[g, hf][:, a, :], in0=acc[g, hf, a][:],
+                                               scalar=ts_col[:, g, a:a + 1], in1=yT[g, hf][:, a, :],
                                                op0=MULT, op1=SUB)
 
         def tanh(g, hf):
@@ -250,27 +241,26 @@ def tile_attend_gpq_lch_x_kernel(tc, xT, cb, norm, ts, y, wt, offs, out):
             place(g, slice(0, 1), on_v)
         for g in range(G):
             gather(1, g)
-        load_y(0, 1, on_window(1, 0, [P, 2, KP], F32, "y01"))
+        load_y(2, on_window(1, 0, [P, N], F32, "y2"))
         load_x(0, on_window(1, 1, [P, PACK, HALF], F32, "x0"))
-        load_y(1, 1, on_window(1, 3, [P, 2, KP], F32, "y11"))
-        load_x(1, on_window(1, 2, [P, PACK, HALF], F32, "x1"))
+        load_y(3, on_window(1, 3, [P, N], F32, "y3"))
         turn_early_k(6, 1)
         for g in range(G):
             place(g, slice(1, 2), on_v)
         for g in range(G):
             gather(2, g)
+        load_x(1, on_window(2, 3, [P, PACK, HALF], F32, "x1"))
         place(0, slice(2, 3), on_s, slice(0, 2))
         place(0, slice(2, 3), on_v, slice(2, 4))
         place(1, slice(2, 3), on_v)
         for g in range(G):
-            upper[g] = keep.tile([P, PACK, HALF], F32, name="yT%d_0" % g, tag="yT%d" % g, align_bytes=64)
-            yT[g, 0] = [upper[g][:, a, :] for a in range(PACK)]
-            turn_y_tile(g, g, 0, 0, y_early[0][:, g * KP:(g + 1) * KP])
+            yT[g, 0] = keep.tile([P, PACK, HALF], F32, name="yT%d_0" % g, tag="yT%d" % g, align_bytes=64)
+            turn_y(g, g, 0)
         turn_early_k(5, 2)
         quant_kn(0)
         quant_kn(2)
         for g in range(G):
-            turn_y_tile(g, g, 0, 1, y_early[1][:, g * KP:(g + 1) * KP])
+            turn_y(g, g, 1)
 
         gather(last, 0)
         place(0, slice(last, PACK), on_s, slice(0, 2))
@@ -282,40 +272,34 @@ def tile_attend_gpq_lch_x_kernel(tc, xT, cb, norm, ts, y, wt, offs, out):
         quant_x(0, "x_codes0")
         quant_kd(1, "x_bf0")
         for g in range(G):
-            for pair in range(2):
-                scores(2 + 2 * g + pair, g, 0, pair)
-        lower = on_window(1, 1, [P, PACK, HALF], F32, "yT0_1")
-        yT[0, 1] = [lower[:, a, :] for a in range(PACK)]
-        for pair in range(2):
-            turn_y(6 + pair, 0, 1, pair, lower[:, 2 * pair:2 * pair + 2, :])
-        last_first = keep.tile([P, 2, HALF], F32, name="yT1_1a", align_bytes=64)
-        turn_y(0, 1, 1, 0, last_first[:])
+            yT[g, 1] = on_window(1, 0.5 + g, [P, PACK, HALF], F32, "yT%d_1" % g)
+            turn_y(6 + g, g, 2)
+        turn_y(0, 0, 3)
+        scores(0, 0, (1, 2, 3, 4))
+        scores(1, 0, (5, 6, 7, 0))
         round_x(1, keep.tile([P, HALF, PACK], BF16, name="x_bf1", align_bytes=64))
         rounded = keep.tile([P, G, KP], BF16, name="rounded3", tag="k_d1", align_bytes=64)
         nc.gpsimd.tensor_scalar(rounded[:], picked[:, last], 1.0, 0.0, MULT, ADD)
         for g in range(G):
             residual(g, 0, keep.tile([P, PACK, HALF], F32, name="z%d_0" % g, tag="z%d_0" % g, align_bytes=64))
         tanh(0, 0)
-        turn_k(2, last, rounded)
+        turn_k(1, last, rounded)
         th_woven = keep.tile([P, HALF, PACK], F32, name="th_woven")
         for i in range(2):
             rows = slice(i * P, (i + 1) * P)
             nc.scalar.activation(out=th_woven[:, rows, :], in_=z[1, 0][:, :, rows].rearrange("m a r -> m r a"),
                                  func=TANH)
-        last_second = keep.tile([P, 2, HALF], F32, name="yT1_1b", tag="z1_0", align_bytes=64)
-        yT[1, 1] = [half[:, e, :] for half in (last_first, last_second) for e in range(2)]
-        turn_y(4, 1, 1, 1, last_second[:])
+        turn_y(0, 1, 3)
         quant_x(1, "yT1")
-        for g, banks in enumerate(((6, 7), (3, 0))):
-            for pair in range(2):
-                scores(banks[pair], g, 1, pair)
+        scores(0, 1, (2, 3, 4, 1))
+        scores(1, 1, (5, 6, 7, 0))
         weigh(0, 0, 0, 2, "h_first")
         quant_kn(last)
         quant_h(0, 0, 0, 2)
         h_bf[1, 0, 0] = on_window(2, 1, [P, HALF, PACK], BF16, "h_bf1_0")
         nc.gpsimd.tensor_tensor(h_bf[1, 0, 0][:], th_woven[:], weight_woven[:], MULT)
         for i in range(2):
-            grad(0, 0, i, ((1,), (5,))[i])
+            grad(0, 0, i, (2 + i,))
         residual(0, 1, on_window(2, 1.5, [P, PACK, HALF], F32, "z0_1"))
         tanh(0, 1)
         residual(1, 1, keep.tile([P, PACK, HALF], F32, name="z1_1", tag="z1_1", align_bytes=64))
@@ -331,7 +315,7 @@ def tile_attend_gpq_lch_x_kernel(tc, xT, cb, norm, ts, y, wt, offs, out):
         grad(0, 1, 0, (4,))
         weigh(1, 1, 0, 1, "h_tile2")
         quant_h(0, 1, 1, 1)
-        grad(0, 1, 1, (2, 6))
+        grad(0, 1, 1, (1, 5))
         for i in range(2):
             quant_h(1, 1, i, 1)
             grad(1, 1, i)

@@ -18,6 +18,7 @@ MULT = mybir.AluOpType.mult
 ADD = mybir.AluOpType.add
 SUB = mybir.AluOpType.subtract
 TANH = mybir.ActivationFunctionType.Tanh
+COPY = mybir.ActivationFunctionType.Copy
 
 P = 128
 PACK = 4
@@ -25,6 +26,7 @@ KP = P * PACK
 G = N // KP
 RT = R // P
 HALF = R // 2
+LEAD = 1280
 
 
 def tile_attend_gpq_lch_x_kernel(tc, xT, cb, norm, ts, y, wt, offs, out):
@@ -46,9 +48,10 @@ def tile_attend_gpq_lch_x_kernel(tc, xT, cb, norm, ts, y, wt, offs, out):
 
         win = [on_window(t, 0, [P, C], F32, "win%d" % t) for t in range(PACK)]
         x_raw, y_raw = {}, {}
-        norm_col = keep.tile([P, G, PACK], F32, name="norm_col")
+        rows_in = keep.tile([P, P + KP], F32, name="rows_in")
+        nc.vector.memset(rows_in[:], 0.0)
         ts_col = keep.tile([P, G, PACK], F32, name="ts_col")
-        wt_col = keep.tile([P, PACK], F32, name="wt_col")
+        runs = N // P
         cb_planes = cb.rearrange("(p t) c -> t p c", t=PACK)
         x_planes = xT.rearrange("(p t) r -> p t r", t=PACK)
 
@@ -60,12 +63,12 @@ def tile_attend_gpq_lch_x_kernel(tc, xT, cb, norm, ts, y, wt, offs, out):
             y_raw[i] = tile
             nc.sync.dma_start(out=tile[:], in_=y[i * P:(i + 1) * P, :])
 
-        nc.sync.dma_start(out=win[0][:, 0:N], in_=cb_planes[0][:, 0:N])
-        nc.sync.dma_start(out=wt_col[:], in_=wt.rearrange("(p j) o -> p (j o)", j=PACK))
-        nc.sync.dma_start(out=ts_col[:], in_=ts[0:1, :].rearrange("o (g p j) -> p (o g) j", g=G, j=PACK))
-        nc.sync.dma_start(out=norm_col[:], in_=norm[0:1, :].rearrange("o (g p j) -> p (o g) j", g=G, j=PACK))
+        nc.sync.dma_start(out=win[0][:, 0:LEAD], in_=cb_planes[0][:, 0:LEAD])
+        nc.sync.dma_start(out=rows_in[0:runs, 0:P], in_=norm[0:1, :].rearrange("o (k c) -> (o k) c", c=P))
+        nc.sync.dma_start(out=rows_in[runs:runs + RT, 0:P], in_=wt.rearrange("(k c) o -> k (c o)", c=P))
+        nc.sync.dma_start(out=rows_in[0:G, P:], in_=ts[0:1, :].rearrange("o (g c) -> (o g) c", g=G))
         nc.sync.dma_start(offsets[:], offs)
-        nc.sync.dma_start(out=win[0][:, N:C], in_=cb_planes[0][:, N:C])
+        nc.sync.dma_start(out=win[0][:, LEAD:C], in_=cb_planes[0][:, LEAD:C])
         nc.sync.dma_start(out=win[1][:], in_=cb_planes[1])
         nc.sync.dma_start(out=win[2][:], in_=cb_planes[2])
         for i in range(2):
@@ -75,24 +78,32 @@ def tile_attend_gpq_lch_x_kernel(tc, xT, cb, norm, ts, y, wt, offs, out):
         ident = keep.tile([P, P], F32, name="ident")
         make_identity(nc, ident[:])
 
-        def spread(b, col):
+        turned_rows = bank(0, [P, P])
+        nc.tensor.transpose(turned_rows[:], rows_in[:, 0:P], ident[:])
+        columns = keep.tile([P, runs + RT], F32, name="columns")
+        nc.scalar.copy(out=columns[:], in_=turned_rows[:, 0:runs + RT])
+        turned_ts = bank(3, [P, PACK, P])
+        for a in range(PACK):
+            nc.tensor.transpose(turned_ts[:, a, :], rows_in[:, P + a:P + KP:PACK], ident[:])
+        nc.scalar.copy(out=ts_col[:], in_=turned_ts[:, :, 0:G].rearrange("m a g -> m g a"))
+
+        def spread(b, first, row):
             turned = bank(b, [P, PACK, P])
             for j in range(PACK):
-                nc.tensor.transpose(turned[:, j, :], col[:, j:j + 1].to_broadcast([P, P]), ident[:])
-            return turned
+                nc.tensor.transpose(turned[:, j, :], columns[:, first + j:first + j + 1].to_broadcast([P, P]), ident[:])
+            nc.scalar.copy(out=row, in_=turned[:].rearrange("q j p -> q (j p)"))
 
         wt_row = keep.tile([P, R], F32, name="wt_row", tag="wt_row")
-        nc.scalar.copy(out=wt_row[:].rearrange("q (p j) -> q p j", j=PACK),
-                       in_=spread(6, wt_col[:])[:].rearrange("q j p -> q p j"))
+        spread(6, runs, wt_row[:])
         norm_row = keep.tile([P, G, KP], F32, name="norm_row")
         for g in range(G):
-            nc.scalar.copy(out=norm_row[:, g, :].rearrange("q (p j) -> q p j", j=PACK),
-                           in_=spread(1 + g, norm_col[:, g, :])[:].rearrange("q j p -> q p j"))
+            spread(1 + g, g * PACK, norm_row[:, g, :])
         weight = keep.tile([P, G, PACK, R], F32, name="weight")
         for g in range(G):
             for a in range(PACK):
                 rows = slice(g * HALF, R)
-                nc.vector.tensor_scalar(weight[:, g, a, rows], wt_row[:, rows], ts_col[:, g, a:a + 1], None, MULT)
+                nc.scalar.activation(out=weight[:, g, a, rows], in_=wt_row[:, rows], func=COPY,
+                                     scale=ts_col[:, g, a:a + 1])
         weight_woven = keep.tile([P, HALF, PACK], F32, name="weight_woven")
         nc.vector.tensor_tensor(weight_woven[:],
                                 wt_row[:, 0:HALF].rearrange("q (r o) -> q r o", o=1).to_broadcast([P, HALF, PACK]),

@@ -121,14 +121,13 @@ def tile_attend_gpq_lch_x_kernel(tc, xT, cb, norm, ts, y, wt, offs, out):
         kd_scales = [keep.tile([P, KP], U8, name="kd_scales%d" % g, align_bytes=64) for g in range(G)]
         picked = keep.tile([P, PACK, G, KP], F32, name="picked")
 
-        def gather(t, g):
-            first = g * KP // 16
-            nc.vector.tensor_tensor(picked[:, t, g], win[t][:].indirect(offsets[:, first:first + KP // 16]),
-                                    norm_row[:, g, :], MULT)
+        def gather(t, g, cols=slice(0, KP)):
+            lists = offsets[:, (g * KP + cols.start) // 16:(g * KP + cols.stop) // 16]
+            nc.vector.tensor_tensor(picked[:, t, g, cols], win[t][:].indirect(lists), norm_row[:, g, cols], MULT)
 
-        def place(g, planes, copy, slots=slice(0, PACK)):
-            copy(out=k_d[g][:, slots, :, planes],
-                 in_=picked[:, planes, g].rearrange("p t (m a) -> p a m t", a=PACK)[:, slots])
+        def place(g, planes, copy, cols=slice(0, KP)):
+            copy(out=k_d[g][:, :, cols.start // PACK:cols.stop // PACK, planes],
+                 in_=picked[:, planes, g, cols].rearrange("p t (m a) -> p a m t", a=PACK))
 
         def turn_k(b, t, rounded):
             words = rounded[:].rearrange("p g c -> p (g c)").bitcast(F32).rearrange("p (g w) -> p g w", g=G)
@@ -141,10 +140,10 @@ def tile_attend_gpq_lch_x_kernel(tc, xT, cb, norm, ts, y, wt, offs, out):
                 "m (g h t p u) -> m g h t p u", g=G, h=2, t=planes, u=2)
             nc.scalar.copy(out=dst[:, :, :, t % planes], in_=turned[:].rearrange("m g u (h p) -> m g h p u", h=2))
 
-        def turn_early_k(b, t):
+        def turn_early_k(b, t, copy):
             rounded = keep.tile([P, G, KP], BF16, name="rounded%d" % t)
             for g in range(G):
-                nc.scalar.copy(out=rounded[:, g], in_=picked[:, t, g])
+                copy(out=rounded[:, g], in_=picked[:, t, g])
             turn_k(b, t, rounded)
 
         def quant_kn(t):
@@ -203,12 +202,13 @@ def tile_attend_gpq_lch_x_kernel(tc, xT, cb, norm, ts, y, wt, offs, out):
         def weigh(g, hf, first, tiles, tag):
             h_bf[g, hf, first] = keep.tile([P, tiles * P, PACK], BF16, name="h_bf%d_%d_%d" % (g, hf, first), tag=tag,
                                            align_bytes=64)
-            rows = slice(first * P, (first + tiles) * P)
-            whole = slice(hf * HALF + rows.start, hf * HALF + rows.stop)
             walk = "m a (c i) -> m c a i"
-            nc.vector.tensor_tensor(h_bf[g, hf, first][:].rearrange("m (c i) a -> m c a i", i=2),
-                                    th[g, hf][:, :, rows].rearrange(walk, i=2),
-                                    weight[:, g, :, whole].rearrange(walk, i=2), MULT)
+            for e in range(tiles):
+                rows = slice((first + e) * P, (first + e + 1) * P)
+                whole = slice(hf * HALF + rows.start, hf * HALF + rows.stop)
+                nc.vector.tensor_tensor(h_bf[g, hf, first][:, e * P:(e + 1) * P].rearrange("m (c i) a -> m c a i", i=2),
+                                        th[g, hf][:, :, rows].rearrange(walk, i=2),
+                                        weight[:, g, :, whole].rearrange(walk, i=2), MULT)
 
         def quant_h(g, hf, first, tiles):
             if first == 0:
@@ -247,7 +247,7 @@ def tile_attend_gpq_lch_x_kernel(tc, xT, cb, norm, ts, y, wt, offs, out):
         on_v, on_s = nc.vector.tensor_copy, nc.scalar.copy
         for g in range(G):
             gather(0, g)
-        turn_early_k(6, 0)
+        turn_early_k(6, 0, on_s)
         for g in range(G):
             place(g, slice(0, 1), on_v)
         for g in range(G):
@@ -255,31 +255,33 @@ def tile_attend_gpq_lch_x_kernel(tc, xT, cb, norm, ts, y, wt, offs, out):
         load_y(2, on_window(1, 0, [P, N], F32, "y2"))
         load_x(0, on_window(1, 1, [P, PACK, HALF], F32, "x0"))
         load_y(3, on_window(1, 3, [P, N], F32, "y3"))
-        turn_early_k(6, 1)
+        turn_early_k(6, 1, on_s)
         for g in range(G):
             place(g, slice(1, 2), on_v)
         for g in range(G):
             gather(2, g)
         load_x(1, on_window(2, 3, [P, PACK, HALF], F32, "x1"))
-        place(0, slice(2, 3), on_s, slice(0, 2))
-        place(0, slice(2, 3), on_v, slice(2, 4))
-        place(1, slice(2, 3), on_v)
+        turn_early_k(5, 2, on_v)
+        for g, copy in enumerate((on_s, on_v)):
+            place(g, slice(2, 3), copy)
         for g in range(G):
             yT[g, 0] = keep.tile([P, PACK, HALF], F32, name="yT%d_0" % g, tag="yT%d" % g, align_bytes=64)
             turn_y(g, g, 0)
-        turn_early_k(5, 2)
         quant_kn(0)
         quant_kn(2)
         for g in range(G):
             turn_y(g, g, 1)
 
-        gather(last, 0)
-        place(0, slice(last, PACK), on_s, slice(0, 2))
-        gather(last, 1)
-        place(0, slice(last, PACK), on_v, slice(2, 4))
+        halves = (slice(0, KP // 2), slice(KP // 2, KP))
+        for cols in halves:
+            gather(last, 0, cols)
+            place(0, slice(last, PACK), on_s, cols)
+        for cols in halves:
+            gather(last, 1, cols)
         round_x(0, keep.tile([P, HALF, PACK], BF16, name="x_bf0", tag="x_bf0", align_bytes=64))
         quant_kd(0, "kd_codes0")
-        place(1, slice(last, PACK), on_v)
+        for cols in halves:
+            place(1, slice(last, PACK), on_v, cols)
         quant_x(0, "x_codes0")
         quant_kd(1, "x_bf0")
         for g in range(G):

@@ -94,16 +94,31 @@ def tile_attend_gpq_lch_x_kernel(tc, xT, cb, norm, ts, y, wt, offs, out):
             nc.scalar.copy(out=row, in_=turned[:].rearrange("q j p -> q (j p)"))
 
         wt_row = keep.tile([P, R], F32, name="wt_row", tag="wt_row")
-        spread(6, runs, wt_row[:])
+        spread(4, runs, wt_row[:])
         norm_row = keep.tile([P, G, KP], F32, name="norm_row")
         for g in range(G):
             spread(1 + g, g * PACK, norm_row[:, g, :])
-        weight = keep.tile([P, G, PACK, R], F32, name="weight")
-        for g in range(G):
+        weight = {}
+        ts_row = bank(5, [P, PACK, P])
+        for a in range(PACK):
+            nc.tensor.transpose(ts_row[:, a, :], ts_col[:, 0, a:a + 1].to_broadcast([P, P]), ident[:])
+        by_rows = {}
+
+        def turn_weight(b, i):
+            weight[0, i] = bank(b, [P, PACK, P])
             for a in range(PACK):
-                rows = slice(g * HALF, R)
-                nc.scalar.activation(out=weight[:, g, a, rows], in_=wt_row[:, rows], func=COPY,
+                nc.tensor.transpose(weight[0, i][:, a, :], by_rows[i][:, a, :], ident[:])
+
+        by_rows[2] = keep.tile([P, PACK, P], F32, name="by_rows")
+        nc.scalar.activation(out=by_rows[2][:], in_=ts_row[:], func=COPY, scale=columns[:, runs + 2:runs + 3])
+        turn_weight(7, 2)
+        for g, first, tiles in ((0, 0, 2), (0, 3, 1), (1, 2, 2)):
+            table = keep.tile([P, PACK, tiles * P], F32, name="weight%d_%d" % (g, first))
+            for a in range(PACK):
+                nc.scalar.activation(out=table[:, a, :], in_=wt_row[:, first * P:(first + tiles) * P], func=COPY,
                                      scale=ts_col[:, g, a:a + 1])
+            for e in range(tiles):
+                weight[g, first + e] = table[:, :, e * P:(e + 1) * P]
         weight_woven = keep.tile([P, HALF, PACK], F32, name="weight_woven")
         nc.vector.tensor_tensor(weight_woven[:],
                                 wt_row[:, 0:HALF].rearrange("q (r o) -> q r o", o=1).to_broadcast([P, HALF, PACK]),
@@ -113,8 +128,7 @@ def tile_attend_gpq_lch_x_kernel(tc, xT, cb, norm, ts, y, wt, offs, out):
         k_d = [keep.tile([P, PACK, P, PACK], BF16, name="k_d%d" % g, tag="k_d%d" % g, align_bytes=64) for g in range(G)]
         k_n_early = keep.tile([P, G, 2, 2, P // 2, PACK], BF16, name="k_n_early", align_bytes=64)
         k_n_third = keep.tile([P, G, 2, 1, P // 2, PACK], BF16, name="k_n_third", align_bytes=64)
-        k_n_last = on_window(2, 1.25, [P, G, 2, 1, P // 2, PACK], BF16, "k_n_last")
-        k_n = (k_n_early, k_n_early, k_n_third, k_n_last)
+        k_n = {0: k_n_early, 1: k_n_early, 2: k_n_third}
         kn_codes = on_window(2, 0, [P, G, D], U32, "kn_codes")
         kn_scales = keep.tile([P, G, D], U8, name="kn_scales", align_bytes=64)
         kd_codes = {}
@@ -193,30 +207,29 @@ def tile_attend_gpq_lch_x_kernel(tc, xT, cb, norm, ts, y, wt, offs, out):
                                                scalar=ts_col[:, g, a:a + 1], in1=yT[g, hf][:, a, :],
                                                op0=MULT, op1=SUB)
 
-        def tanh(g, hf):
-            th[g, hf] = keep.tile([P, PACK, HALF], F32, name="th%d_%d" % (g, hf), tag="th%d_%d" % (g, hf), align_bytes=64)
-            for i in range(2):
-                rows = slice(i * P, (i + 1) * P)
-                nc.scalar.activation(out=th[g, hf][:, :, rows], in_=z[g, hf][:, :, rows], func=TANH)
+        def tanh(g, i, tile=None):
+            th[g, i] = keep.tile([P, PACK, P], F32, name="th%d_%d" % (g, i), align_bytes=64) if tile is None else tile
+            nc.scalar.activation(out=th[g, i][:], in_=z[g, i // 2][:, :, i % 2 * P:(i % 2 + 1) * P], func=TANH)
 
-        def weigh(g, hf, first, tiles, tag):
-            h_bf[g, hf, first] = keep.tile([P, tiles * P, PACK], BF16, name="h_bf%d_%d_%d" % (g, hf, first), tag=tag,
-                                           align_bytes=64)
-            walk = "m a (c i) -> m c a i"
+        def h_tile(g, first, tiles, tag):
+            tile = keep.tile([P, tiles * P, PACK], BF16, name="h_bf%d_%d" % (g, first), tag=tag, align_bytes=64)
+            h_bf[g, first, tiles] = tile
             for e in range(tiles):
-                rows = slice((first + e) * P, (first + e + 1) * P)
-                whole = slice(hf * HALF + rows.start, hf * HALF + rows.stop)
-                nc.vector.tensor_tensor(h_bf[g, hf, first][:, e * P:(e + 1) * P].rearrange("m (c i) a -> m c a i", i=2),
-                                        th[g, hf][:, :, rows].rearrange(walk, i=2),
-                                        weight[:, g, :, whole].rearrange(walk, i=2), MULT)
+                h_bf[g, first + e] = tile[:, e * P:(e + 1) * P]
 
-        def quant_h(g, hf, first, tiles):
-            if first == 0:
-                h_codes[g, hf] = keep.tile([P, HALF], U32, name="h_codes%d_%d" % (g, hf), align_bytes=64)
-                h_scales[g, hf] = keep.tile([P, HALF], U8, name="h_scales%d_%d" % (g, hf), align_bytes=64)
-            rows = slice(first * P, (first + tiles) * P)
+        def weigh(g, i):
+            walk = "m a (c i) -> m c a i"
+            nc.vector.tensor_tensor(h_bf[g, i].rearrange("m (c i) a -> m c a i", i=2),
+                                    th[g, i][:].rearrange(walk, i=2), weight[g, i][:].rearrange(walk, i=2), MULT)
+
+        def quant_h(g, first, tiles, codes=None, scales=None):
+            hf = first // 2
+            if first % 2 == 0:
+                h_codes[g, hf] = keep.tile([P, HALF], U32, name="h_codes%d_%d" % (g, hf), align_bytes=64) if codes is None else codes
+                h_scales[g, hf] = keep.tile([P, HALF], U8, name="h_scales%d_%d" % (g, hf), align_bytes=64) if scales is None else scales
+            rows = slice(first % 2 * P, (first % 2 + tiles) * P)
             nc.vector.quantize_mx(out=h_codes[g, hf][:, rows].bitcast(E5), scales=h_scales[g, hf][:, rows],
-                                  in_=h_bf[g, hf, first][:].rearrange("m r a -> m (r a)"))
+                                  in_=h_bf[g, first, tiles][:].rearrange("m r a -> m (r a)"))
 
         def grad(g, hf, i, banks=None):
             rows = slice(i * P, (i + 1) * P)
@@ -230,8 +243,7 @@ def tile_attend_gpq_lch_x_kernel(tc, xT, cb, norm, ts, y, wt, offs, out):
                                     rhs=kn_codes[:, g, cols].bitcast(E4), rhs_scale=kn_scales[:, g, cols],
                                     start=(g == 0), stop=(g == G - 1))
 
-        def finish(hf, i, tag):
-            res = keep.tile([P, D], F32, name="res%d_%d" % (hf, i), tag=tag, align_bytes=64)
+        def finish(hf, i, res):
             rows = slice(hf * HALF + i * P, hf * HALF + (i + 1) * P)
             if len(sums[hf, i]) == 1:
                 nc.scalar.copy(out=res[:].rearrange("r (h p t) -> r h p t", h=2, t=PACK),
@@ -247,7 +259,7 @@ def tile_attend_gpq_lch_x_kernel(tc, xT, cb, norm, ts, y, wt, offs, out):
         on_v, on_s = nc.vector.tensor_copy, nc.scalar.copy
         for g in range(G):
             gather(0, g)
-        turn_early_k(6, 0, on_s)
+        turn_early_k(4, 0, on_s)
         for g in range(G):
             place(g, slice(0, 1), on_v)
         for g in range(G):
@@ -255,13 +267,13 @@ def tile_attend_gpq_lch_x_kernel(tc, xT, cb, norm, ts, y, wt, offs, out):
         load_y(2, on_window(1, 0, [P, N], F32, "y2"))
         load_x(0, on_window(1, 1, [P, PACK, HALF], F32, "x0"))
         load_y(3, on_window(1, 3, [P, N], F32, "y3"))
-        turn_early_k(6, 1, on_s)
+        turn_early_k(4, 1, on_s)
         for g in range(G):
             place(g, slice(1, 2), on_v)
         for g in range(G):
             gather(2, g)
         load_x(1, on_window(2, 3, [P, PACK, HALF], F32, "x1"))
-        turn_early_k(5, 2, on_v)
+        turn_early_k(3, 2, on_v)
         for g, copy in enumerate((on_s, on_v)):
             place(g, slice(2, 3), copy)
         for g in range(G):
@@ -286,52 +298,62 @@ def tile_attend_gpq_lch_x_kernel(tc, xT, cb, norm, ts, y, wt, offs, out):
         quant_kd(1, "x_bf0")
         for g in range(G):
             yT[g, 1] = on_window(1, 0.5 + g, [P, PACK, HALF], F32, "yT%d_1" % g)
-            turn_y(6 + g, g, 2)
+            turn_y(5 + g, g, 2)
         turn_y(0, 0, 3)
         scores(0, 0, (1, 2, 3, 4))
-        scores(1, 0, (5, 6, 7, 0))
+        scores(1, 0, (5, 6, 0, 1))
         round_x(1, keep.tile([P, HALF, PACK], BF16, name="x_bf1", align_bytes=64))
         rounded = keep.tile([P, G, KP], BF16, name="rounded3", tag="k_d1", align_bytes=64)
         nc.gpsimd.tensor_scalar(rounded[:], picked[:, last], 1.0, 0.0, MULT, ADD)
         for g in range(G):
-            residual(g, 0, keep.tile([P, PACK, HALF], F32, name="z%d_0" % g, tag="z%d_0" % g, align_bytes=64))
-        tanh(0, 0)
-        turn_k(1, last, rounded)
-        th_woven = keep.tile([P, HALF, PACK], F32, name="th_woven")
+            residual(g, 0, keep.tile([P, PACK, HALF], F32, name="z%d_0" % g, align_bytes=64))
+        for i in range(2):
+            tanh(0, i)
+        k_n[last] = on_window(2, 1.25, [P, G, 2, 1, P // 2, PACK], BF16, "k_n_last")
+        turn_k(2, last, rounded)
+        th_woven = on_window(3, 2, [P, HALF, PACK], F32, "th_woven")
         for i in range(2):
             rows = slice(i * P, (i + 1) * P)
             nc.scalar.activation(out=th_woven[:, rows, :], in_=z[1, 0][:, :, rows].rearrange("m a r -> m r a"),
                                  func=TANH)
-        turn_y(0, 1, 3)
+        turn_y(1, 1, 3)
         quant_x(1, "yT1")
-        scores(0, 1, (2, 3, 4, 1))
-        scores(1, 1, (5, 6, 7, 0))
-        weigh(0, 0, 0, 2, "h_first")
-        quant_kn(last)
-        quant_h(0, 0, 0, 2)
-        h_bf[1, 0, 0] = on_window(2, 1, [P, HALF, PACK], BF16, "h_bf1_0")
-        nc.gpsimd.tensor_tensor(h_bf[1, 0, 0][:], th_woven[:], weight_woven[:], MULT)
+        scores(0, 1, (3, 4, 5, 2))
+        scores(1, 1, (6, 0, 3, 1))
+        h_tile(0, 0, 2, "h_first")
         for i in range(2):
-            grad(0, 0, i, (2 + i,))
+            weigh(0, i)
+        quant_kn(last)
+        quant_h(0, 0, 2)
+        h_bf[1, 0, 2] = on_window(2, 1, [P, HALF, PACK], BF16, "h_bf1_0")
+        nc.gpsimd.tensor_tensor(h_bf[1, 0, 2][:], th_woven[:], weight_woven[:], MULT)
+        for i in range(2):
+            grad(0, 0, i, (4 + i,))
         residual(0, 1, on_window(2, 1.5, [P, PACK, HALF], F32, "z0_1"))
-        tanh(0, 1)
-        residual(1, 1, keep.tile([P, PACK, HALF], F32, name="z1_1", tag="z1_1", align_bytes=64))
-        tanh(1, 1)
-        quant_h(1, 0, 0, 2)
+        tanh(0, 2, on_window(3, 1, [P, PACK, P], F32, "th0_2"))
+        tanh(0, 3)
+        residual(1, 1, on_window(3, 3, [P, PACK, HALF], F32, "z1_1"))
+        for i in range(2, RT):
+            tanh(1, i)
+        h_tile(0, 2, 1, "h_tile0")
+        weigh(0, 2)
+        quant_h(1, 0, 2, on_window(3, 1, [P, HALF], U32, "h_codes1_0"))
         for i in range(2):
             grad(1, 0, i)
+        finish(0, 0, keep.tile([P, D], F32, name="res0_0", align_bytes=64))
+        finish(0, 1, on_window(3, 3, [P, D], F32, "res0_1"))
+        h_tile(0, 3, 1, "h_tile1")
+        weigh(0, 3)
+        quant_h(0, 2, 1)
+        grad(0, 1, 0, (2,))
+        h_tile(1, 2, 1, "h_tile2")
+        weigh(1, 2)
+        quant_h(0, 3, 1)
+        grad(0, 1, 1, (6, 0))
         for i in range(2):
-            finish(0, i, ("res_first", "z1_1")[i])
-        for i in range(2):
-            weigh(0, 1, i, 1, "h_tile%d" % i)
-        quant_h(0, 1, 0, 1)
-        grad(0, 1, 0, (4,))
-        weigh(1, 1, 0, 1, "h_tile2")
-        quant_h(0, 1, 1, 1)
-        grad(0, 1, 1, (1, 5))
-        for i in range(2):
-            quant_h(1, 1, i, 1)
+            quant_h(1, 2 + i, 1)
             grad(1, 1, i)
-            finish(1, i, "res%d" % i)
+            finish(1, i, keep.tile([P, D], F32, name="res1_%d" % i, align_bytes=64))
             if i == 0:
-                weigh(1, 1, 1, 1, "h_tile1")
+                h_tile(1, 3, 1, "h_tile1")
+                weigh(1, 3)

@@ -99,15 +99,17 @@ def tile_attend_gpq_lch_x_kernel(tc, xT, cb, norm, ts, y, wt, offs, out):
         for g in range(G):
             spread(1 + g, g * PACK, norm_row[:, g, :])
         weight = {}
+        walk = "m a (c i) -> m c a i"
         ts_row = bank(5, [P, PACK, P])
         for a in range(PACK):
             nc.tensor.transpose(ts_row[:, a, :], ts_col[:, 0, a:a + 1].to_broadcast([P, P]), ident[:])
         by_rows = {}
 
         def turn_weight(b, i):
-            weight[0, i] = bank(b, [P, PACK, P])
+            turned = bank(b, [P, P // 2, PACK, 2])
             for a in range(PACK):
-                nc.tensor.transpose(weight[0, i][:, a, :], by_rows[i][:, a, :], ident[:])
+                nc.tensor.transpose(turned[:, :, a, :], by_rows[i][:, a, :], ident[:])
+            weight[0, i] = turned[:]
 
         by_rows[2] = keep.tile([P, PACK, P], F32, name="by_rows")
         nc.scalar.activation(out=by_rows[2][:], in_=ts_row[:], func=COPY, scale=columns[:, runs + 2:runs + 3])
@@ -118,7 +120,7 @@ def tile_attend_gpq_lch_x_kernel(tc, xT, cb, norm, ts, y, wt, offs, out):
                 nc.scalar.activation(out=table[:, a, :], in_=wt_row[:, first * P:(first + tiles) * P], func=COPY,
                                      scale=ts_col[:, g, a:a + 1])
             for e in range(tiles):
-                weight[g, first + e] = table[:, :, e * P:(e + 1) * P]
+                weight[g, first + e] = table[:, :, e * P:(e + 1) * P].rearrange(walk, i=2)
         weight_woven = keep.tile([P, HALF, PACK], F32, name="weight_woven")
         nc.vector.tensor_tensor(weight_woven[:],
                                 wt_row[:, 0:HALF].rearrange("q (r o) -> q r o", o=1).to_broadcast([P, HALF, PACK]),
@@ -217,10 +219,10 @@ def tile_attend_gpq_lch_x_kernel(tc, xT, cb, norm, ts, y, wt, offs, out):
             for e in range(tiles):
                 h_bf[g, first + e] = tile[:, e * P:(e + 1) * P]
 
-        def weigh(g, i):
-            walk = "m a (c i) -> m c a i"
-            nc.vector.tensor_tensor(h_bf[g, i].rearrange("m (c i) a -> m c a i", i=2),
-                                    th[g, i][:].rearrange(walk, i=2), weight[g, i][:].rearrange(walk, i=2), MULT)
+        def weigh(g, i, rows=slice(0, P)):
+            nc.vector.tensor_tensor(h_bf[g, i][:, rows].rearrange("m (c i) a -> m c a i", i=2),
+                                    th[g, i][:, :, rows].rearrange(walk, i=2),
+                                    weight[g, i][:, rows.start // 2:rows.stop // 2], MULT)
 
         def quant_h(g, first, tiles, codes=None, scales=None):
             hf = first // 2
@@ -350,10 +352,16 @@ def tile_attend_gpq_lch_x_kernel(tc, xT, cb, norm, ts, y, wt, offs, out):
         weigh(1, 2)
         quant_h(0, 3, 1)
         grad(0, 1, 1, (6, 0))
-        for i in range(2):
-            quant_h(1, 2 + i, 1)
-            grad(1, 1, i)
-            finish(1, i, keep.tile([P, D], F32, name="res1_%d" % i, align_bytes=64))
-            if i == 0:
-                h_tile(1, 3, 1, "h_tile1")
-                weigh(1, 3)
+        quant_h(1, 2, 1)
+        grad(1, 1, 0)
+        finish(1, 0, keep.tile([P, D], F32, name="res1_0", align_bytes=64))
+        h_tile(1, 3, 1, "h_tile1")
+        parts = (slice(0, P // 2), slice(P // 2, P))
+        for rows in parts:
+            weigh(1, 3, rows)
+        for rows in parts:
+            cols = slice(P + rows.start, P + rows.stop)
+            nc.vector.quantize_mx(out=h_codes[1, 1][:, cols].bitcast(E5), scales=h_scales[1, 1][:, cols],
+                                  in_=h_bf[1, 3][:, rows].rearrange("m r a -> m (r a)"))
+        grad(1, 1, 1)
+        finish(1, 1, keep.tile([P, D], F32, name="res1_1", align_bytes=64))

from contextlib import ExitStack

import concourse.mybir as mybir
from concourse.masks import make_identity

N, C, D, R = 1024, 4096, 512, 512
FLOPS = 2 * 2 * R * D * N
BYTES = 4 * (D * R + D * C + 2 * N + R * N + R + R * D) + 2 * 128 * (N // 16)

F32 = mybir.dt.float32
BF16 = mybir.dt.bfloat16
U32 = mybir.dt.uint32
U16 = mybir.dt.uint16
U8 = mybir.dt.uint8
E4 = mybir.dt.float8_e4m3fn_x4
E5 = mybir.dt.float8_e5m2_x4
MULT = mybir.AluOpType.mult
ADD = mybir.AluOpType.add
SUB = mybir.AluOpType.subtract
TANH = mybir.ActivationFunctionType.Tanh
COPY = mybir.ActivationFunctionType.Copy

P = 128
PACK = 4
KP = P * PACK
G = N // KP
RT = R // P
HALF = R // 2
LEAD = 1280


def tile_attend_gpq_lch_x_kernel(tc, xT, cb, norm, ts, y, wt, offs, out):
    nc = tc.nc
    with ExitStack() as ctx:
        keep = ctx.enter_context(tc.tile_pool(name="keep", bufs=1))
        wide = ctx.enter_context(tc.tile_pool(name="wide", bufs=1))
        psum = ctx.enter_context(tc.psum_pool(name="psum", bufs=1))

        def bank(b, shape, dtype=F32):
            return psum.tile(shape, dtype, name="bank%d" % b, tag="bank%d" % b)

        offsets = keep.tile([P, N // 16], U16, name="offsets")
        window_bytes, piece_bytes = 4 * C, 4 * PACK * HALF

        def on_window(t, piece, shape, dtype, name):
            offset = t * window_bytes + int(piece * piece_bytes)
            return wide.tile(shape, dtype, name=name, offset=offset, align_bytes=64)

        win = [on_window(t, 0, [P, C], F32, "win%d" % t) for t in range(PACK)]
        x_raw, y_raw = {}, {}
        rows_in = keep.tile([P, P + KP], F32, name="rows_in")
        nc.vector.memset(rows_in[:], 0.0)
        ts_col = keep.tile([P, G, PACK], F32, name="ts_col")
        runs = N // P
        cb_planes = cb.rearrange("(p t) c -> t p c", t=PACK)
        x_planes = xT.rearrange("(p t) r -> p t r", t=PACK)

        def load_x(hf, tile):
            x_raw[hf] = tile
            nc.sync.dma_start(out=x_raw[hf][:], in_=x_planes[:, :, hf * HALF:(hf + 1) * HALF])

        def load_y(i, tile):
            y_raw[i] = tile
            nc.sync.dma_start(out=tile[:], in_=y[i * P:(i + 1) * P, :])

        nc.sync.dma_start(out=win[0][:, 0:LEAD], in_=cb_planes[0][:, 0:LEAD])
        nc.sync.dma_start(out=rows_in[0:runs, 0:P], in_=norm[0:1, :].rearrange("o (k c) -> (o k) c", c=P))
        nc.sync.dma_start(out=rows_in[runs:runs + RT, 0:P], in_=wt.rearrange("(k c) o -> k (c o)", c=P))
        nc.sync.dma_start(out=rows_in[0:G, P:], in_=ts[0:1, :].rearrange("o (g c) -> (o g) c", g=G))
        nc.sync.dma_start(offsets[:], offs)
        nc.sync.dma_start(out=win[0][:, LEAD:C], in_=cb_planes[0][:, LEAD:C])
        nc.sync.dma_start(out=win[1][:], in_=cb_planes[1])
        nc.sync.dma_start(out=win[2][:], in_=cb_planes[2])
        for i in range(2):
            load_y(i, keep.tile([P, N], F32, name="y_early%d" % i))
        nc.sync.dma_start(out=win[3][:], in_=cb_planes[3])

        ident = keep.tile([P, P], F32, name="ident")
        make_identity(nc, ident[:])

        turned_rows = bank(0, [P, P])
        nc.tensor.transpose(turned_rows[:], rows_in[:, 0:P], ident[:])
        columns = keep.tile([P, runs + RT], F32, name="columns")
        nc.scalar.copy(out=columns[:], in_=turned_rows[:, 0:runs + RT])
        turned_ts = bank(3, [P, PACK, P])
        for a in range(PACK):
            nc.tensor.transpose(turned_ts[:, a, :], rows_in[:, P + a:P + KP:PACK], ident[:])
        nc.scalar.copy(out=ts_col[:], in_=turned_ts[:, :, 0:G].rearrange("m a g -> m g a"))

        def spread(b, first, row):
            turned = bank(b, [P, PACK, P])
            for j in range(PACK):
                nc.tensor.transpose(turned[:, j, :], columns[:, first + j:first + j + 1].to_broadcast([P, P]), ident[:])
            nc.scalar.copy(out=row, in_=turned[:].rearrange("q j p -> q (j p)"))

        wt_row = keep.tile([P, R], F32, name="wt_row", tag="wt_row")
        spread(4, runs, wt_row[:])
        norm_row = keep.tile([P, G, KP], F32, name="norm_row")
        for g in range(G):
            spread(1 + g, g * PACK, norm_row[:, g, :])
        weight = {}
        walk = "m a (c i) -> m c a i"
        ts_row = bank(5, [P, PACK, P])
        for a in range(PACK):
            nc.tensor.transpose(ts_row[:, a, :], ts_col[:, 0, a:a + 1].to_broadcast([P, P]), ident[:])
        by_rows = {}

        def turn_weight(b, i):
            turned = bank(b, [P, P // 2, PACK, 2])
            for a in range(PACK):
                nc.tensor.transpose(turned[:, :, a, :], by_rows[i][:, a, :], ident[:])
            weight[0, i] = turned[:]

        by_rows[2] = keep.tile([P, PACK, P], F32, name="by_rows")
        nc.scalar.activation(out=by_rows[2][:], in_=ts_row[:], func=COPY, scale=columns[:, runs + 2:runs + 3])
        turn_weight(7, 2)
        for g, first, tiles in ((0, 0, 2), (0, 3, 1), (1, 2, 2)):
            table = keep.tile([P, PACK, tiles * P], F32, name="weight%d_%d" % (g, first))
            for a in range(PACK):
                nc.scalar.activation(out=table[:, a, :], in_=wt_row[:, first * P:(first + tiles) * P], func=COPY,
                                     scale=ts_col[:, g, a:a + 1])
            for e in range(tiles):
                weight[g, first + e] = table[:, :, e * P:(e + 1) * P].rearrange(walk, i=2)
        weight_woven = keep.tile([P, HALF, PACK], F32, name="weight_woven")
        nc.vector.tensor_tensor(weight_woven[:],
                                wt_row[:, 0:HALF].rearrange("q (r o) -> q r o", o=1).to_broadcast([P, HALF, PACK]),
                                ts_col[:, 1:2, :].to_broadcast([P, HALF, PACK]), MULT)

        last = PACK - 1
        k_d = [keep.tile([P, PACK, P, PACK], BF16, name="k_d%d" % g, tag="k_d%d" % g, align_bytes=64) for g in range(G)]
        k_n_early = keep.tile([P, G, 2, 2, P // 2, PACK], BF16, name="k_n_early", align_bytes=64)
        k_n_third = keep.tile([P, G, 2, 1, P // 2, PACK], BF16, name="k_n_third", align_bytes=64)
        k_n = {0: k_n_early, 1: k_n_early, 2: k_n_third}
        kn_codes = on_window(2, 0, [P, G, D], U32, "kn_codes")
        kn_scales = keep.tile([P, G, D], U8, name="kn_scales", align_bytes=64)
        kd_codes = {}
        kd_scales = [keep.tile([P, KP], U8, name="kd_scales%d" % g, align_bytes=64) for g in range(G)]
        picked = keep.tile([P, PACK, G, KP], F32, name="picked")

        def gather(t, g, cols=slice(0, KP)):
            lists = offsets[:, (g * KP + cols.start) // 16:(g * KP + cols.stop) // 16]
            nc.vector.tensor_tensor(picked[:, t, g, cols], win[t][:].indirect(lists), norm_row[:, g, cols], MULT)

        def place(g, planes, copy, cols=slice(0, KP)):
            copy(out=k_d[g][:, :, cols.start // PACK:cols.stop // PACK, planes],
                 in_=picked[:, planes, g, cols].rearrange("p t (m a) -> p a m t", a=PACK))

        def turn_k(b, t, rounded):
            words = rounded[:].rearrange("p g c -> p (g c)").bitcast(F32).rearrange("p (g w) -> p g w", g=G)
            turned = bank(b, [P, G, 2, P])
            for g in range(G):
                for u in range(2):
                    nc.tensor.transpose(turned[:, g, u, :], words[:, g, u:2 * P:2], ident[:])
            planes = k_n[t].shape[3]
            dst = k_n[t][:].rearrange("m g h t p a -> m (g h t p a)").bitcast(F32).rearrange(
                "m (g h t p u) -> m g h t p u", g=G, h=2, t=planes, u=2)
            nc.scalar.copy(out=dst[:, :, :, t % planes], in_=turned[:].rearrange("m g u (h p) -> m g h p u", h=2))

        def turn_early_k(b, t, copy):
            rounded = keep.tile([P, G, KP], BF16, name="rounded%d" % t)
            for g in range(G):
                copy(out=rounded[:, g], in_=picked[:, t, g])
            turn_k(b, t, rounded)

        def quant_kn(t):
            for g in range(G):
                for h in range(2):
                    start = h * D // 2 + t * P // 2
                    cols = slice(start, start + k_n[t].shape[3] * P // 2)
                    nc.vector.quantize_mx(out=kn_codes[:, g, cols].bitcast(E4), scales=kn_scales[:, g, cols],
                                          in_=k_n[t][:, g, h].rearrange("m t p a -> m (t p a)"))

        def quant_kd(g, tag):
            kd_codes[g] = keep.tile([P, KP], U32, name="kd_codes%d" % g, tag=tag, align_bytes=64)
            nc.vector.quantize_mx(out=kd_codes[g][:].bitcast(E4), scales=kd_scales[g][:],
                                  in_=k_d[g][:].rearrange("p a m t -> p (a m t)"))

        x_bf, x_codes, x_scales, yT, acc, z, th, h_bf, h_codes, h_scales, sums = ({} for e in range(11))

        def round_x(hf, tile):
            x_bf[hf] = tile
            nc.scalar.copy(out=x_bf[hf][:].rearrange("p (c i) t -> p c t i", i=2),
                           in_=x_raw[hf][:].rearrange("p t (c i) -> p c t i", i=2))

        def quant_x(hf, tag):
            x_codes[hf] = keep.tile([P, HALF], U32, name="x_codes%d" % hf, tag=tag, align_bytes=64)
            x_scales[hf] = keep.tile([P, HALF], U8, name="x_scales%d" % hf, align_bytes=64)
            nc.vector.quantize_mx(out=x_codes[hf][:].bitcast(E4), scales=x_scales[hf][:],
                                  in_=x_bf[hf][:].rearrange("p r t -> p (r t)"))

        def turn_y(b, g, i):
            turned = bank(b, [P, PACK, P])
            for a in range(PACK):
                nc.tensor.transpose(turned[:, a, :], y_raw[i][:, g * KP + a:(g + 1) * KP:PACK], ident[:])
            nc.scalar.copy(out=yT[g, i // 2][:, :, i % 2 * P:(i % 2 + 1) * P], in_=turned[:])

        def scores(g, hf, banks):
            for a, b in enumerate(banks):
                acc[g, hf, a] = bank(b, [P, HALF])
                cols = slice(a * P, (a + 1) * P)
                nc.tensor.matmul_mx(out=acc[g, hf, a][:], lhsT=kd_codes[g][:, cols].bitcast(E4),
                                    lhsT_scale=kd_scales[g][:, cols], rhs=x_codes[hf][:].bitcast(E4),
                                    rhs_scale=x_scales[hf][:], start=True, stop=True)

        def residual(g, hf, tile):
            z[g, hf] = tile
            for a in range(PACK):
                nc.vector.scalar_tensor_tensor(out=z[g, hf][:, a, :], in0=acc[g, hf, a][:],
                                               scalar=ts_col[:, g, a:a + 1], in1=yT[g, hf][:, a, :],
                                               op0=MULT, op1=SUB)

        def tanh(g, i, tile=None):
            th[g, i] = keep.tile([P, PACK, P], F32, name="th%d_%d" % (g, i), align_bytes=64) if tile is None else tile
            nc.scalar.activation(out=th[g, i][:], in_=z[g, i // 2][:, :, i % 2 * P:(i % 2 + 1) * P], func=TANH)

        def h_tile(g, first, tiles, tag):
            tile = keep.tile([P, tiles * P, PACK], BF16, name="h_bf%d_%d" % (g, first), tag=tag, align_bytes=64)
            h_bf[g, first, tiles] = tile
            for e in range(tiles):
                h_bf[g, first + e] = tile[:, e * P:(e + 1) * P]

        def weigh(g, i, rows=slice(0, P)):
            nc.vector.tensor_tensor(h_bf[g, i][:, rows].rearrange("m (c i) a -> m c a i", i=2),
                                    th[g, i][:, :, rows].rearrange(walk, i=2),
                                    weight[g, i][:, rows.start // 2:rows.stop // 2], MULT)

        def quant_h(g, first, tiles, codes=None, scales=None):
            hf = first // 2
            if first % 2 == 0:
                h_codes[g, hf] = keep.tile([P, HALF], U32, name="h_codes%d_%d" % (g, hf), align_bytes=64) if codes is None else codes
                h_scales[g, hf] = keep.tile([P, HALF], U8, name="h_scales%d_%d" % (g, hf), align_bytes=64) if scales is None else scales
            rows = slice(first % 2 * P, (first % 2 + tiles) * P)
            nc.vector.quantize_mx(out=h_codes[g, hf][:, rows].bitcast(E5), scales=h_scales[g, hf][:, rows],
                                  in_=h_bf[g, first, tiles][:].rearrange("m r a -> m (r a)"))

        def grad(g, hf, i, banks=None):
            rows = slice(i * P, (i + 1) * P)
            if g == 0:
                sums[hf, i] = [bank(b, [P, D // len(banks)]) for b in banks]
            width = D // len(sums[hf, i])
            for h, total in enumerate(sums[hf, i]):
                cols = slice(h * width, (h + 1) * width)
                nc.tensor.matmul_mx(out=total[:], lhsT=h_codes[g, hf][:, rows].bitcast(E5),
                                    lhsT_scale=h_scales[g, hf][:, rows],
                                    rhs=kn_codes[:, g, cols].bitcast(E4), rhs_scale=kn_scales[:, g, cols],
                                    start=(g == 0), stop=(g == G - 1))

        def finish(hf, i, res):
            rows = slice(hf * HALF + i * P, hf * HALF + (i + 1) * P)
            if len(sums[hf, i]) == 1:
                nc.scalar.copy(out=res[:].rearrange("r (h p t) -> r h p t", h=2, t=PACK),
                               in_=sums[hf, i][0][:].rearrange("r (h t p) -> r h p t", h=2, t=PACK))
                nc.sync.dma_start(out=out[rows, :], in_=res[:])
            else:
                for h, copy in enumerate((nc.vector.tensor_copy, nc.scalar.copy)):
                    cols = slice(h * D // 2, (h + 1) * D // 2)
                    copy(out=res[:, cols].rearrange("r (p t) -> r p t", t=PACK),
                         in_=sums[hf, i][h][:].rearrange("r (t p) -> r p t", t=PACK))
                    nc.sync.dma_start(out=out[rows, cols], in_=res[:, cols])

        on_v, on_s = nc.vector.tensor_copy, nc.scalar.copy
        for g in range(G):
            gather(0, g)
        turn_early_k(4, 0, on_s)
        for g in range(G):
            place(g, slice(0, 1), on_v)
        for g in range(G):
            gather(1, g)
        load_y(2, on_window(1, 0, [P, N], F32, "y2"))
        load_x(0, on_window(1, 1, [P, PACK, HALF], F32, "x0"))
        load_y(3, on_window(1, 3, [P, N], F32, "y3"))
        turn_early_k(4, 1, on_s)
        for g in range(G):
            place(g, slice(1, 2), on_v)
        for g in range(G):
            gather(2, g)
        load_x(1, on_window(2, 3, [P, PACK, HALF], F32, "x1"))
        turn_early_k(3, 2, on_v)
        for g, copy in enumerate((on_s, on_v)):
            place(g, slice(2, 3), copy)
        for g in range(G):
            yT[g, 0] = keep.tile([P, PACK, HALF], F32, name="yT%d_0" % g, tag="yT%d" % g, align_bytes=64)
            turn_y(g, g, 0)
        quant_kn(0)
        quant_kn(2)
        for g in range(G):
            turn_y(g, g, 1)

        halves = (slice(0, KP // 2), slice(KP // 2, KP))
        for cols in halves:
            gather(last, 0, cols)
            place(0, slice(last, PACK), on_s, cols)
        for cols in halves:
            gather(last, 1, cols)
        round_x(0, keep.tile([P, HALF, PACK], BF16, name="x_bf0", tag="x_bf0", align_bytes=64))
        quant_kd(0, "kd_codes0")
        for cols in halves:
            place(1, slice(last, PACK), on_v, cols)
        quant_x(0, "x_codes0")
        quant_kd(1, "x_bf0")
        for g in range(G):
            yT[g, 1] = on_window(1, 0.5 + g, [P, PACK, HALF], F32, "yT%d_1" % g)
            turn_y(5 + g, g, 2)
        turn_y(0, 0, 3)
        scores(0, 0, (1, 2, 3, 4))
        scores(1, 0, (5, 6, 0, 1))
        round_x(1, keep.tile([P, HALF, PACK], BF16, name="x_bf1", align_bytes=64))
        rounded = keep.tile([P, G, KP], BF16, name="rounded3", tag="k_d1", align_bytes=64)
        nc.gpsimd.tensor_scalar(rounded[:], picked[:, last], 1.0, 0.0, MULT, ADD)
        for g in range(G):
            residual(g, 0, keep.tile([P, PACK, HALF], F32, name="z%d_0" % g, align_bytes=64))
        for i in range(2):
            tanh(0, i)
        k_n[last] = on_window(2, 1.25, [P, G, 2, 1, P // 2, PACK], BF16, "k_n_last")
        turn_k(2, last, rounded)
        th_woven = on_window(3, 2, [P, HALF, PACK], F32, "th_woven")
        for i in range(2):
            rows = slice(i * P, (i + 1) * P)
            nc.scalar.activation(out=th_woven[:, rows, :], in_=z[1, 0][:, :, rows].rearrange("m a r -> m r a"),
                                 func=TANH)
        turn_y(1, 1, 3)
        quant_x(1, "yT1")
        scores(0, 1, (3, 4, 5, 2))
        scores(1, 1, (6, 0, 3, 1))
        h_tile(0, 0, 2, "h_first")
        for i in range(2):
            weigh(0, i)
        quant_kn(last)
        quant_h(0, 0, 2)
        h_bf[1, 0, 2] = on_window(2, 1, [P, HALF, PACK], BF16, "h_bf1_0")
        nc.gpsimd.tensor_tensor(h_bf[1, 0, 2][:], th_woven[:], weight_woven[:], MULT)
        for i in range(2):
            grad(0, 0, i, (4 + i,))
        residual(0, 1, on_window(2, 1.5, [P, PACK, HALF], F32, "z0_1"))
        tanh(0, 2, on_window(3, 1, [P, PACK, P], F32, "th0_2"))
        tanh(0, 3)
        residual(1, 1, on_window(3, 3, [P, PACK, HALF], F32, "z1_1"))
        for i in range(2, RT):
            tanh(1, i)
        h_tile(0, 2, 1, "h_tile0")
        weigh(0, 2)
        quant_h(1, 0, 2, on_window(3, 1, [P, HALF], U32, "h_codes1_0"))
        for i in range(2):
            grad(1, 0, i)
        finish(0, 0, keep.tile([P, D], F32, name="res0_0", align_bytes=64))
        finish(0, 1, on_window(3, 3, [P, D], F32, "res0_1"))
        h_tile(0, 3, 1, "h_tile1")
        weigh(0, 3)
        quant_h(0, 2, 1)
        grad(0, 1, 0, (2,))
        h_tile(1, 2, 1, "h_tile2")
        weigh(1, 2)
        quant_h(0, 3, 1)
        grad(0, 1, 1, (6, 0))
        quant_h(1, 2, 1)
        grad(1, 1, 0)
        finish(1, 0, keep.tile([P, D], F32, name="res1_0", align_bytes=64))
        h_tile(1, 3, 1, "h_tile1")
        parts = (slice(0, P // 2), slice(P // 2, P))
        for rows in parts:
            weigh(1, 3, rows)
        for rows in parts:
            cols = slice(P + rows.start, P + rows.stop)
            nc.vector.quantize_mx(out=h_codes[1, 1][:, cols].bitcast(E5), scales=h_scales[1, 1][:, cols],
                                  in_=h_bf[1, 3][:, rows].rearrange("m r a -> m (r a)"))
        grad(1, 1, 1)
        finish(1, 1, keep.tile([P, D], F32, name="res1_1", align_bytes=64))
